import numpy as np
import ml_dtypes


def mxq(x, axis, fmt="e4m3"):
    dtype, down = {"e4m3": (ml_dtypes.float8_e4m3fn, 7), "e5m2": (ml_dtypes.float8_e5m2, 14)}[fmt]
    v = np.moveaxis(np.asarray(x, np.float32).astype(ml_dtypes.bfloat16).astype(np.float64), axis, -1)
    blocks = v.reshape(v.shape[:-1] + (-1, 32))
    amax = np.abs(blocks).max(-1, keepdims=True)
    byte = np.maximum(np.where(amax > 0, np.frexp(amax)[1] - 1 + 127, 0) - down, 1)
    scale = np.exp2(byte - 127.0)
    codes = (blocks / scale).astype(np.float32).astype(dtype).astype(np.float64)
    return np.moveaxis((codes * scale).reshape(v.shape), -1, axis)


WIDE = False


def mx_kscale(k):
    if not WIDE:
        return np.ones(k)
    levels = np.array([18, -18])
    if k % 512:
        return np.exp2(np.random.permutation(np.resize(levels, k // 32))).repeat(32)
    a = np.empty((k // 512, 16))
    for p in range(k // 512):
        a[p, :8] = np.random.permutation(np.resize(levels, 8))
        for g in range(8):
            far = levels[np.abs(levels - a[p, g]) >= 10]
            a[p, g + 8] = far[np.random.randint(len(far))]
    return np.exp2(a.ravel()).repeat(32)


def f64(x):
    return np.asarray(x).astype(np.float64)


def striped(idx):
    return np.tile(np.asarray(idx).reshape(-1, 16).T, (8, 1)).astype(np.uint16)


def unstriped(offs):
    return offs[:16].T.reshape(-1).astype(np.int64)


def setup_inputs():
    n = np.random.standard_normal
    uni = np.random.uniform
    idx = np.random.permutation(2048)[:512]
    seg = np.random.permutation(1024)[:512]
    f_e = mx_kscale(512)
    return {
        "aT": (0.2 + n((512, 2048))).astype(np.float32),
        "bT": (0.5 * n((512, 1024))).astype(np.float32),
        "W": (n((512, 512)) / np.sqrt(512) * f_e[:, None]).astype(np.float32),
        "dz": (n((512, 512)) / f_e[:, None]).astype(np.float32),
        "gam": np.tile(uni(0.75, 1.3, 512), (128, 1)).astype(np.float32),
        "offs": striped(idx),
        "soffs": striped(seg),
    }


def reference(aT, bT, W, dz, gam, offs, soffs):
    idx = unstriped(offs)
    seg = unstriped(soffs)
    a = f64(aT)[:, idx]
    b = f64(bT)[:, seg]
    x = a + b
    xr = x.T
    dn = mxq(f64(dz), 0, "e5m2").T @ mxq(f64(W), 0, "e4m3")
    h = f64(gam)[:1] * dn
    s2 = (np.square(xr)).sum(-1, keepdims=True)
    rstd = 1.0 / np.sqrt(s2 / 512.0)
    n = xr * rstd
    h2 = (h * n).sum(-1, keepdims=True)
    dx = rstd * (h - n * h2 / 512.0)
    dxt = dx.T
    out_0 = np.zeros((512, 2048))
    out_0[:, idx] = dxt
    out_1 = np.zeros((512, 1024))
    out_1[:, seg] = dxt
    return out_0, out_1

@@ -1,0 +1,219 @@
+from contextlib import ExitStack
+
+import concourse.mybir as mybir
+from concourse.masks import make_identity
+
+FLOPS = 2 * 512 * 512 * 512
+
+F32 = mybir.dt.float32
+BF16 = mybir.dt.bfloat16
+U32 = mybir.dt.uint32
+U16 = mybir.dt.uint16
+U8 = mybir.dt.uint8
+E4M3 = mybir.dt.float8_e4m3fn_x4
+E5M2 = mybir.dt.float8_e5m2_x4
+ACT = mybir.ActivationFunctionType
+ALU = mybir.AluOpType
+
+P = 128
+PACK = 4
+D = 512
+SLOTS = 512
+TOKENS = 2048
+SEGMENTS = 1024
+BLOCKS = 4
+HALF = D // 2
+
+
+def cols(block):
+    return slice(block * P, (block + 1) * P)
+
+
+def entries(first_block, last_block):
+    return slice(first_block * P // 16, last_block * P // 16)
+
+
+def tile_attend_gtwoemb_rms_kernel(tc, aT, bT, W, dz, gam, offs, soffs, out_0, out_1):
+    nc = tc.nc
+    with ExitStack() as ctx:
+        pool = ctx.enter_context(tc.tile_pool(name="pool", bufs=1))
+        held = ctx.enter_context(tc.psum_pool(name="held", bufs=1))
+        ring = ctx.enter_context(tc.psum_pool(name="ring", bufs=4))
+
+        def sb(name, shape, dtype=F32):
+            return pool.tile(shape, dtype, name=name, align_bytes=64)
+
+        def bank(name):
+            return ring.tile([P, SLOTS], F32, name=name, tag="bank")
+
+        dz_raw = sb("dz_raw", [P, PACK, SLOTS])
+        nc.sync.dma_start(dz_raw[:], dz.rearrange("(p t) i -> p t i", t=PACK))
+        w_raw = sb("w_raw", [P, PACK, D])
+        nc.sync.dma_start(w_raw[:], W.rearrange("(p t) d -> p t d", t=PACK))
+        tok = pool.tile([P, SLOTS // 16], U16, name="tok")
+        nc.sync.dma_start(tok[:], offs)
+        seg = pool.tile([P, SLOTS // 16], U16, name="seg")
+        nc.sync.dma_start(seg[:], soffs)
+        gam_rows = sb("gam_rows", [P, P])
+        nc.sync.dma_start(gam_rows[:], gam.rearrange("r (j c) -> (r j) c", c=P)[0:P, :])
+        a_tab = [sb("a_tab%d" % j, [P, TOKENS]) for j in range(BLOCKS)]
+        b_tab = [sb("b_tab%d" % j, [P, SEGMENTS]) for j in range(BLOCKS)]
+        order = [("b", 0), ("a", 0), ("b", 1), ("a", 1), ("b", 2), ("b", 3), ("a", 2), ("a", 3)]
+        for which, j in order:
+            if which == "a":
+                nc.sync.dma_start(a_tab[j][:], aT[cols(j), :])
+            else:
+                nc.sync.dma_start(b_tab[j][:], bT[cols(j), :])
+
+        ident = sb("ident", [P, P])
+        make_identity(nc, ident[:])
+        one = sb("one", [P, 1])
+        nc.gpsimd.memset(one[:], 1.0)
+        warm = sb("warm", [P, 1])
+        nc.scalar.activation(warm[:], one[:], ACT.Sqrt)
+
+        win1 = [sb("win1_%d" % j, [P, SEGMENTS]) for j in range(BLOCKS)]
+        win0 = [sb("win0_%d" % j, [P, TOKENS]) for j in range(BLOCKS)]
+        for window in win1 + win0:
+            nc.gpsimd.memset(window[:], 0.0)
+
+        def quantise(name, raw, fmt):
+            woven = sb(name + "_woven", [P, SLOTS, PACK], BF16)
+            nc.scalar.copy(
+                woven[:].rearrange("p (c i) t -> p c t i", i=4),
+                raw[:].rearrange("p t (c i) -> p c t i", i=4),
+            )
+            codes = sb(name + "_codes", [P, SLOTS], U32)
+            scales = sb(name + "_scales", [P, SLOTS], U8)
+            nc.vector.quantize_mx(out=codes[:].bitcast(fmt), scales=scales[:], in_=woven[:].rearrange("p c t -> p (c t)"))
+            return codes, scales
+
+        dz_codes, dz_scales = quantise("dz", dz_raw, E5M2)
+        w_codes, w_scales = quantise("w", w_raw, E4M3)
+
+        gam_ps = bank("gam_ps")
+        nc.tensor.transpose(gam_ps[:, 0:P], gam_rows[:], ident[:])
+        gam_col = sb("gam_col", [P, BLOCKS])
+        nc.scalar.copy(gam_col[:], gam_ps[:, 0:BLOCKS])
+
+        h_ps = [held.tile([P, D], F32, name="h_ps%d" % ib) for ib in range(BLOCKS)]
+        for j in range(BLOCKS):
+            dn_ps = bank("dn_ps")
+            nc.tensor.matmul_mx(
+                out=dn_ps[:],
+                lhsT=w_codes[:, cols(j)].bitcast(E4M3),
+                lhsT_scale=w_scales[:, cols(j)],
+                rhs=dz_codes[:].bitcast(E5M2),
+                rhs_scale=dz_scales[:],
+                start=True,
+                stop=True,
+            )
+            hT = sb("hT%d" % j, [P, SLOTS])
+            nc.scalar.activation(hT[:], dn_ps[:], ACT.Copy, scale=gam_col[:, j : j + 1])
+            for ib in range(BLOCKS):
+                nc.tensor.transpose(h_ps[ib][:, cols(j)], hT[:, cols(ib)], ident[:])
+
+        x = [sb("x%d" % ib, [P, D]) for ib in range(BLOCKS)]
+        a_got = [sb("a_got%d" % j, [P, SLOTS]) for j in range(BLOCKS)]
+        b_got = [sb("b_got%d" % j, [P, SLOTS]) for j in range(BLOCKS)]
+        mean_part = sb("mean_part", [P, 2, BLOCKS])
+        dot_part = sb("dot_part", [P, 2, BLOCKS])
+        junk_s = sb("junk_s", [P, HALF])
+        junk_v = sb("junk_v", [P, HALF])
+
+        def turn_x(j, ibs, summed):
+            x_ps = bank("x_ps")
+            for ib in ibs:
+                if ib in summed:
+                    nc.tensor.transpose(x_ps[:, cols(ib)], a_got[j][:, cols(ib)], ident[:])
+                else:
+                    nc.tensor.matmul(x_ps[:, cols(ib)], b_got[j][:, cols(ib)], ident[:], start=True, stop=False, is_transpose=True)
+                    nc.tensor.matmul(x_ps[:, cols(ib)], a_got[j][:, cols(ib)], ident[:], start=False, stop=True, is_transpose=True)
+            for ib in ibs:
+                nc.scalar.copy(x[ib][:, cols(j)], x_ps[:, cols(ib)])
+
+        def partial_sums(ib, half):
+            span = slice(half * HALF, (half + 1) * HALF)
+            nc.scalar.activation(junk_s[:], x[ib][:, span], ACT.Square, scale=float(D) ** -0.5,
+                                 accum_out=mean_part[:, half, ib : ib + 1])
+            nc.vector.scalar_tensor_tensor(junk_v[:], h_ps[ib][:, span], -1.0 / D, x[ib][:, span], ALU.mult, ALU.mult,
+                                           accum_out=dot_part[:, half, ib : ib + 1])
+
+        last = BLOCKS - 1
+        for which, j in order[:-1]:
+            if which == "a":
+                nc.vector.tensor_copy(a_got[j][:], a_tab[j][:].indirect(tok[:]))
+                turn_x(j, range(BLOCKS), [])
+                if j == 1:
+                    for ib in range(BLOCKS):
+                        partial_sums(ib, 0)
+            else:
+                nc.vector.tensor_copy(b_got[j][:], b_tab[j][:].indirect(seg[:]))
+
+        mean = sb("mean", [P, BLOCKS])
+        inv_mean = sb("inv_mean", [P, BLOCKS])
+        rstd = sb("rstd", [P, BLOCKS])
+        coef_v = sb("coef_v", [P, 1])
+        dot = sb("dot", [P, BLOCKS])
+        coef = sb("coef", [P, BLOCKS])
+        slope = sb("slope", [P, BLOCKS])
+        t1 = [sb("t1_%d" % ib, [P, D]) for ib in range(BLOCKS)]
+        t2 = [sb("t2_%d" % ib, [P, D]) for ib in range(BLOCKS)]
+        y = [sb("y%d" % j, [P, SLOTS]) for j in range(BLOCKS)]
+
+        def add_turned(out, ib, j):
+            nc.tensor.matmul(out, t1[ib][:, cols(j)], ident[:], start=True, stop=False, is_transpose=True)
+            nc.tensor.matmul(out, t2[ib][:, cols(j)], ident[:], start=False, stop=True, is_transpose=True)
+
+        nc.vector.tensor_tensor(a_got[last][:, cols(0)], a_tab[last][:].indirect(tok[:, entries(0, 1)]),
+                                b_got[last][:, cols(0)], ALU.add)
+        turn_x(last, [0], [0])
+        partial_sums(0, 1)
+        nc.scalar.activation(mean[:, 0:1], mean_part[:, 1, 0:1], ACT.Identity, bias=mean_part[:, 0, 0:1])
+        nc.vector.reciprocal(inv_mean[:, 0:1], mean[:, 0:1])
+        nc.scalar.activation(rstd[:, 0:1], inv_mean[:, 0:1], ACT.Sqrt)
+        nc.vector.tensor_scalar(coef_v[:], dot_part[:, 0, 0:1], dot_part[:, 1, 0:1], inv_mean[:, 0:1], ALU.add, ALU.mult)
+        nc.vector.tensor_scalar(t2[0][:], x[0][:], coef_v[:], rstd[:, 0:1], ALU.mult, ALU.mult)
+        nc.scalar.activation(t1[0][:, cols(0)], h_ps[0][:, cols(0)], ACT.Copy, scale=rstd[:, 0:1])
+        y_first = bank("y_first")
+        add_turned(y_first[:, cols(0)], 0, 0)
+        nc.scalar.copy(y[0][:, cols(0)], y_first[:, cols(0)])
+        nc.scalar.activation(t1[0][:, P:D], h_ps[0][:, P:D], ACT.Copy, scale=rstd[:, 0:1])
+        y_next = bank("y_next")
+        for j in range(1, BLOCKS):
+            add_turned(y_next[:, cols(j)], 0, j)
+        for j in range(1, BLOCKS):
+            nc.scalar.copy(y[j][:, cols(0)], y_next[:, cols(j)])
+
+        rest = range(1, BLOCKS)
+        nc.vector.tensor_copy(a_got[last][:, P:SLOTS], a_tab[last][:].indirect(tok[:, entries(1, BLOCKS)]))
+        turn_x(last, rest, [])
+        for ib in rest:
+            partial_sums(ib, 1)
+        for ib in rest:
+            nc.scalar.activation(mean[:, ib : ib + 1], mean_part[:, 1, ib : ib + 1], ACT.Identity,
+                                 bias=mean_part[:, 0, ib : ib + 1])
+        nc.vector.reciprocal(inv_mean[:, 1:BLOCKS], mean[:, 1:BLOCKS])
+        for ib in rest:
+            nc.scalar.activation(dot[:, ib : ib + 1], dot_part[:, 1, ib : ib + 1], ACT.Identity,
+                                 bias=dot_part[:, 0, ib : ib + 1])
+        nc.scalar.activation(rstd[:, 1:BLOCKS], inv_mean[:, 1:BLOCKS], ACT.Sqrt)
+        for ib in rest:
+            nc.scalar.activation(coef[:, ib : ib + 1], dot[:, ib : ib + 1], ACT.Copy, scale=inv_mean[:, ib : ib + 1])
+        for ib in rest:
+            nc.scalar.activation(slope[:, ib : ib + 1], coef[:, ib : ib + 1], ACT.Copy, scale=rstd[:, ib : ib + 1])
+
+        for j in range(BLOCKS):
+            nc.vector.tensor_copy(win1[j][:].indirect(seg[:, entries(0, 1)]), y[j][:, cols(0)])
+
+        for j in range(BLOCKS):
+            y_ps = bank("y_ps")
+            for ib in rest:
+                nc.scalar.activation(t1[ib][:, cols(j)], h_ps[ib][:, cols(j)], ACT.Copy, scale=rstd[:, ib : ib + 1])
+                nc.scalar.activation(t2[ib][:, cols(j)], x[ib][:, cols(j)], ACT.Copy, scale=slope[:, ib : ib + 1])
+                add_turned(y_ps[:, cols(ib)], ib, j)
+            nc.scalar.copy(y[j][:, P:SLOTS], y_ps[:, P:SLOTS])
+            nc.vector.tensor_copy(win0[j][:].indirect(tok[:]), y[j][:])
+            nc.sync.dma_start(out_0[cols(j), :], win0[j][:])
+            nc.vector.tensor_copy(win1[j][:].indirect(seg[:, entries(1, BLOCKS)]), y[j][:, P:SLOTS])
+            nc.sync.dma_start(out_1[cols(j), :], win1[j][:])

@@ -73,47 +73,63 @@ def tile_attend_gtwoemb_rms_kernel(tc, aT, bT, W, dz, gam, offs, soffs, out_0, o
         nc.scalar.activation(warm[:], one[:], ACT.Sqrt)
 
         win1 = [sb("win1_%d" % j, [P, SEGMENTS]) for j in range(BLOCKS)]
-        win0 = [sb("win0_%d" % j, [P, TOKENS]) for j in range(BLOCKS)]
+        win0 = [sb("win0_%d" % j, [P, TOKENS]) for j in range(2)]
         for window in win1 + win0:
-            nc.gpsimd.memset(window[:], 0.0)
+            nc.vector.memset(window[:], 0.0)
 
-        def quantise(name, raw, fmt):
-            woven = sb(name + "_woven", [P, SLOTS, PACK], BF16)
-            nc.scalar.copy(
+        def quantise(name, raw, fmt, copy, tag):
+            width = raw.shape[2]
+            woven = pool.tile([P, width, PACK], BF16, name=name + "_woven", tag=tag, align_bytes=64)
+            copy(
                 woven[:].rearrange("p (c i) t -> p c t i", i=4),
-                raw[:].rearrange("p t (c i) -> p c t i", i=4),
+                raw.rearrange("p t (c i) -> p c t i", i=4),
             )
-            codes = sb(name + "_codes", [P, SLOTS], U32)
-            scales = sb(name + "_scales", [P, SLOTS], U8)
-            nc.vector.quantize_mx(out=codes[:].bitcast(fmt), scales=scales[:], in_=woven[:].rearrange("p c t -> p (c t)"))
-            return codes, scales
+            codes = sb(name + "_codes", [P, width], U32)
+            scales = sb(name + "_scales", [P, width], U8)
+            return woven, codes, scales, fmt
 
-        dz_codes, dz_scales = quantise("dz", dz_raw, E5M2)
-        w_codes, w_scales = quantise("w", w_raw, E4M3)
+        def run_quantise(woven, codes, scales, fmt):
+            nc.vector.quantize_mx(out=codes[:].bitcast(fmt), scales=scales[:], in_=woven[:].rearrange("p c t -> p (c t)"))
+
+        dz_q = quantise("dz", dz_raw[:], E5M2, nc.vector.tensor_copy, "dz_woven")
+        run_quantise(*dz_q)
+        w_q = [
+            quantise("w0", w_raw[:, :, 0:HALF], E4M3, nc.vector.tensor_copy, "late0"),
+            quantise("w1", w_raw[:, :, HALF:D], E4M3, nc.scalar.copy, "late1"),
+        ]
+        for q in w_q:
+            run_quantise(*q)
+        for j in range(2, BLOCKS):
+            window = pool.tile([P, TOKENS], F32, name="win0_%d" % j, tag="late%d" % (BLOCKS - 1 - j), align_bytes=64)
+            nc.gpsimd.memset(window[:], 0.0)
+            win0.append(window)
 
         gam_ps = bank("gam_ps")
         nc.tensor.transpose(gam_ps[:, 0:P], gam_rows[:], ident[:])
         gam_col = sb("gam_col", [P, BLOCKS])
         nc.scalar.copy(gam_col[:], gam_ps[:, 0:BLOCKS])
 
-        h_ps = [held.tile([P, D], F32, name="h_ps%d" % ib) for ib in range(BLOCKS)]
+        hT = [sb("hT%d" % j, [P, SLOTS]) for j in range(BLOCKS)]
         for j in range(BLOCKS):
             dn_ps = bank("dn_ps")
             nc.tensor.matmul_mx(
                 out=dn_ps[:],
-                lhsT=w_codes[:, cols(j)].bitcast(E4M3),
-                lhsT_scale=w_scales[:, cols(j)],
-                rhs=dz_codes[:].bitcast(E5M2),
-                rhs_scale=dz_scales[:],
+                lhsT=w_q[j // 2][1][:, cols(j % 2)].bitcast(E4M3),
+                lhsT_scale=w_q[j // 2][2][:, cols(j % 2)],
+                rhs=dz_q[1][:].bitcast(E5M2),
+                rhs_scale=dz_q[2][:],
                 start=True,
                 stop=True,
             )
-            hT = sb("hT%d" % j, [P, SLOTS])
-            nc.scalar.activation(hT[:], dn_ps[:], ACT.Copy, scale=gam_col[:, j : j + 1])
-            for ib in range(BLOCKS):
-                nc.tensor.transpose(h_ps[ib][:, cols(j)], hT[:, cols(ib)], ident[:])
+            nc.scalar.activation(hT[j][:], dn_ps[:], ACT.Copy, scale=gam_col[:, j : j + 1])
+        h = [sb("h%d" % ib, [P, D]) for ib in range(BLOCKS)]
+        for ib in range(BLOCKS):
+            h_ps = bank("h_ps")
+            for j in range(BLOCKS):
+                nc.tensor.transpose(h_ps[:, cols(j)], hT[j][:, cols(ib)], ident[:])
+            nc.scalar.copy(h[ib][:], h_ps[:])
 
-        x = [sb("x%d" % ib, [P, D]) for ib in range(BLOCKS)]
+        x_ps = [held.tile([P, D], F32, name="x_ps%d" % ib) for ib in range(BLOCKS)]
         a_got = [sb("a_got%d" % j, [P, SLOTS]) for j in range(BLOCKS)]
         b_got = [sb("b_got%d" % j, [P, SLOTS]) for j in range(BLOCKS)]
         mean_part = sb("mean_part", [P, 2, BLOCKS])
@@ -121,34 +137,31 @@ def tile_attend_gtwoemb_rms_kernel(tc, aT, bT, W, dz, gam, offs, soffs, out_0, o
         junk_s = sb("junk_s", [P, HALF])
         junk_v = sb("junk_v", [P, HALF])
 
-        def turn_x(j, ibs, summed):
-            x_ps = bank("x_ps")
+        def turn(got, j, ibs, start, stop):
             for ib in ibs:
-                if ib in summed:
-                    nc.tensor.transpose(x_ps[:, cols(ib)], a_got[j][:, cols(ib)], ident[:])
-                else:
-                    nc.tensor.matmul(x_ps[:, cols(ib)], b_got[j][:, cols(ib)], ident[:], start=True, stop=False, is_transpose=True)
-                    nc.tensor.matmul(x_ps[:, cols(ib)], a_got[j][:, cols(ib)], ident[:], start=False, stop=True, is_transpose=True)
-            for ib in ibs:
-                nc.scalar.copy(x[ib][:, cols(j)], x_ps[:, cols(ib)])
+                nc.tensor.matmul(x_ps[ib][:, cols(j)], got[j][:, cols(ib)], ident[:], start=start, stop=stop, is_transpose=True)
 
         def partial_sums(ib, half):
             span = slice(half * HALF, (half + 1) * HALF)
-            nc.scalar.activation(junk_s[:], x[ib][:, span], ACT.Square, scale=float(D) ** -0.5,
+            nc.scalar.activation(junk_s[:], x_ps[ib][:, span], ACT.Square, scale=float(D) ** -0.5,
                                  accum_out=mean_part[:, half, ib : ib + 1])
-            nc.vector.scalar_tensor_tensor(junk_v[:], h_ps[ib][:, span], -1.0 / D, x[ib][:, span], ALU.mult, ALU.mult,
+            nc.vector.scalar_tensor_tensor(junk_v[:], x_ps[ib][:, span], -1.0 / D, h[ib][:, span], ALU.mult, ALU.mult,
                                            accum_out=dot_part[:, half, ib : ib + 1])
 
         last = BLOCKS - 1
+        every = range(BLOCKS)
+        rest = range(1, BLOCKS)
         for which, j in order[:-1]:
             if which == "a":
                 nc.vector.tensor_copy(a_got[j][:], a_tab[j][:].indirect(tok[:]))
-                turn_x(j, range(BLOCKS), [])
-                if j == 1:
-                    for ib in range(BLOCKS):
-                        partial_sums(ib, 0)
+                turn(b_got, j, every, True, False)
+                turn(a_got, j, every, False, True)
             else:
                 nc.vector.tensor_copy(b_got[j][:], b_tab[j][:].indirect(seg[:]))
+                if j == last:
+                    for ib in every:
+                        partial_sums(ib, 0)
+        turn(b_got, last, rest, True, False)
 
         mean = sb("mean", [P, BLOCKS])
         inv_mean = sb("inv_mean", [P, BLOCKS])
@@ -156,38 +169,43 @@ def tile_attend_gtwoemb_rms_kernel(tc, aT, bT, W, dz, gam, offs, soffs, out_0, o
         coef_v = sb("coef_v", [P, 1])
         dot = sb("dot", [P, BLOCKS])
         coef = sb("coef", [P, BLOCKS])
-        slope = sb("slope", [P, BLOCKS])
-        t1 = [sb("t1_%d" % ib, [P, D]) for ib in range(BLOCKS)]
         t2 = [sb("t2_%d" % ib, [P, D]) for ib in range(BLOCKS)]
         y = [sb("y%d" % j, [P, SLOTS]) for j in range(BLOCKS)]
+        rstd_row = sb("rstd_row", [P, SLOTS])
 
         def add_turned(out, ib, j):
-            nc.tensor.matmul(out, t1[ib][:, cols(j)], ident[:], start=True, stop=False, is_transpose=True)
+            nc.tensor.matmul(out, h[ib][:, cols(j)], ident[:], start=True, stop=False, is_transpose=True)
             nc.tensor.matmul(out, t2[ib][:, cols(j)], ident[:], start=False, stop=True, is_transpose=True)
+
+        def spread_rstd(ibs):
+            row_ps = bank("row_ps")
+            for ib in ibs:
+                nc.tensor.transpose(row_ps[:, cols(ib)], rstd[:, ib : ib + 1].to_broadcast([P, P]), ident[:])
+            span = slice(ibs[0] * P, (ibs[-1] + 1) * P)
+            nc.scalar.copy(rstd_row[:, span], row_ps[:, span])
 
         nc.vector.tensor_tensor(a_got[last][:, cols(0)], a_tab[last][:].indirect(tok[:, entries(0, 1)]),
                                 b_got[last][:, cols(0)], ALU.add)
-        turn_x(last, [0], [0])
+        turn(a_got, last, [0], True, True)
         partial_sums(0, 1)
         nc.scalar.activation(mean[:, 0:1], mean_part[:, 1, 0:1], ACT.Identity, bias=mean_part[:, 0, 0:1])
         nc.vector.reciprocal(inv_mean[:, 0:1], mean[:, 0:1])
         nc.scalar.activation(rstd[:, 0:1], inv_mean[:, 0:1], ACT.Sqrt)
         nc.vector.tensor_scalar(coef_v[:], dot_part[:, 0, 0:1], dot_part[:, 1, 0:1], inv_mean[:, 0:1], ALU.add, ALU.mult)
-        nc.vector.tensor_scalar(t2[0][:], x[0][:], coef_v[:], rstd[:, 0:1], ALU.mult, ALU.mult)
-        nc.scalar.activation(t1[0][:, cols(0)], h_ps[0][:, cols(0)], ACT.Copy, scale=rstd[:, 0:1])
+        nc.vector.tensor_scalar(t2[0][:, cols(0)], x_ps[0][:, cols(0)], coef_v[:], None, ALU.mult)
+        spread_rstd([0])
         y_first = bank("y_first")
         add_turned(y_first[:, cols(0)], 0, 0)
         nc.scalar.copy(y[0][:, cols(0)], y_first[:, cols(0)])
-        nc.scalar.activation(t1[0][:, P:D], h_ps[0][:, P:D], ACT.Copy, scale=rstd[:, 0:1])
+        nc.vector.tensor_scalar(t2[0][:, P:D], x_ps[0][:, P:D], coef_v[:], None, ALU.mult)
         y_next = bank("y_next")
-        for j in range(1, BLOCKS):
+        for j in rest:
             add_turned(y_next[:, cols(j)], 0, j)
-        for j in range(1, BLOCKS):
+        for j in rest:
             nc.scalar.copy(y[j][:, cols(0)], y_next[:, cols(j)])
 
-        rest = range(1, BLOCKS)
         nc.vector.tensor_copy(a_got[last][:, P:SLOTS], a_tab[last][:].indirect(tok[:, entries(1, BLOCKS)]))
-        turn_x(last, rest, [])
+        turn(a_got, last, rest, False, True)
         for ib in rest:
             partial_sums(ib, 1)
         for ib in rest:
@@ -200,20 +218,22 @@ def tile_attend_gtwoemb_rms_kernel(tc, aT, bT, W, dz, gam, offs, soffs, out_0, o
         nc.scalar.activation(rstd[:, 1:BLOCKS], inv_mean[:, 1:BLOCKS], ACT.Sqrt)
         for ib in rest:
             nc.scalar.activation(coef[:, ib : ib + 1], dot[:, ib : ib + 1], ACT.Copy, scale=inv_mean[:, ib : ib + 1])
-        for ib in rest:
-            nc.scalar.activation(slope[:, ib : ib + 1], coef[:, ib : ib + 1], ACT.Copy, scale=rstd[:, ib : ib + 1])
+        spread_rstd(list(rest))
 
-        for j in range(BLOCKS):
-            nc.vector.tensor_copy(win1[j][:].indirect(seg[:, entries(0, 1)]), y[j][:, cols(0)])
+        def scatter(window, offsets, j, span):
+            nc.vector.tensor_tensor(window[:].indirect(offsets), y[j][:, span], rstd_row[:, span], ALU.mult)
 
-        for j in range(BLOCKS):
+        for j in every:
+            scatter(win1[j], seg[:, entries(0, 1)], j, cols(0))
+
+        for j in every:
             y_ps = bank("y_ps")
             for ib in rest:
-                nc.scalar.activation(t1[ib][:, cols(j)], h_ps[ib][:, cols(j)], ACT.Copy, scale=rstd[:, ib : ib + 1])
-                nc.scalar.activation(t2[ib][:, cols(j)], x[ib][:, cols(j)], ACT.Copy, scale=slope[:, ib : ib + 1])
+                nc.scalar.activation(t2[ib][:, cols(j)], x_ps[ib][:, cols(j)], ACT.Copy, scale=coef[:, ib : ib + 1])
+            for ib in rest:
                 add_turned(y_ps[:, cols(ib)], ib, j)
             nc.scalar.copy(y[j][:, P:SLOTS], y_ps[:, P:SLOTS])
-            nc.vector.tensor_copy(win0[j][:].indirect(tok[:]), y[j][:])
+            scatter(win0[j], tok[:], j, slice(0, SLOTS))
             nc.sync.dma_start(out_0[cols(j), :], win0[j][:])
-            nc.vector.tensor_copy(win1[j][:].indirect(seg[:, entries(1, BLOCKS)]), y[j][:, P:SLOTS])
+            scatter(win1[j], seg[:, entries(1, BLOCKS)], j, slice(P, SLOTS))
             nc.sync.dma_start(out_1[cols(j), :], win1[j][:])

@@ -14,6 +14,7 @@ E4M3 = mybir.dt.float8_e4m3fn_x4
 E5M2 = mybir.dt.float8_e5m2_x4
 ACT = mybir.ActivationFunctionType
 ALU = mybir.AluOpType
+AXIS = mybir.AxisListType
 
 P = 128
 PACK = 4
@@ -22,29 +23,36 @@ SLOTS = 512
 TOKENS = 2048
 SEGMENTS = 1024
 BLOCKS = 4
+LAST = BLOCKS - 1
 HALF = D // 2
 
 
-def cols(block):
-    return slice(block * P, (block + 1) * P)
+def cols(first, end=None):
+    return slice(first * P, (first + 1 if end is None else end) * P)
 
 
-def entries(first_block, last_block):
-    return slice(first_block * P // 16, last_block * P // 16)
+def entries(first, end):
+    return slice(first * P // 16, end * P // 16)
+
+
+def block_rows(table, j):
+    return table.rearrange("(p j) c -> j p c", j=BLOCKS)[j]
 
 
 def tile_attend_gtwoemb_rms_kernel(tc, aT, bT, W, dz, gam, offs, soffs, out_0, out_1):
     nc = tc.nc
     with ExitStack() as ctx:
         pool = ctx.enter_context(tc.tile_pool(name="pool", bufs=1))
-        held = ctx.enter_context(tc.psum_pool(name="held", bufs=1))
-        ring = ctx.enter_context(tc.psum_pool(name="ring", bufs=4))
+        psum = ctx.enter_context(tc.psum_pool(name="psum", bufs=1))
 
-        def sb(name, shape, dtype=F32):
-            return pool.tile(shape, dtype, name=name, align_bytes=64)
+        def sb(name, shape, dtype=F32, tag=None):
+            return pool.tile(shape, dtype, name=name, tag=tag or name, align_bytes=64)
 
-        def bank(name):
-            return ring.tile([P, SLOTS], F32, name=name, tag="bank")
+        def bank(name, tag):
+            return psum.tile([P, SLOTS], F32, name=name, tag=tag)
+
+        every = range(BLOCKS)
+        rest = range(1, BLOCKS)
 
         dz_raw = sb("dz_raw", [P, PACK, SLOTS])
         nc.sync.dma_start(dz_raw[:], dz.rearrange("(p t) i -> p t i", t=PACK))
@@ -54,16 +62,13 @@ def tile_attend_gtwoemb_rms_kernel(tc, aT, bT, W, dz, gam, offs, soffs, out_0, o
         nc.sync.dma_start(tok[:], offs)
         seg = pool.tile([P, SLOTS // 16], U16, name="seg")
         nc.sync.dma_start(seg[:], soffs)
-        gam_rows = sb("gam_rows", [P, P])
-        nc.sync.dma_start(gam_rows[:], gam.rearrange("r (j c) -> (r j) c", c=P)[0:P, :])
-        a_tab = [sb("a_tab%d" % j, [P, TOKENS]) for j in range(BLOCKS)]
-        b_tab = [sb("b_tab%d" % j, [P, SEGMENTS]) for j in range(BLOCKS)]
-        order = [("b", 0), ("a", 0), ("b", 1), ("a", 1), ("b", 2), ("b", 3), ("a", 2), ("a", 3)]
-        for which, j in order:
-            if which == "a":
-                nc.sync.dma_start(a_tab[j][:], aT[cols(j), :])
-            else:
-                nc.sync.dma_start(b_tab[j][:], bT[cols(j), :])
+        gam_col = sb("gam_col", [P, BLOCKS])
+        nc.sync.dma_start(gam_col[:], gam[0:1, :].rearrange("r (p j) -> (r p) j", j=BLOCKS))
+        a_tab = [sb("a_tab%d" % j, [P, TOKENS]) for j in every]
+        b_tab = [sb("b_tab%d" % j, [P, SEGMENTS]) for j in every]
+        for j in every:
+            nc.sync.dma_start(b_tab[j][:], block_rows(bT, j))
+            nc.sync.dma_start(a_tab[j][:], block_rows(aT, j))
 
         ident = sb("ident", [P, P])
         make_identity(nc, ident[:])
@@ -72,168 +77,197 @@ def tile_attend_gtwoemb_rms_kernel(tc, aT, bT, W, dz, gam, offs, soffs, out_0, o
         warm = sb("warm", [P, 1])
         nc.scalar.activation(warm[:], one[:], ACT.Sqrt)
 
-        win1 = [sb("win1_%d" % j, [P, SEGMENTS]) for j in range(BLOCKS)]
+        win1 = [sb("win1_%d" % j, [P, SEGMENTS]) for j in every]
         win0 = [sb("win0_%d" % j, [P, TOKENS]) for j in range(2)]
         for window in win1 + win0:
-            nc.vector.memset(window[:], 0.0)
+            nc.vector.memset(window[:].bitcast(U32), 0)
 
-        def quantise(name, raw, fmt, copy, tag):
-            width = raw.shape[2]
-            woven = pool.tile([P, width, PACK], BF16, name=name + "_woven", tag=tag, align_bytes=64)
-            copy(
-                woven[:].rearrange("p (c i) t -> p c t i", i=4),
-                raw.rearrange("p t (c i) -> p c t i", i=4),
-            )
+        def quantise(name, woven, fmt):
+            width = woven.shape[1]
             codes = sb(name + "_codes", [P, width], U32)
             scales = sb(name + "_scales", [P, width], U8)
-            return woven, codes, scales, fmt
-
-        def run_quantise(woven, codes, scales, fmt):
             nc.vector.quantize_mx(out=codes[:].bitcast(fmt), scales=scales[:], in_=woven[:].rearrange("p c t -> p (c t)"))
+            return codes, scales
 
-        dz_q = quantise("dz", dz_raw[:], E5M2, nc.vector.tensor_copy, "dz_woven")
-        run_quantise(*dz_q)
-        w_q = [
-            quantise("w0", w_raw[:, :, 0:HALF], E4M3, nc.vector.tensor_copy, "late0"),
-            quantise("w1", w_raw[:, :, HALF:D], E4M3, nc.scalar.copy, "late1"),
-        ]
-        for q in w_q:
-            run_quantise(*q)
-        for j in range(2, BLOCKS):
-            window = pool.tile([P, TOKENS], F32, name="win0_%d" % j, tag="late%d" % (BLOCKS - 1 - j), align_bytes=64)
-            nc.gpsimd.memset(window[:], 0.0)
-            win0.append(window)
+        dz_woven = sb("dz_woven", [P, SLOTS, PACK], BF16)
+        nc.vector.tensor_copy(dz_woven[:].rearrange("p (c i) t -> p c t i", i=4), dz_raw[:].rearrange("p t (c i) -> p c t i", i=4))
+        dz_codes, dz_scales = quantise("dz", dz_woven, E5M2)
+        w_woven = [sb("w_woven%d" % half, [P, HALF, PACK], BF16) for half in range(2)]
+        for half, copy in enumerate((nc.vector.tensor_copy, nc.scalar.copy)):
+            copy(w_woven[half][:].rearrange("p (u m) t -> p m t u", u=2),
+                 w_raw[:].rearrange("p t (m j) -> p m t j", j=BLOCKS)[:, :, :, 2 * half : 2 * half + 2])
+        w_q = [quantise("w%d" % half, w_woven[half], E4M3) for half in range(2)]
 
-        gam_ps = bank("gam_ps")
-        nc.tensor.transpose(gam_ps[:, 0:P], gam_rows[:], ident[:])
-        gam_col = sb("gam_col", [P, BLOCKS])
-        nc.scalar.copy(gam_col[:], gam_ps[:, 0:BLOCKS])
+        def turn(out, src, start=True, stop=True):
+            nc.tensor.matmul(out, src, ident[:], start=start, stop=stop, is_transpose=True)
 
-        hT = [sb("hT%d" % j, [P, SLOTS]) for j in range(BLOCKS)]
-        for j in range(BLOCKS):
-            dn_ps = bank("dn_ps")
-            nc.tensor.matmul_mx(
-                out=dn_ps[:],
-                lhsT=w_q[j // 2][1][:, cols(j % 2)].bitcast(E4M3),
-                lhsT_scale=w_q[j // 2][2][:, cols(j % 2)],
-                rhs=dz_q[1][:].bitcast(E5M2),
-                rhs_scale=dz_q[2][:],
-                start=True,
-                stop=True,
-            )
-            nc.scalar.activation(hT[j][:], dn_ps[:], ACT.Copy, scale=gam_col[:, j : j + 1])
-        h = [sb("h%d" % ib, [P, D]) for ib in range(BLOCKS)]
-        for ib in range(BLOCKS):
-            h_ps = bank("h_ps")
-            for j in range(BLOCKS):
-                nc.tensor.transpose(h_ps[:, cols(j)], hT[j][:, cols(ib)], ident[:])
-            nc.scalar.copy(h[ib][:], h_ps[:])
+        neg_gam = sb("neg_gam", [P, BLOCKS])
+        nc.gpsimd.tensor_scalar(neg_gam[:], gam_col[:], -1.0, 0.0, ALU.mult, ALU.add)
+        xT = [sb("xT%d" % j, [P, SLOTS]) for j in every]
+        neg_hT = [sb("neg_hT%d" % j, [P, SLOTS]) for j in every]
+        neg_h_first = xT[LAST][:, cols(2)]
 
-        x_ps = [held.tile([P, D], F32, name="x_ps%d" % ib) for ib in range(BLOCKS)]
-        a_got = [sb("a_got%d" % j, [P, SLOTS]) for j in range(BLOCKS)]
-        b_got = [sb("b_got%d" % j, [P, SLOTS]) for j in range(BLOCKS)]
-        mean_part = sb("mean_part", [P, 2, BLOCKS])
-        dot_part = sb("dot_part", [P, 2, BLOCKS])
-        junk_s = sb("junk_s", [P, HALF])
-        junk_v = sb("junk_v", [P, HALF])
+        def neg_h_cols(j, first, end):
+            return neg_h_first if (j, first) == (LAST, 0) else neg_hT[j][:, cols(first, end)]
 
-        def turn(got, j, ibs, start, stop):
-            for ib in ibs:
-                nc.tensor.matmul(x_ps[ib][:, cols(j)], got[j][:, cols(ib)], ident[:], start=start, stop=stop, is_transpose=True)
+        for j in every:
+            dn_ps = bank("dn_ps", "x%d" % j)
+            codes, scales = w_q[j // 2]
+            nc.tensor.matmul_mx(out=dn_ps[:], lhsT=codes[:, cols(j % 2)].bitcast(E4M3), lhsT_scale=scales[:, cols(j % 2)],
+                                rhs=dz_codes[:].bitcast(E5M2), rhs_scale=dz_scales[:], start=True, stop=True)
+            for first, end in ((0, BLOCKS),) if j < LAST else ((0, 1), (1, BLOCKS)):
+                nc.scalar.activation(neg_h_cols(j, first, end), dn_ps[:, cols(first, end)], ACT.Copy, scale=neg_gam[:, j : j + 1])
+        h = [sb("h%d" % ib, [P, D]) for ib in every]
 
-        def partial_sums(ib, half):
-            span = slice(half * HALF, (half + 1) * HALF)
-            nc.scalar.activation(junk_s[:], x_ps[ib][:, span], ACT.Square, scale=float(D) ** -0.5,
-                                 accum_out=mean_part[:, half, ib : ib + 1])
-            nc.vector.scalar_tensor_tensor(junk_v[:], x_ps[ib][:, span], -1.0 / D, h[ib][:, span], ALU.mult, ALU.mult,
-                                           accum_out=dot_part[:, half, ib : ib + 1])
+        def turn_h(ib):
+            h_ps = bank("h_ps", "spare")
+            for j in every:
+                turn(h_ps[:, cols(j)], neg_h_cols(j, ib, ib + 1))
+            nc.scalar.activation(h[ib][:], h_ps[:], ACT.Copy, scale=-1.0)
 
-        last = BLOCKS - 1
-        every = range(BLOCKS)
-        rest = range(1, BLOCKS)
-        for which, j in order[:-1]:
-            if which == "a":
-                nc.vector.tensor_copy(a_got[j][:], a_tab[j][:].indirect(tok[:]))
-                turn(b_got, j, every, True, False)
-                turn(a_got, j, every, False, True)
-            else:
-                nc.vector.tensor_copy(b_got[j][:], b_tab[j][:].indirect(seg[:]))
-                if j == last:
-                    for ib in every:
-                        partial_sums(ib, 0)
-        turn(b_got, last, rest, True, False)
+        x_ps = [bank("x_ps%d" % ib, "x%d" % ib) for ib in every]
+        first_sums = bank("first_sums", "sums0")
+        mean_sums = bank("mean_sums", "sums1")
+        dot_sums = bank("dot_sums", "sums2")
+        b_got = [sb("b_got%d" % j, [P, SLOTS]) for j in every]
+        squares = [sb("squares%d" % j, [P, SLOTS]) for j in every]
+        products = [sb("products%d" % j, [P, SLOTS]) for j in every]
+        t2 = [sb("t2_%d" % ib, [P, D]) for ib in every]
 
-        mean = sb("mean", [P, BLOCKS])
-        inv_mean = sb("inv_mean", [P, BLOCKS])
+        def gather_b(j):
+            nc.vector.tensor_copy(b_got[j][:], b_tab[j][:].indirect(seg[:]))
+
+        def gather_a(j, first, end):
+            span = cols(first, end)
+            nc.vector.tensor_tensor(xT[j][:, span], a_tab[j][:].indirect(tok[:, entries(first, end)]), b_got[j][:, span], ALU.add)
+
+        def terms(j, first, end, engine, square_from=None):
+            span = cols(first, end)
+            engine.tensor_tensor(products[j][:, span], xT[j][:, span], neg_h_cols(j, first, end), ALU.mult)
+            span = cols(first if square_from is None else square_from, end)
+            nc.scalar.activation(squares[j][:, span], xT[j][:, span], ACT.Square)
+
+        def sum_first(j):
+            turn(first_sums[:, cols(0)], squares[j][:, cols(0)], j == 0, False)
+            turn(first_sums[:, cols(1)], products[j][:, cols(0)], False, j == LAST)
+            turn(x_ps[0][:, cols(j)], xT[j][:, cols(0)])
+
+        def sum_rest(j):
+            for ib in rest:
+                turn(mean_sums[:, cols(ib)], squares[j][:, cols(ib)], j == 0 and ib == 1, j == LAST and ib == LAST)
+            for ib in rest:
+                turn(dot_sums[:, cols(ib)], products[j][:, cols(ib)], j == 0 and ib == 1, j == LAST and ib == LAST)
+            for ib in rest:
+                turn(x_ps[ib][:, cols(j)], xT[j][:, cols(ib)])
+
+        for j in range(LAST):
+            gather_b(j)
+            gather_a(j, 0, BLOCKS)
+            terms(j, 0, BLOCKS, nc.gpsimd)
+            sum_first(j)
+            sum_rest(j)
+            turn_h(j)
+        gather_b(LAST)
+        turn_h(LAST)
+
+        inv0 = sb("inv0", [P, 1])
+        coef0 = sb("coef0", [P, 1])
+        sums = sb("sums", [P, BLOCKS])
+        inv = sb("inv", [P, BLOCKS])
         rstd = sb("rstd", [P, BLOCKS])
-        coef_v = sb("coef_v", [P, 1])
-        dot = sb("dot", [P, BLOCKS])
         coef = sb("coef", [P, BLOCKS])
-        t2 = [sb("t2_%d" % ib, [P, D]) for ib in range(BLOCKS)]
-        y = [sb("y%d" % j, [P, SLOTS]) for j in range(BLOCKS)]
+        scaled = sb("scaled", [P, SLOTS])
+        y_early = sb("y_early", [P, LAST, SLOTS])
+        y = [sb("y0", [P, SLOTS])[:], y_early[:, 0, :]]
         rstd_row = sb("rstd_row", [P, SLOTS])
 
         def add_turned(out, ib, j):
-            nc.tensor.matmul(out, h[ib][:, cols(j)], ident[:], start=True, stop=False, is_transpose=True)
-            nc.tensor.matmul(out, t2[ib][:, cols(j)], ident[:], start=False, stop=True, is_transpose=True)
+            turn(out, h[ib][:, cols(j)], True, False)
+            turn(out, t2[ib][:, cols(j)], False, True)
 
-        def spread_rstd(ibs):
-            row_ps = bank("row_ps")
-            for ib in ibs:
-                nc.tensor.transpose(row_ps[:, cols(ib)], rstd[:, ib : ib + 1].to_broadcast([P, P]), ident[:])
-            span = slice(ibs[0] * P, (ibs[-1] + 1) * P)
-            nc.scalar.copy(rstd_row[:, span], row_ps[:, span])
+        def spread_rstd(first, end, tag):
+            row_ps = bank("row_ps", tag)
+            for ib in range(first, end):
+                turn(row_ps[:, cols(ib)], rstd[:, ib : ib + 1].to_broadcast([P, P]))
+            nc.scalar.copy(rstd_row[:, cols(first, end)], row_ps[:, cols(first, end)])
 
-        nc.vector.tensor_tensor(a_got[last][:, cols(0)], a_tab[last][:].indirect(tok[:, entries(0, 1)]),
-                                b_got[last][:, cols(0)], ALU.add)
-        turn(a_got, last, [0], True, True)
-        partial_sums(0, 1)
-        nc.scalar.activation(mean[:, 0:1], mean_part[:, 1, 0:1], ACT.Identity, bias=mean_part[:, 0, 0:1])
-        nc.vector.reciprocal(inv_mean[:, 0:1], mean[:, 0:1])
-        nc.scalar.activation(rstd[:, 0:1], inv_mean[:, 0:1], ACT.Sqrt)
-        nc.vector.tensor_scalar(coef_v[:], dot_part[:, 0, 0:1], dot_part[:, 1, 0:1], inv_mean[:, 0:1], ALU.add, ALU.mult)
-        nc.vector.tensor_scalar(t2[0][:, cols(0)], x_ps[0][:, cols(0)], coef_v[:], None, ALU.mult)
-        spread_rstd([0])
-        y_first = bank("y_first")
+        def scale_x(ib, first, end, factor):
+            nc.scalar.activation(t2[ib][:, cols(first, end)], x_ps[ib][:, cols(first, end)], ACT.Copy, scale=factor)
+
+        def scatter(window, offsets, j, first, end, values=None):
+            span = cols(first, end)
+            nc.vector.tensor_tensor(window[:].indirect(offsets[:, entries(first, end)]), y[j][:, span] if values is None else values,
+                                    rstd_row[:, span], ALU.mult)
+
+        def product(j, first, end, engine):
+            span = cols(first, end)
+            engine.tensor_tensor(products[j][:, span], xT[j][:, span], neg_h_cols(j, first, end), ALU.mult)
+
+        gather_a(LAST, 0, 1)
+        gather_a(LAST, 1, 2)
+        terms(LAST, 0, 1, nc.vector)
+        sum_first(LAST)
+        product(LAST, 1, 2, nc.gpsimd)
+        gather_a(LAST, 2, BLOCKS)
+        terms(LAST, 2, BLOCKS, nc.gpsimd, 1)
+        sums0 = sums[:, 1:3]
+        nc.vector.tensor_reduce(sums0, first_sums[:, cols(0, 2)].rearrange("p (k c) -> p k c", c=P), AXIS.X, ALU.add)
+        nc.vector.reciprocal(inv0[:], sums0[:, 0:1])
+        nc.vector.tensor_scalar(t2[0][:, cols(0)], x_ps[0][:, cols(0)], sums0[:, 1:2], inv0[:], ALU.mult, ALU.mult)
+        nc.scalar.activation(rstd[:, 0:1], inv0[:], ACT.Sqrt, scale=float(D))
+        nc.scalar.activation(coef0[:], sums0[:, 1:2], ACT.Copy, scale=inv0[:])
+        scale_x(0, 1, 2, coef0[:])
+        spread_rstd(0, 1, "spare")
+        y_first = bank("y_first", "sums0")
         add_turned(y_first[:, cols(0)], 0, 0)
         nc.scalar.copy(y[0][:, cols(0)], y_first[:, cols(0)])
-        nc.vector.tensor_scalar(t2[0][:, P:D], x_ps[0][:, P:D], coef_v[:], None, ALU.mult)
-        y_next = bank("y_next")
-        for j in rest:
+        sum_rest(LAST)
+        nc.vector.tensor_reduce(sums[:, 1:BLOCKS], mean_sums[:, cols(1, BLOCKS)].rearrange("p (k c) -> p k c", c=P), AXIS.X, ALU.add)
+        nc.vector.reciprocal(inv[:, 1:BLOCKS], sums[:, 1:BLOCKS])
+        scale_x(0, 2, BLOCKS, coef0[:])
+        y_second = bank("y_second", "spare")
+        add_turned(y_second[:, cols(0)], 0, 1)
+        nc.scalar.copy(y[1][:, cols(0)], y_second[:, cols(0)])
+        y_next = bank("y_next", "x0")
+        for j in (2, 3):
             add_turned(y_next[:, cols(j)], 0, j)
+
+        def coefficient(ib):
+            nc.scalar.activation(scaled[:, cols(ib)], dot_sums[:, cols(ib)], ACT.Copy, scale=inv[:, ib : ib + 1],
+                                 accum_out=coef[:, ib : ib + 1])
+            scale_x(ib, 0, 1, coef[:, ib : ib + 1])
+
+        nc.scalar.activation(rstd[:, 1:BLOCKS], inv[:, 1:BLOCKS], ACT.Sqrt, scale=float(D))
+        coefficient(1)
+        nc.scalar.copy(y_early[:, 1:LAST, cols(0)], y_next[:, cols(2, BLOCKS)].rearrange("p (j i) -> p j i", i=P))
+        spread_rstd(1, BLOCKS, "sums1")
+        y_ps = bank("y_ps", "sums0")
+        add_turned(y_ps[:, cols(1)], 1, 0)
+        nc.scalar.copy(y[0][:, cols(1)], y_ps[:, cols(1)])
+        for j in every:
+            scatter(win1[j], seg, j, 0, 1, None if j < 2 else y_early[:, j - 1, cols(0)])
+        scatter(win0[0], tok, 0, 0, 2)
+        y_ps = bank("y_ps", "spare")
+        for ib in (2, 3):
+            coefficient(ib)
+            add_turned(y_ps[:, cols(ib)], ib, 0)
+        nc.scalar.copy(y[0][:, cols(2, BLOCKS)], y_ps[:, cols(2, BLOCKS)])
+        scatter(win1[0], seg, 0, 1, BLOCKS)
+        nc.sync.dma_start(block_rows(out_1, 0), win1[0][:])
+        scatter(win0[0], tok, 0, 2, BLOCKS)
+        nc.sync.dma_start(block_rows(out_0, 0), win0[0][:])
+
         for j in rest:
-            nc.scalar.copy(y[j][:, cols(0)], y_next[:, cols(j)])
-
-        nc.vector.tensor_copy(a_got[last][:, P:SLOTS], a_tab[last][:].indirect(tok[:, entries(1, BLOCKS)]))
-        turn(a_got, last, rest, False, True)
-        for ib in rest:
-            partial_sums(ib, 1)
-        for ib in rest:
-            nc.scalar.activation(mean[:, ib : ib + 1], mean_part[:, 1, ib : ib + 1], ACT.Identity,
-                                 bias=mean_part[:, 0, ib : ib + 1])
-        nc.vector.reciprocal(inv_mean[:, 1:BLOCKS], mean[:, 1:BLOCKS])
-        for ib in rest:
-            nc.scalar.activation(dot[:, ib : ib + 1], dot_part[:, 1, ib : ib + 1], ACT.Identity,
-                                 bias=dot_part[:, 0, ib : ib + 1])
-        nc.scalar.activation(rstd[:, 1:BLOCKS], inv_mean[:, 1:BLOCKS], ACT.Sqrt)
-        for ib in rest:
-            nc.scalar.activation(coef[:, ib : ib + 1], dot[:, ib : ib + 1], ACT.Copy, scale=inv_mean[:, ib : ib + 1])
-        spread_rstd(list(rest))
-
-        def scatter(window, offsets, j, span):
-            nc.vector.tensor_tensor(window[:].indirect(offsets), y[j][:, span], rstd_row[:, span], ALU.mult)
-
-        for j in every:
-            scatter(win1[j], seg[:, entries(0, 1)], j, cols(0))
-
-        for j in every:
-            y_ps = bank("y_ps")
+            y_ps = bank("y_ps", "sums%d" % j if j < LAST else "sums0")
             for ib in rest:
-                nc.scalar.activation(t2[ib][:, cols(j)], x_ps[ib][:, cols(j)], ACT.Copy, scale=coef[:, ib : ib + 1])
+                scale_x(ib, j, j + 1, coef[:, ib : ib + 1])
             for ib in rest:
                 add_turned(y_ps[:, cols(ib)], ib, j)
-            nc.scalar.copy(y[j][:, P:SLOTS], y_ps[:, P:SLOTS])
-            scatter(win0[j], tok[:], j, slice(0, SLOTS))
-            nc.sync.dma_start(out_0[cols(j), :], win0[j][:])
-            scatter(win1[j], seg[:, entries(1, BLOCKS)], j, slice(P, SLOTS))
-            nc.sync.dma_start(out_1[cols(j), :], win1[j][:])
+            if j >= 2:
+                y.append(sb("y%d" % j, [P, SLOTS], tag="win1_%d" % (j - 2))[:])
+                nc.scalar.copy(y[j][:, cols(0)], y_early[:, j - 1, cols(0)])
+            nc.scalar.copy(y[j][:, cols(1, BLOCKS)], y_ps[:, cols(1, BLOCKS)])
+            scatter(win0[j % 2], tok, j, 0, BLOCKS)
+            nc.sync.dma_start(block_rows(out_0, j), win0[j % 2][:])
+            scatter(win1[j], seg, j, 1, BLOCKS)
+            nc.sync.dma_start(block_rows(out_1, j), win1[j][:])

@@ -90,12 +90,12 @@ def tile_attend_gtwoemb_rms_kernel(tc, aT, bT, W, dz, gam, offs, soffs, out_0, o
             return codes, scales
 
         dz_woven = sb("dz_woven", [P, SLOTS, PACK], BF16)
-        nc.vector.tensor_copy(dz_woven[:].rearrange("p (c i) t -> p c t i", i=4), dz_raw[:].rearrange("p t (c i) -> p c t i", i=4))
+        nc.scalar.copy(dz_woven[:].rearrange("p (c i) t -> p c t i", i=4), dz_raw[:].rearrange("p t (c i) -> p c t i", i=4))
         dz_codes, dz_scales = quantise("dz", dz_woven, E5M2)
         w_woven = [sb("w_woven%d" % half, [P, HALF, PACK], BF16) for half in range(2)]
-        for half, copy in enumerate((nc.vector.tensor_copy, nc.scalar.copy)):
-            copy(w_woven[half][:].rearrange("p (u m) t -> p m t u", u=2),
-                 w_raw[:].rearrange("p t (m j) -> p m t j", j=BLOCKS)[:, :, :, 2 * half : 2 * half + 2])
+        for half in range(2):
+            nc.scalar.copy(w_woven[half][:].rearrange("p (u m) t -> p m t u", u=2),
+                           w_raw[:].rearrange("p t (m j) -> p m t j", j=BLOCKS)[:, :, :, 2 * half : 2 * half + 2])
         w_q = [quantise("w%d" % half, w_woven[half], E4M3) for half in range(2)]
 
         def turn(out, src, start=True, stop=True):

@@ -157,6 +157,8 @@ def tile_attend_gtwoemb_rms_kernel(tc, aT, bT, W, dz, gam, offs, soffs, out_0, o
                 turn(mean_sums[:, cols(ib)], squares[j][:, cols(ib)], j == 0 and ib == 1, j == LAST and ib == LAST)
             for ib in rest:
                 turn(dot_sums[:, cols(ib)], products[j][:, cols(ib)], j == 0 and ib == 1, j == LAST and ib == LAST)
+
+        def turn_x_rest(j):
             for ib in rest:
                 turn(x_ps[ib][:, cols(j)], xT[j][:, cols(ib)])
 
@@ -166,6 +168,7 @@ def tile_attend_gtwoemb_rms_kernel(tc, aT, bT, W, dz, gam, offs, soffs, out_0, o
             terms(j, 0, BLOCKS, nc.gpsimd)
             sum_first(j)
             sum_rest(j)
+            turn_x_rest(j)
             turn_h(j)
         gather_b(LAST)
         turn_h(LAST)
@@ -178,7 +181,7 @@ def tile_attend_gtwoemb_rms_kernel(tc, aT, bT, W, dz, gam, offs, soffs, out_0, o
         coef = sb("coef", [P, BLOCKS])
         scaled = sb("scaled", [P, SLOTS])
         y_early = sb("y_early", [P, LAST, SLOTS])
-        y = [sb("y0", [P, SLOTS])[:], y_early[:, 0, :]]
+        y = [sb("y0", [P, SLOTS])[:]] + [y_early[:, j - 1, :] for j in rest]
         rstd_row = sb("rstd_row", [P, SLOTS])
 
         def add_turned(out, ib, j):
@@ -207,7 +210,7 @@ def tile_attend_gtwoemb_rms_kernel(tc, aT, bT, W, dz, gam, offs, soffs, out_0, o
         gather_a(LAST, 1, 2)
         terms(LAST, 0, 1, nc.vector)
         sum_first(LAST)
-        product(LAST, 1, 2, nc.gpsimd)
+        product(LAST, 1, 2, nc.vector)
         gather_a(LAST, 2, BLOCKS)
         terms(LAST, 2, BLOCKS, nc.gpsimd, 1)
         sums0 = sums[:, 1:3]
@@ -245,29 +248,33 @@ def tile_attend_gtwoemb_rms_kernel(tc, aT, bT, W, dz, gam, offs, soffs, out_0, o
         add_turned(y_ps[:, cols(1)], 1, 0)
         nc.scalar.copy(y[0][:, cols(1)], y_ps[:, cols(1)])
         for j in every:
-            scatter(win1[j], seg, j, 0, 1, None if j < 2 else y_early[:, j - 1, cols(0)])
+            scatter(win1[j], seg, j, 0, 1)
         scatter(win0[0], tok, 0, 0, 2)
         y_ps = bank("y_ps", "spare")
         for ib in (2, 3):
             coefficient(ib)
             add_turned(y_ps[:, cols(ib)], ib, 0)
         nc.scalar.copy(y[0][:, cols(2, BLOCKS)], y_ps[:, cols(2, BLOCKS)])
+        turn_x_rest(LAST)
         scatter(win1[0], seg, 0, 1, BLOCKS)
         nc.sync.dma_start(block_rows(out_1, 0), win1[0][:])
         scatter(win0[0], tok, 0, 2, BLOCKS)
         nc.sync.dma_start(block_rows(out_0, 0), win0[0][:])
 
         for j in rest:
-            y_ps = bank("y_ps", "sums%d" % j if j < LAST else "sums0")
+            y_ps = bank("y_ps", "sums%d" % (j % LAST))
             for ib in rest:
                 scale_x(ib, j, j + 1, coef[:, ib : ib + 1])
             for ib in rest:
                 add_turned(y_ps[:, cols(ib)], ib, j)
-            if j >= 2:
-                y.append(sb("y%d" % j, [P, SLOTS], tag="win1_%d" % (j - 2))[:])
-                nc.scalar.copy(y[j][:, cols(0)], y_early[:, j - 1, cols(0)])
             nc.scalar.copy(y[j][:, cols(1, BLOCKS)], y_ps[:, cols(1, BLOCKS)])
             scatter(win0[j % 2], tok, j, 0, BLOCKS)
             nc.sync.dma_start(block_rows(out_0, j), win0[j % 2][:])
-            scatter(win1[j], seg, j, 1, BLOCKS)
+            if j == 1:
+                scatter(win1[j], seg, j, 1, BLOCKS)
+                nc.sync.dma_start(block_rows(out_1, j), win1[j][:])
+        y_tail = sb("y_tail", [P, 2, LAST * P], tag="win1_1")
+        nc.scalar.copy(y_tail[:], y_early[:, 1:LAST, cols(1, BLOCKS)])
+        for j in (2, 3):
+            scatter(win1[j], seg, j, 1, BLOCKS, y_tail[:, j - 2, :])
             nc.sync.dma_start(block_rows(out_1, j), win1[j][:])

@@ -25,6 +25,8 @@ SEGMENTS = 1024
 BLOCKS = 4
 LAST = BLOCKS - 1
 HALF = D // 2
+LIST_ROWS = 16
+RUN = 4
 
 
 def cols(first, end=None):
@@ -32,7 +34,7 @@ def cols(first, end=None):
 
 
 def entries(first, end):
-    return slice(first * P // 16, end * P // 16)
+    return slice(first * P // LIST_ROWS, end * P // LIST_ROWS)
 
 
 def block_rows(table, j):
@@ -58,9 +60,9 @@ def tile_attend_gtwoemb_rms_kernel(tc, aT, bT, W, dz, gam, offs, soffs, out_0, o
         nc.sync.dma_start(dz_raw[:], dz.rearrange("(p t) i -> p t i", t=PACK))
         w_raw = sb("w_raw", [P, PACK, D])
         nc.sync.dma_start(w_raw[:], W.rearrange("(p t) d -> p t d", t=PACK))
-        tok = pool.tile([P, SLOTS // 16], U16, name="tok")
+        tok = pool.tile([P, SLOTS // LIST_ROWS], U16, name="tok")
         nc.sync.dma_start(tok[:], offs)
-        seg = pool.tile([P, SLOTS // 16], U16, name="seg")
+        seg = pool.tile([P, SLOTS // LIST_ROWS], U16, name="seg")
         nc.sync.dma_start(seg[:], soffs)
         gam_col = sb("gam_col", [P, BLOCKS])
         nc.sync.dma_start(gam_col[:], gam[0:1, :].rearrange("r (p j) -> (r p) j", j=BLOCKS))
@@ -78,7 +80,7 @@ def tile_attend_gtwoemb_rms_kernel(tc, aT, bT, W, dz, gam, offs, soffs, out_0, o
         nc.scalar.activation(warm[:], one[:], ACT.Sqrt)
 
         win1 = [sb("win1_%d" % j, [P, SEGMENTS]) for j in every]
-        win0 = [sb("win0_%d" % j, [P, TOKENS]) for j in range(2)]
+        win0 = [sb("win0_%d" % half, [P, TOKENS]) for half in range(2)]
         for window in win1 + win0:
             nc.vector.memset(window[:].bitcast(U32), 0)
 
@@ -90,12 +92,13 @@ def tile_attend_gtwoemb_rms_kernel(tc, aT, bT, W, dz, gam, offs, soffs, out_0, o
             return codes, scales
 
         dz_woven = sb("dz_woven", [P, SLOTS, PACK], BF16)
-        nc.scalar.copy(dz_woven[:].rearrange("p (c i) t -> p c t i", i=4), dz_raw[:].rearrange("p t (c i) -> p c t i", i=4))
+        nc.vector.tensor_copy(dz_woven[:].rearrange("p (c i) t -> p c t i", i=RUN),
+                              dz_raw[:].rearrange("p t (c i) -> p c t i", i=RUN))
         dz_codes, dz_scales = quantise("dz", dz_woven, E5M2)
         w_woven = [sb("w_woven%d" % half, [P, HALF, PACK], BF16) for half in range(2)]
-        for half in range(2):
-            nc.scalar.copy(w_woven[half][:].rearrange("p (u m) t -> p m t u", u=2),
-                           w_raw[:].rearrange("p t (m j) -> p m t j", j=BLOCKS)[:, :, :, 2 * half : 2 * half + 2])
+        for half, copy in enumerate((nc.vector.tensor_copy, nc.scalar.copy)):
+            copy(w_woven[half][:].rearrange("p (u m) t -> p m t u", u=2),
+                 w_raw[:].rearrange("p t (m j) -> p m t j", j=BLOCKS)[:, :, :, 2 * half : 2 * half + 2])
         w_q = [quantise("w%d" % half, w_woven[half], E4M3) for half in range(2)]
 
         def turn(out, src, start=True, stop=True):
@@ -106,6 +109,7 @@ def tile_attend_gtwoemb_rms_kernel(tc, aT, bT, W, dz, gam, offs, soffs, out_0, o
         xT = [sb("xT%d" % j, [P, SLOTS]) for j in every]
         neg_hT = [sb("neg_hT%d" % j, [P, SLOTS]) for j in every]
         neg_h_first = xT[LAST][:, cols(2)]
+        products = [sb("products%d" % j, [P, SLOTS + (BLOCKS if j == LAST else 0)]) for j in every]
 
         def neg_h_cols(j, first, end):
             return neg_h_first if (j, first) == (LAST, 0) else neg_hT[j][:, cols(first, end)]
@@ -118,21 +122,19 @@ def tile_attend_gtwoemb_rms_kernel(tc, aT, bT, W, dz, gam, offs, soffs, out_0, o
             for first, end in ((0, BLOCKS),) if j < LAST else ((0, 1), (1, BLOCKS)):
                 nc.scalar.activation(neg_h_cols(j, first, end), dn_ps[:, cols(first, end)], ACT.Copy, scale=neg_gam[:, j : j + 1])
         h = [sb("h%d" % ib, [P, D]) for ib in every]
-
-        def turn_h(ib):
-            h_ps = bank("h_ps", "spare")
+        for ib, tag in enumerate(("sums0", "sums1", "sums2", "spare")):
+            h_ps = bank("h_ps", tag)
             for j in every:
                 turn(h_ps[:, cols(j)], neg_h_cols(j, ib, ib + 1))
             nc.scalar.activation(h[ib][:], h_ps[:], ACT.Copy, scale=-1.0)
 
         x_ps = [bank("x_ps%d" % ib, "x%d" % ib) for ib in every]
         first_sums = bank("first_sums", "sums0")
-        mean_sums = bank("mean_sums", "sums1")
-        dot_sums = bank("dot_sums", "sums2")
+        square_sums = bank("square_sums", "sums1")
+        product_sums = bank("product_sums", "sums2")
         b_got = [sb("b_got%d" % j, [P, SLOTS]) for j in every]
         squares = [sb("squares%d" % j, [P, SLOTS]) for j in every]
-        products = [sb("products%d" % j, [P, SLOTS]) for j in every]
-        t2 = [sb("t2_%d" % ib, [P, D]) for ib in every]
+        shift = [sb("shift%d" % ib, [P, D]) for ib in every]
 
         def gather_b(j):
             nc.vector.tensor_copy(b_got[j][:], b_tab[j][:].indirect(seg[:]))
@@ -141,11 +143,14 @@ def tile_attend_gtwoemb_rms_kernel(tc, aT, bT, W, dz, gam, offs, soffs, out_0, o
             span = cols(first, end)
             nc.vector.tensor_tensor(xT[j][:, span], a_tab[j][:].indirect(tok[:, entries(first, end)]), b_got[j][:, span], ALU.add)
 
-        def terms(j, first, end, engine, square_from=None):
-            span = cols(first, end)
-            engine.tensor_tensor(products[j][:, span], xT[j][:, span], neg_h_cols(j, first, end), ALU.mult)
-            span = cols(first if square_from is None else square_from, end)
-            nc.scalar.activation(squares[j][:, span], xT[j][:, span], ACT.Square)
+        def product_cols(j, first, end):
+            return products[j][:, cols(0) if (j, first) == (LAST, 1) else cols(first, end)]
+
+        def square(j, first, end):
+            nc.scalar.activation(squares[j][:, cols(first, end)], xT[j][:, cols(first, end)], ACT.Square)
+
+        def product(j, first, end, engine):
+            engine.tensor_tensor(product_cols(j, first, end), xT[j][:, cols(first, end)], neg_h_cols(j, first, end), ALU.mult)
 
         def sum_first(j):
             turn(first_sums[:, cols(0)], squares[j][:, cols(0)], j == 0, False)
@@ -154,9 +159,9 @@ def tile_attend_gtwoemb_rms_kernel(tc, aT, bT, W, dz, gam, offs, soffs, out_0, o
 
         def sum_rest(j):
             for ib in rest:
-                turn(mean_sums[:, cols(ib)], squares[j][:, cols(ib)], j == 0 and ib == 1, j == LAST and ib == LAST)
+                turn(square_sums[:, cols(ib)], squares[j][:, cols(ib)], j == 0 and ib == 1, j == LAST and ib == LAST)
             for ib in rest:
-                turn(dot_sums[:, cols(ib)], products[j][:, cols(ib)], j == 0 and ib == 1, j == LAST and ib == LAST)
+                turn(product_sums[:, cols(ib)], product_cols(j, ib, ib + 1), j == 0 and ib == 1, j == LAST and ib == LAST)
 
         def turn_x_rest(j):
             for ib in rest:
@@ -165,28 +170,33 @@ def tile_attend_gtwoemb_rms_kernel(tc, aT, bT, W, dz, gam, offs, soffs, out_0, o
         for j in range(LAST):
             gather_b(j)
             gather_a(j, 0, BLOCKS)
-            terms(j, 0, BLOCKS, nc.gpsimd)
+            product(j, 0, BLOCKS, nc.gpsimd)
+            square(j, 0, BLOCKS)
             sum_first(j)
             sum_rest(j)
             turn_x_rest(j)
-            turn_h(j)
         gather_b(LAST)
-        turn_h(LAST)
 
         inv0 = sb("inv0", [P, 1])
         coef0 = sb("coef0", [P, 1])
-        sums = sb("sums", [P, BLOCKS])
+        sums = products[LAST][:, SLOTS : SLOTS + BLOCKS]
         inv = sb("inv", [P, BLOCKS])
         rstd = sb("rstd", [P, BLOCKS])
         coef = sb("coef", [P, BLOCKS])
-        scaled = sb("scaled", [P, SLOTS])
-        y_early = sb("y_early", [P, LAST, SLOTS])
-        y = [sb("y0", [P, SLOTS])[:]] + [y_early[:, j - 1, :] for j in rest]
+        terms = sb("terms", [P, SLOTS])
+        y_rest = sb("y_rest", [P, LAST, SLOTS])
+        y = [sb("y0", [P, SLOTS])[:]] + [y_rest[:, j - 1, :] for j in rest]
         rstd_row = sb("rstd_row", [P, SLOTS])
 
         def add_turned(out, ib, j):
             turn(out, h[ib][:, cols(j)], True, False)
-            turn(out, t2[ib][:, cols(j)], False, True)
+            turn(out, shift[ib][:, cols(j)], False, True)
+
+        def add_turned_group(y_bank, places):
+            for n, (place, ib, j) in enumerate(places):
+                turn(y_bank[:, cols(place)], h[ib][:, cols(j)], n == 0, False)
+            for n, (place, ib, j) in enumerate(places):
+                turn(y_bank[:, cols(place)], shift[ib][:, cols(j)], False, n == len(places) - 1)
 
         def spread_rstd(first, end, tag):
             row_ps = bank("row_ps", tag)
@@ -194,77 +204,76 @@ def tile_attend_gtwoemb_rms_kernel(tc, aT, bT, W, dz, gam, offs, soffs, out_0, o
                 turn(row_ps[:, cols(ib)], rstd[:, ib : ib + 1].to_broadcast([P, P]))
             nc.scalar.copy(rstd_row[:, cols(first, end)], row_ps[:, cols(first, end)])
 
-        def scale_x(ib, first, end, factor):
-            nc.scalar.activation(t2[ib][:, cols(first, end)], x_ps[ib][:, cols(first, end)], ACT.Copy, scale=factor)
+        def make_shift(ib, first, end, factor):
+            nc.scalar.activation(shift[ib][:, cols(first, end)], x_ps[ib][:, cols(first, end)], ACT.Copy, scale=factor)
 
         def scatter(window, offsets, j, first, end, values=None):
             span = cols(first, end)
             nc.vector.tensor_tensor(window[:].indirect(offsets[:, entries(first, end)]), y[j][:, span] if values is None else values,
                                     rstd_row[:, span], ALU.mult)
 
-        def product(j, first, end, engine):
-            span = cols(first, end)
-            engine.tensor_tensor(products[j][:, span], xT[j][:, span], neg_h_cols(j, first, end), ALU.mult)
-
         gather_a(LAST, 0, 1)
         gather_a(LAST, 1, 2)
-        terms(LAST, 0, 1, nc.vector)
+        product(LAST, 0, 1, nc.vector)
+        square(LAST, 0, 1)
         sum_first(LAST)
-        product(LAST, 1, 2, nc.vector)
+        square(LAST, 1, 2)
         gather_a(LAST, 2, BLOCKS)
-        terms(LAST, 2, BLOCKS, nc.gpsimd, 1)
-        sums0 = sums[:, 1:3]
+        square(LAST, 2, BLOCKS)
+        sums0 = products[LAST][:, SLOTS - 1 : SLOTS + 2 : 2]
         nc.vector.tensor_reduce(sums0, first_sums[:, cols(0, 2)].rearrange("p (k c) -> p k c", c=P), AXIS.X, ALU.add)
         nc.vector.reciprocal(inv0[:], sums0[:, 0:1])
-        nc.vector.tensor_scalar(t2[0][:, cols(0)], x_ps[0][:, cols(0)], sums0[:, 1:2], inv0[:], ALU.mult, ALU.mult)
+        product(LAST, 1, 2, nc.vector)
+        nc.vector.tensor_scalar(shift[0][:, cols(0)], x_ps[0][:, cols(0)], sums0[:, 1:2], inv0[:], ALU.mult, ALU.mult)
+        product(LAST, 2, BLOCKS, nc.vector)
         nc.scalar.activation(rstd[:, 0:1], inv0[:], ACT.Sqrt, scale=float(D))
         nc.scalar.activation(coef0[:], sums0[:, 1:2], ACT.Copy, scale=inv0[:])
-        scale_x(0, 1, 2, coef0[:])
+        make_shift(0, 1, 2, coef0[:])
         spread_rstd(0, 1, "spare")
         y_first = bank("y_first", "sums0")
         add_turned(y_first[:, cols(0)], 0, 0)
         nc.scalar.copy(y[0][:, cols(0)], y_first[:, cols(0)])
         sum_rest(LAST)
-        nc.vector.tensor_reduce(sums[:, 1:BLOCKS], mean_sums[:, cols(1, BLOCKS)].rearrange("p (k c) -> p k c", c=P), AXIS.X, ALU.add)
+        nc.vector.tensor_reduce(sums[:, 1:BLOCKS], square_sums[:, cols(1, BLOCKS)].rearrange("p (k c) -> p k c", c=P), AXIS.X, ALU.add)
         nc.vector.reciprocal(inv[:, 1:BLOCKS], sums[:, 1:BLOCKS])
-        scale_x(0, 2, BLOCKS, coef0[:])
+        make_shift(0, 2, BLOCKS, coef0[:])
         y_second = bank("y_second", "spare")
         add_turned(y_second[:, cols(0)], 0, 1)
         nc.scalar.copy(y[1][:, cols(0)], y_second[:, cols(0)])
-        y_next = bank("y_next", "x0")
-        for j in (2, 3):
-            add_turned(y_next[:, cols(j)], 0, j)
+        y_next = bank("y_next", "sums1")
+        add_turned_group(y_next, [(j, 0, j) for j in range(2, BLOCKS)])
 
-        def coefficient(ib):
-            nc.scalar.activation(scaled[:, cols(ib)], dot_sums[:, cols(ib)], ACT.Copy, scale=inv[:, ib : ib + 1],
+        def first_shift(ib):
+            nc.scalar.activation(terms[:, cols(ib)], product_sums[:, cols(ib)], ACT.Copy, scale=inv[:, ib : ib + 1],
                                  accum_out=coef[:, ib : ib + 1])
-            scale_x(ib, 0, 1, coef[:, ib : ib + 1])
+            make_shift(ib, 0, 1, coef[:, ib : ib + 1])
 
         nc.scalar.activation(rstd[:, 1:BLOCKS], inv[:, 1:BLOCKS], ACT.Sqrt, scale=float(D))
-        coefficient(1)
-        nc.scalar.copy(y_early[:, 1:LAST, cols(0)], y_next[:, cols(2, BLOCKS)].rearrange("p (j i) -> p j i", i=P))
-        spread_rstd(1, BLOCKS, "sums1")
+        first_shift(1)
+        nc.scalar.copy(y_rest[:, 1:LAST, cols(0)], y_next[:, cols(2, BLOCKS)].rearrange("p (j i) -> p j i", i=P))
+        spread_rstd(1, BLOCKS, "x0")
         y_ps = bank("y_ps", "sums0")
         add_turned(y_ps[:, cols(1)], 1, 0)
         nc.scalar.copy(y[0][:, cols(1)], y_ps[:, cols(1)])
         for j in every:
             scatter(win1[j], seg, j, 0, 1)
         scatter(win0[0], tok, 0, 0, 2)
+        scatter(win1[0], seg, 0, 1, 2)
         y_ps = bank("y_ps", "spare")
-        for ib in (2, 3):
-            coefficient(ib)
-            add_turned(y_ps[:, cols(ib)], ib, 0)
+        for ib in range(2, BLOCKS):
+            first_shift(ib)
+        add_turned_group(y_ps, [(ib, ib, 0) for ib in range(2, BLOCKS)])
         nc.scalar.copy(y[0][:, cols(2, BLOCKS)], y_ps[:, cols(2, BLOCKS)])
         turn_x_rest(LAST)
-        scatter(win1[0], seg, 0, 1, BLOCKS)
-        nc.sync.dma_start(block_rows(out_1, 0), win1[0][:])
         scatter(win0[0], tok, 0, 2, BLOCKS)
         nc.sync.dma_start(block_rows(out_0, 0), win0[0][:])
+        scatter(win1[0], seg, 0, 2, BLOCKS)
+        nc.sync.dma_start(block_rows(out_1, 0), win1[0][:])
 
         for j in rest:
             y_ps = bank("y_ps", "sums%d" % (j % LAST))
             for ib in rest:
-                scale_x(ib, j, j + 1, coef[:, ib : ib + 1])
+                make_shift(ib, j, j + 1, coef[:, ib : ib + 1])
             for ib in rest:
                 add_turned(y_ps[:, cols(ib)], ib, j)
             nc.scalar.copy(y[j][:, cols(1, BLOCKS)], y_ps[:, cols(1, BLOCKS)])
@@ -274,7 +283,7 @@ def tile_attend_gtwoemb_rms_kernel(tc, aT, bT, W, dz, gam, offs, soffs, out_0, o
                 scatter(win1[j], seg, j, 1, BLOCKS)
                 nc.sync.dma_start(block_rows(out_1, j), win1[j][:])
         y_tail = sb("y_tail", [P, 2, LAST * P], tag="win1_1")
-        nc.scalar.copy(y_tail[:], y_early[:, 1:LAST, cols(1, BLOCKS)])
-        for j in (2, 3):
+        nc.scalar.copy(y_tail[:], y_rest[:, 1:LAST, cols(1, BLOCKS)])
+        for j in range(2, BLOCKS):
             scatter(win1[j], seg, j, 1, BLOCKS, y_tail[:, j - 2, :])
             nc.sync.dma_start(block_rows(out_1, j), win1[j][:])

@@ -74,12 +74,12 @@ def tile_attend_gtwoemb_rms_kernel(tc, aT, bT, W, dz, gam, offs, soffs, out_0, o
 
         ident = sb("ident", [P, P])
         make_identity(nc, ident[:])
-        one = sb("one", [P, 1])
-        nc.gpsimd.memset(one[:], 1.0)
+        h = [sb("h%d" % ib, [P, D + (P if ib == 0 else 0)]) for ib in every]
+        nc.gpsimd.memset(h[0][:, cols(BLOCKS)], 1.0)
         warm = sb("warm", [P, 1])
-        nc.scalar.activation(warm[:], one[:], ACT.Sqrt)
+        nc.scalar.activation(warm[:], h[0][:, D : D + 1], ACT.Sqrt)
 
-        win1 = [sb("win1_%d" % j, [P, SEGMENTS]) for j in every]
+        win1 = [sb("win1_%d" % n, [P, SEGMENTS]) for n in every]
         win0 = [sb("win0_%d" % half, [P, TOKENS]) for half in range(2)]
         for window in win1 + win0:
             nc.vector.memset(window[:].bitcast(U32), 0)
@@ -104,186 +104,181 @@ def tile_attend_gtwoemb_rms_kernel(tc, aT, bT, W, dz, gam, offs, soffs, out_0, o
         def turn(out, src, start=True, stop=True):
             nc.tensor.matmul(out, src, ident[:], start=start, stop=stop, is_transpose=True)
 
-        neg_gam = sb("neg_gam", [P, BLOCKS])
-        nc.gpsimd.tensor_scalar(neg_gam[:], gam_col[:], -1.0, 0.0, ALU.mult, ALU.add)
-        xT = [sb("xT%d" % j, [P, SLOTS]) for j in every]
-        neg_hT = [sb("neg_hT%d" % j, [P, SLOTS]) for j in every]
-        neg_h_first = xT[LAST][:, cols(2)]
-        products = [sb("products%d" % j, [P, SLOTS + (BLOCKS if j == LAST else 0)]) for j in every]
-
-        def neg_h_cols(j, first, end):
-            return neg_h_first if (j, first) == (LAST, 0) else neg_hT[j][:, cols(first, end)]
-
+        hT = [sb("hT%d" % j, [P, SLOTS]) for j in every]
         for j in every:
             dn_ps = bank("dn_ps", "x%d" % j)
             codes, scales = w_q[j // 2]
             nc.tensor.matmul_mx(out=dn_ps[:], lhsT=codes[:, cols(j % 2)].bitcast(E4M3), lhsT_scale=scales[:, cols(j % 2)],
                                 rhs=dz_codes[:].bitcast(E5M2), rhs_scale=dz_scales[:], start=True, stop=True)
-            for first, end in ((0, BLOCKS),) if j < LAST else ((0, 1), (1, BLOCKS)):
-                nc.scalar.activation(neg_h_cols(j, first, end), dn_ps[:, cols(first, end)], ACT.Copy, scale=neg_gam[:, j : j + 1])
-        h = [sb("h%d" % ib, [P, D]) for ib in every]
-        for ib, tag in enumerate(("sums0", "sums1", "sums2", "spare")):
+            nc.scalar.activation(hT[j][:], dn_ps[:], ACT.Copy, scale=gam_col[:, j : j + 1])
+        for ib, tag in enumerate("ABCD"):
             h_ps = bank("h_ps", tag)
             for j in every:
-                turn(h_ps[:, cols(j)], neg_h_cols(j, ib, ib + 1))
-            nc.scalar.activation(h[ib][:], h_ps[:], ACT.Copy, scale=-1.0)
+                turn(h_ps[:, cols(j)], hT[j][:, cols(ib)])
+            nc.scalar.copy(h[ib][:, 0:D], h_ps[:])
 
         x_ps = [bank("x_ps%d" % ib, "x%d" % ib) for ib in every]
-        first_sums = bank("first_sums", "sums0")
-        square_sums = bank("square_sums", "sums1")
-        product_sums = bank("product_sums", "sums2")
+        first = bank("first", "A")
+        early = bank("early", "B")
         b_got = [sb("b_got%d" % j, [P, SLOTS]) for j in every]
-        squares = [sb("squares%d" % j, [P, SLOTS]) for j in every]
+        xT = [sb("xT%d" % j, [P, SLOTS]) for j in range(LAST)]
+        products = [sb("products%d" % j, [P, SLOTS]) for j in range(LAST)]
+        x_first = sb("x_first", [P, P])
+        a_late = sb("a_late", [P, LAST * P])
+        squares = [sb("squares%d" % ib, [P, D]) for ib in every]
+        first_terms = sb("first_terms", [P, 2 * P])
+        parts = sb("parts", [P, BLOCKS, 4])
+        dots = sb("dots", [P, BLOCKS, 2])
+        small = sb("small", [P, BLOCKS, 8])
+        s2 = sb("s2", [P, BLOCKS])
+        inv = sb("inv", [P, BLOCKS])
+        coef = sb("coef", [P, BLOCKS])
+        late_terms = sb("late_terms", [P, 2 * P])
+        dot0 = late_terms[:, 0:1]
+        inv0 = late_terms[:, P : P + 1]
         shift = [sb("shift%d" % ib, [P, D]) for ib in every]
 
         def gather_b(j):
             nc.vector.tensor_copy(b_got[j][:], b_tab[j][:].indirect(seg[:]))
 
-        def gather_a(j, first, end):
-            span = cols(first, end)
-            nc.vector.tensor_tensor(xT[j][:, span], a_tab[j][:].indirect(tok[:, entries(first, end)]), b_got[j][:, span], ALU.add)
+        def product(j, lo, hi):
+            nc.gpsimd.tensor_tensor(products[j][:, cols(lo, hi)], xT[j][:, cols(lo, hi)], hT[j][:, cols(lo, hi)], ALU.mult)
 
-        def product_cols(j, first, end):
-            return products[j][:, cols(0) if (j, first) == (LAST, 1) else cols(first, end)]
-
-        def square(j, first, end):
-            nc.scalar.activation(squares[j][:, cols(first, end)], xT[j][:, cols(first, end)], ACT.Square)
-
-        def product(j, first, end, engine):
-            engine.tensor_tensor(product_cols(j, first, end), xT[j][:, cols(first, end)], neg_h_cols(j, first, end), ALU.mult)
-
-        def sum_first(j):
-            turn(first_sums[:, cols(0)], squares[j][:, cols(0)], j == 0, False)
-            turn(first_sums[:, cols(1)], products[j][:, cols(0)], False, j == LAST)
-            turn(x_ps[0][:, cols(j)], xT[j][:, cols(0)])
-
-        def sum_rest(j):
-            for ib in rest:
-                turn(square_sums[:, cols(ib)], squares[j][:, cols(ib)], j == 0 and ib == 1, j == LAST and ib == LAST)
-            for ib in rest:
-                turn(product_sums[:, cols(ib)], product_cols(j, ib, ib + 1), j == 0 and ib == 1, j == LAST and ib == LAST)
-
-        def turn_x_rest(j):
-            for ib in rest:
-                turn(x_ps[ib][:, cols(j)], xT[j][:, cols(ib)])
+        def square_part(ib, part, lo, hi, out=None):
+            nc.scalar.activation(squares[ib][:, cols(lo, hi)] if out is None else out, x_ps[ib][:, cols(lo, hi)], ACT.Square,
+                                 accum_out=parts[:, ib, part : part + 1])
 
         for j in range(LAST):
             gather_b(j)
-            gather_a(j, 0, BLOCKS)
-            product(j, 0, BLOCKS, nc.gpsimd)
-            square(j, 0, BLOCKS)
-            sum_first(j)
-            sum_rest(j)
-            turn_x_rest(j)
+            nc.vector.tensor_tensor(xT[j][:], a_tab[j][:].indirect(tok[:]), b_got[j][:], ALU.add)
+            for lo, hi in ((0, BLOCKS),) if j < LAST - 1 else ((1, BLOCKS), (0, 1)):
+                product(j, lo, hi)
+            for ib in every:
+                turn(x_ps[ib][:, cols(j)], xT[j][:, cols(ib)])
+            for ib in rest:
+                turn(early[:, cols(ib)], products[j][:, cols(ib)], j == 0 and ib == 1, j == LAST - 1 and ib == LAST)
+            turn(first[:, cols(1)], products[j][:, cols(0)], j == 0, False)
+            if j > 0:
+                for ib in rest if j == 1 else (1, 2):
+                    square_part(ib, j - 1, 0 if j == 1 else j, j + 1)
         gather_b(LAST)
 
-        inv0 = sb("inv0", [P, 1])
-        coef0 = sb("coef0", [P, 1])
-        sums = products[LAST][:, SLOTS : SLOTS + BLOCKS]
-        inv = sb("inv", [P, BLOCKS])
-        rstd = sb("rstd", [P, BLOCKS])
-        coef = sb("coef", [P, BLOCKS])
-        terms = sb("terms", [P, SLOTS])
+        order = [LAST, 0, 1, 2]
         y_rest = sb("y_rest", [P, LAST, SLOTS])
-        y = [sb("y0", [P, SLOTS])[:]] + [y_rest[:, j - 1, :] for j in rest]
+        y = [y_rest[:, j, :] for j in range(LAST)] + [sb("y_last", [P, SLOTS])[:]]
         rstd_row = sb("rstd_row", [P, SLOTS])
 
-        def add_turned(out, ib, j):
-            turn(out, h[ib][:, cols(j)], True, False)
-            turn(out, shift[ib][:, cols(j)], False, True)
-
-        def add_turned_group(y_bank, places):
+        def add_turned(y_bank, places):
             for n, (place, ib, j) in enumerate(places):
                 turn(y_bank[:, cols(place)], h[ib][:, cols(j)], n == 0, False)
             for n, (place, ib, j) in enumerate(places):
                 turn(y_bank[:, cols(place)], shift[ib][:, cols(j)], False, n == len(places) - 1)
 
-        def spread_rstd(first, end, tag):
+        def spread_rstd(lo, hi, tag):
             row_ps = bank("row_ps", tag)
-            for ib in range(first, end):
-                turn(row_ps[:, cols(ib)], rstd[:, ib : ib + 1].to_broadcast([P, P]))
-            nc.scalar.copy(rstd_row[:, cols(first, end)], row_ps[:, cols(first, end)])
+            for ib in range(lo, hi):
+                turn(row_ps[:, cols(ib)], (inv[:, ib : ib + 1] if ib else inv0).to_broadcast([P, P]))
+            nc.scalar.activation(rstd_row[:, cols(lo, hi)], row_ps[:, cols(lo, hi)], ACT.Sqrt, scale=float(D))
 
-        def make_shift(ib, first, end, factor):
-            nc.scalar.activation(shift[ib][:, cols(first, end)], x_ps[ib][:, cols(first, end)], ACT.Copy, scale=factor)
+        def make_shift(ib, lo, hi):
+            nc.scalar.activation(shift[ib][:, cols(lo, hi)], x_ps[ib][:, cols(lo, hi)], ACT.Copy, scale=coef[:, ib : ib + 1])
 
-        def scatter(window, offsets, j, first, end, values=None):
-            span = cols(first, end)
-            nc.vector.tensor_tensor(window[:].indirect(offsets[:, entries(first, end)]), y[j][:, span] if values is None else values,
+        def scatter(window, offsets, j, lo, hi, values=None):
+            span = cols(lo, hi)
+            nc.vector.tensor_tensor(window[:].indirect(offsets[:, entries(lo, hi)]), y[j][:, span] if values is None else values,
                                     rstd_row[:, span], ALU.mult)
 
-        gather_a(LAST, 0, 1)
-        gather_a(LAST, 1, 2)
-        product(LAST, 0, 1, nc.vector)
-        square(LAST, 0, 1)
-        sum_first(LAST)
-        square(LAST, 1, 2)
-        gather_a(LAST, 2, BLOCKS)
-        square(LAST, 2, BLOCKS)
-        sums0 = products[LAST][:, SLOTS - 1 : SLOTS + 2 : 2]
-        nc.vector.tensor_reduce(sums0, first_sums[:, cols(0, 2)].rearrange("p (k c) -> p k c", c=P), AXIS.X, ALU.add)
-        nc.vector.reciprocal(inv0[:], sums0[:, 0:1])
-        product(LAST, 1, 2, nc.vector)
-        nc.vector.tensor_scalar(shift[0][:, cols(0)], x_ps[0][:, cols(0)], sums0[:, 1:2], inv0[:], ALU.mult, ALU.mult)
-        product(LAST, 2, BLOCKS, nc.vector)
-        nc.scalar.activation(rstd[:, 0:1], inv0[:], ACT.Sqrt, scale=float(D))
-        nc.scalar.activation(coef0[:], sums0[:, 1:2], ACT.Copy, scale=inv0[:])
-        make_shift(0, 1, 2, coef0[:])
-        spread_rstd(0, 1, "spare")
-        y_first = bank("y_first", "sums0")
-        add_turned(y_first[:, cols(0)], 0, 0)
-        nc.scalar.copy(y[0][:, cols(0)], y_first[:, cols(0)])
-        sum_rest(LAST)
-        nc.vector.tensor_reduce(sums[:, 1:BLOCKS], square_sums[:, cols(1, BLOCKS)].rearrange("p (k c) -> p k c", c=P), AXIS.X, ALU.add)
-        nc.vector.reciprocal(inv[:, 1:BLOCKS], sums[:, 1:BLOCKS])
-        make_shift(0, 2, BLOCKS, coef0[:])
-        y_second = bank("y_second", "spare")
-        add_turned(y_second[:, cols(0)], 0, 1)
-        nc.scalar.copy(y[1][:, cols(0)], y_second[:, cols(0)])
-        y_next = bank("y_next", "sums1")
-        add_turned_group(y_next, [(j, 0, j) for j in range(2, BLOCKS)])
+        def late_x(ib):
+            turn(x_ps[ib][:, cols(LAST)], a_late[:, cols(ib - 1)], True, False)
+            turn(x_ps[ib][:, cols(LAST)], b_got[LAST][:, cols(ib)], False, True)
 
-        def first_shift(ib):
-            nc.scalar.activation(terms[:, cols(ib)], product_sums[:, cols(ib)], ACT.Copy, scale=inv[:, ib : ib + 1],
+        def late_dot(ib):
+            nc.vector.scalar_tensor_tensor(late_terms[:, cols(0)], x_ps[ib][:, cols(LAST)], -1.0, h[ib][:, cols(LAST)],
+                                           ALU.mult, ALU.mult, accum_out=dots[:, ib, 1:2])
+
+        def sum_parts(ib):
+            nc.scalar.activation(small[:, ib, 0:LAST], parts[:, ib, 0:LAST], ACT.Copy, accum_out=s2[:, ib : ib + 1])
+
+        def late_coef(ib):
+            nc.scalar.activation(small[:, ib, 4:6], dots[:, ib, :], ACT.Copy, scale=inv[:, ib : ib + 1],
                                  accum_out=coef[:, ib : ib + 1])
-            make_shift(ib, 0, 1, coef[:, ib : ib + 1])
 
-        nc.scalar.activation(rstd[:, 1:BLOCKS], inv[:, 1:BLOCKS], ACT.Sqrt, scale=float(D))
-        first_shift(1)
-        nc.scalar.copy(y_rest[:, 1:LAST, cols(0)], y_next[:, cols(2, BLOCKS)].rearrange("p (j i) -> p j i", i=P))
-        spread_rstd(1, BLOCKS, "x0")
-        y_ps = bank("y_ps", "sums0")
-        add_turned(y_ps[:, cols(1)], 1, 0)
-        nc.scalar.copy(y[0][:, cols(1)], y_ps[:, cols(1)])
-        for j in every:
-            scatter(win1[j], seg, j, 0, 1)
-        scatter(win0[0], tok, 0, 0, 2)
-        scatter(win1[0], seg, 0, 1, 2)
-        y_ps = bank("y_ps", "spare")
-        for ib in range(2, BLOCKS):
-            first_shift(ib)
-        add_turned_group(y_ps, [(ib, ib, 0) for ib in range(2, BLOCKS)])
-        nc.scalar.copy(y[0][:, cols(2, BLOCKS)], y_ps[:, cols(2, BLOCKS)])
-        turn_x_rest(LAST)
-        scatter(win0[0], tok, 0, 2, BLOCKS)
-        nc.sync.dma_start(block_rows(out_0, 0), win0[0][:])
-        scatter(win1[0], seg, 0, 2, BLOCKS)
-        nc.sync.dma_start(block_rows(out_1, 0), win1[0][:])
+        nc.vector.tensor_tensor(x_first[:], a_tab[LAST][:].indirect(tok[:, entries(0, 1)]), b_got[LAST][:, cols(0)], ALU.add)
+        nc.vector.tensor_copy(a_late[:], a_tab[LAST][:].indirect(tok[:, entries(1, BLOCKS)]))
+        turn(x_ps[0][:, cols(LAST)], x_first[:])
+        turn(first[:, cols(0)], x_first[:], False, True)
+        for ib in rest:
+            nc.scalar.activation(squares[0][:, cols(ib)], early[:, cols(ib)], ACT.Copy, scale=-1.0, accum_out=dots[:, ib, 0:1])
+        nc.scalar.activation(squares[0][:], x_ps[0][:], ACT.Square, accum_out=squares[1][:, D - 1 : D])
+        nc.vector.scalar_tensor_tensor(first_terms[:], first[:, cols(0, 2)], -1.0, h[0][:, cols(LAST, LAST + 2)],
+                                       ALU.mult, ALU.mult, accum_out=dot0)
+        nc.vector.reciprocal(inv0, squares[1][:, D - 1 : D])
+        for ib in (1, 2):
+            late_x(ib)
+        nc.vector.tensor_scalar(shift[0][:, cols(LAST)], first[:, cols(0)], dot0, inv0, ALU.mult, ALU.mult)
+        nc.scalar.activation(coef[:, 0:1], dot0, ACT.Copy, scale=inv0)
+        square_part(1, 2, LAST, BLOCKS)
+        make_shift(0, 0, 1)
+        spread_rstd(0, 1, "B")
+        y_first = bank("y_first", "C")
+        add_turned(y_first, [(0, 0, LAST)])
+        nc.scalar.copy(y[LAST][:, cols(0)], y_first[:, cols(0)])
+        square_part(LAST, 1, 2, LAST, late_terms[:, cols(1)])
+        late_dot(2)
+        nc.vector.tensor_reduce(shift[0][:, D - 1 : D], parts[:, 1, 0:LAST], AXIS.X, ALU.add)
+        late_dot(1)
+        nc.vector.reciprocal(inv[:, 1:2], shift[0][:, D - 1 : D])
+        make_shift(0, 1, LAST)
+        y_second = bank("y_second", "D")
+        add_turned(y_second, [(0, 0, 0)])
+        nc.scalar.copy(y[0][:, cols(0)], y_second[:, cols(0)])
+        y_next = bank("y_next", "A")
+        add_turned(y_next, [(j, 0, j) for j in range(1, LAST)])
+        nc.scalar.copy(y_rest[:, 1:LAST, cols(0)], y_next[:, cols(1, LAST)].rearrange("p (j i) -> p j i", i=P))
+        late_x(LAST)
+        scatter(win1[0], seg, LAST, 0, 1)
+        late_dot(3)
+        for ib in (2, 3):
+            square_part(ib, 2, LAST, BLOCKS, shift[0][:, cols(2)] if ib == 2 else None)
+            sum_parts(ib)
+        late_coef(1)
+        make_shift(1, LAST, BLOCKS)
+        spread_rstd(1, 2, "x0")
+        y_ps = bank("y_ps", "C")
+        add_turned(y_ps, [(1, 1, LAST)])
+        nc.scalar.copy(y[LAST][:, cols(1)], y_ps[:, cols(1)])
+        scatter(win1[1], seg, 0, 0, 1)
+        nc.vector.reciprocal(inv[:, 2:BLOCKS], s2[:, 2:BLOCKS])
+        scatter(win1[2], seg, 1, 0, 1)
+        scatter(win1[3], seg, 2, 0, 1)
+        scatter(win0[0], tok, LAST, 0, 2)
+        scatter(win1[0], seg, LAST, 1, 2)
+        for ib in (2, 3):
+            late_coef(ib)
+            make_shift(ib, LAST, BLOCKS)
+        spread_rstd(2, BLOCKS, "B")
+        y_ps = bank("y_ps", "D")
+        add_turned(y_ps, [(ib, ib, LAST) for ib in (2, 3)])
+        nc.scalar.copy(y[LAST][:, cols(2, BLOCKS)], y_ps[:, cols(2, BLOCKS)])
+        scatter(win0[0], tok, LAST, 2, BLOCKS)
+        nc.sync.dma_start(block_rows(out_0, LAST), win0[0][:])
+        scatter(win1[0], seg, LAST, 2, BLOCKS)
+        nc.sync.dma_start(block_rows(out_1, LAST), win1[0][:])
 
-        for j in rest:
-            y_ps = bank("y_ps", "sums%d" % (j % LAST))
-            for ib in rest:
-                make_shift(ib, j, j + 1, coef[:, ib : ib + 1])
-            for ib in rest:
-                add_turned(y_ps[:, cols(ib)], ib, j)
+        for ib in rest:
+            make_shift(ib, 0, LAST)
+        for n in rest:
+            j = order[n]
+            y_ps = bank("y_ps", "ACB"[j])
+            add_turned(y_ps, [(ib, ib, j) for ib in rest])
             nc.scalar.copy(y[j][:, cols(1, BLOCKS)], y_ps[:, cols(1, BLOCKS)])
-            scatter(win0[j % 2], tok, j, 0, BLOCKS)
-            nc.sync.dma_start(block_rows(out_0, j), win0[j % 2][:])
-            if j == 1:
-                scatter(win1[j], seg, j, 1, BLOCKS)
-                nc.sync.dma_start(block_rows(out_1, j), win1[j][:])
+            scatter(win0[n % 2], tok, j, 0, BLOCKS)
+            nc.sync.dma_start(block_rows(out_0, j), win0[n % 2][:])
+            if n == 1:
+                scatter(win1[n], seg, j, 1, BLOCKS)
+                nc.sync.dma_start(block_rows(out_1, j), win1[n][:])
         y_tail = sb("y_tail", [P, 2, LAST * P], tag="win1_1")
         nc.scalar.copy(y_tail[:], y_rest[:, 1:LAST, cols(1, BLOCKS)])
-        for j in range(2, BLOCKS):
-            scatter(win1[j], seg, j, 1, BLOCKS, y_tail[:, j - 2, :])
-            nc.sync.dma_start(block_rows(out_1, j), win1[j][:])
+        for n in range(2, BLOCKS):
+            scatter(win1[n], seg, order[n], 1, BLOCKS, y_tail[:, n - 2, :])
+            nc.sync.dma_start(block_rows(out_1, order[n]), win1[n][:])

@@ -92,12 +92,12 @@ def tile_attend_gtwoemb_rms_kernel(tc, aT, bT, W, dz, gam, offs, soffs, out_0, o
             return codes, scales
 
         dz_woven = sb("dz_woven", [P, SLOTS, PACK], BF16)
-        nc.vector.tensor_copy(dz_woven[:].rearrange("p (c i) t -> p c t i", i=RUN),
-                              dz_raw[:].rearrange("p t (c i) -> p c t i", i=RUN))
+        nc.scalar.copy(dz_woven[:].rearrange("p (c i) t -> p c t i", i=RUN),
+                       dz_raw[:].rearrange("p t (c i) -> p c t i", i=RUN))
         dz_codes, dz_scales = quantise("dz", dz_woven, E5M2)
         w_woven = [sb("w_woven%d" % half, [P, HALF, PACK], BF16) for half in range(2)]
-        for half, copy in enumerate((nc.vector.tensor_copy, nc.scalar.copy)):
-            copy(w_woven[half][:].rearrange("p (u m) t -> p m t u", u=2),
+        for half in range(2):
+            nc.scalar.copy(w_woven[half][:].rearrange("p (u m) t -> p m t u", u=2),
                  w_raw[:].rearrange("p t (m j) -> p m t j", j=BLOCKS)[:, :, :, 2 * half : 2 * half + 2])
         w_q = [quantise("w%d" % half, w_woven[half], E4M3) for half in range(2)]
 
@@ -127,7 +127,8 @@ def tile_attend_gtwoemb_rms_kernel(tc, aT, bT, W, dz, gam, offs, soffs, out_0, o
         a_late = sb("a_late", [P, LAST * P])
         squares = [sb("squares%d" % ib, [P, D]) for ib in every]
         first_terms = sb("first_terms", [P, 2 * P])
-        parts = sb("parts", [P, BLOCKS, 4])
+        y_rest = sb("y_rest", [P, LAST, SLOTS])
+        parts = [None, sb("parts1", [P, LAST])[:], sb("parts2", [P, LAST])[:], y_rest[:, 1, 0:LAST]]
         dots = sb("dots", [P, BLOCKS, 2])
         small = sb("small", [P, BLOCKS, 8])
         s2 = sb("s2", [P, BLOCKS])
@@ -146,7 +147,7 @@ def tile_attend_gtwoemb_rms_kernel(tc, aT, bT, W, dz, gam, offs, soffs, out_0, o
 
         def square_part(ib, part, lo, hi, out=None):
             nc.scalar.activation(squares[ib][:, cols(lo, hi)] if out is None else out, x_ps[ib][:, cols(lo, hi)], ACT.Square,
-                                 accum_out=parts[:, ib, part : part + 1])
+                                 accum_out=parts[ib][:, part : part + 1])
 
         for j in range(LAST):
             gather_b(j)
@@ -164,9 +165,8 @@ def tile_attend_gtwoemb_rms_kernel(tc, aT, bT, W, dz, gam, offs, soffs, out_0, o
         gather_b(LAST)
 
         order = [LAST, 0, 1, 2]
-        y_rest = sb("y_rest", [P, LAST, SLOTS])
         y = [y_rest[:, j, :] for j in range(LAST)] + [sb("y_last", [P, SLOTS])[:]]
-        rstd_row = sb("rstd_row", [P, SLOTS])
+        rstd_row = sb("rstd_row", [P, SLOTS + 1])
 
         def add_turned(y_bank, places):
             for n, (place, ib, j) in enumerate(places):
@@ -180,8 +180,9 @@ def tile_attend_gtwoemb_rms_kernel(tc, aT, bT, W, dz, gam, offs, soffs, out_0, o
                 turn(row_ps[:, cols(ib)], (inv[:, ib : ib + 1] if ib else inv0).to_broadcast([P, P]))
             nc.scalar.activation(rstd_row[:, cols(lo, hi)], row_ps[:, cols(lo, hi)], ACT.Sqrt, scale=float(D))
 
-        def make_shift(ib, lo, hi):
-            nc.scalar.activation(shift[ib][:, cols(lo, hi)], x_ps[ib][:, cols(lo, hi)], ACT.Copy, scale=coef[:, ib : ib + 1])
+        def make_shift(ib, lo, hi, factor=None):
+            nc.scalar.activation(shift[ib][:, cols(lo, hi)], x_ps[ib][:, cols(lo, hi)], ACT.Copy,
+                                 scale=coef[:, ib : ib + 1] if factor is None else factor)
 
         def scatter(window, offsets, j, lo, hi, values=None):
             span = cols(lo, hi)
@@ -197,7 +198,7 @@ def tile_attend_gtwoemb_rms_kernel(tc, aT, bT, W, dz, gam, offs, soffs, out_0, o
                                            ALU.mult, ALU.mult, accum_out=dots[:, ib, 1:2])
 
         def sum_parts(ib):
-            nc.scalar.activation(small[:, ib, 0:LAST], parts[:, ib, 0:LAST], ACT.Copy, accum_out=s2[:, ib : ib + 1])
+            nc.scalar.activation(small[:, ib, 0:LAST], parts[ib], ACT.Copy, accum_out=s2[:, ib : ib + 1])
 
         def late_coef(ib):
             nc.scalar.activation(small[:, ib, 4:6], dots[:, ib, :], ACT.Copy, scale=inv[:, ib : ib + 1],
@@ -216,31 +217,31 @@ def tile_attend_gtwoemb_rms_kernel(tc, aT, bT, W, dz, gam, offs, soffs, out_0, o
         for ib in (1, 2):
             late_x(ib)
         nc.vector.tensor_scalar(shift[0][:, cols(LAST)], first[:, cols(0)], dot0, inv0, ALU.mult, ALU.mult)
-        nc.scalar.activation(coef[:, 0:1], dot0, ACT.Copy, scale=inv0)
+        nc.scalar.activation(rstd_row[:, 0 : SLOTS + 1 : SLOTS], dot0.to_broadcast([P, 2]), ACT.Copy, scale=inv0)
         square_part(1, 2, LAST, BLOCKS)
-        make_shift(0, 0, 1)
+        make_shift(0, 0, 1, rstd_row[:, 0:1])
         spread_rstd(0, 1, "B")
         y_first = bank("y_first", "C")
         add_turned(y_first, [(0, 0, LAST)])
         nc.scalar.copy(y[LAST][:, cols(0)], y_first[:, cols(0)])
-        square_part(LAST, 1, 2, LAST, late_terms[:, cols(1)])
+        square_part(LAST, 1, 2, LAST, shift[0][:, cols(LAST)])
         late_dot(2)
-        nc.vector.tensor_reduce(shift[0][:, D - 1 : D], parts[:, 1, 0:LAST], AXIS.X, ALU.add)
+        nc.vector.tensor_reduce(inv0, parts[1], AXIS.X, ALU.add)
         late_dot(1)
-        nc.vector.reciprocal(inv[:, 1:2], shift[0][:, D - 1 : D])
-        make_shift(0, 1, LAST)
+        nc.vector.reciprocal(inv[:, 1:2], inv0)
+        make_shift(0, 1, LAST, rstd_row[:, SLOTS : SLOTS + 1])
         y_second = bank("y_second", "D")
         add_turned(y_second, [(0, 0, 0)])
         nc.scalar.copy(y[0][:, cols(0)], y_second[:, cols(0)])
         y_next = bank("y_next", "A")
         add_turned(y_next, [(j, 0, j) for j in range(1, LAST)])
-        nc.scalar.copy(y_rest[:, 1:LAST, cols(0)], y_next[:, cols(1, LAST)].rearrange("p (j i) -> p j i", i=P))
         late_x(LAST)
         scatter(win1[0], seg, LAST, 0, 1)
-        late_dot(3)
         for ib in (2, 3):
             square_part(ib, 2, LAST, BLOCKS, shift[0][:, cols(2)] if ib == 2 else None)
             sum_parts(ib)
+        nc.scalar.copy(y_rest[:, 1:LAST, cols(0)], y_next[:, cols(1, LAST)].rearrange("p (j i) -> p j i", i=P))
+        late_dot(3)
         late_coef(1)
         make_shift(1, LAST, BLOCKS)
         spread_rstd(1, 2, "x0")

@@ -128,15 +128,17 @@ def tile_attend_gtwoemb_rms_kernel(tc, aT, bT, W, dz, gam, offs, soffs, out_0, o
         squares = [sb("squares%d" % ib, [P, D]) for ib in every]
         first_terms = sb("first_terms", [P, 2 * P])
         y_rest = sb("y_rest", [P, LAST, SLOTS])
-        parts = [None, sb("parts1", [P, LAST])[:], sb("parts2", [P, LAST])[:], y_rest[:, 1, 0:LAST]]
+        parts = [None, sb("parts1", [P, LAST])[:], sb("parts2", [P, LAST])[:], y_rest[:, 2, 0:LAST]]
         dots = sb("dots", [P, BLOCKS, 2])
         small = sb("small", [P, BLOCKS, 8])
         s2 = sb("s2", [P, BLOCKS])
         inv = sb("inv", [P, BLOCKS])
         coef = sb("coef", [P, BLOCKS])
-        late_terms = sb("late_terms", [P, 2 * P])
-        dot0 = late_terms[:, 0:1]
+        late_terms = sb("late_terms", [P, LAST * P + 1])
+        dot0 = sb("dot0", [P, 1])[:]
+        inv0_pair = late_terms[:, P : LAST * P + 1 : 2 * P]
         inv0 = late_terms[:, P : P + 1]
+        inv0_shift = late_terms[:, LAST * P : LAST * P + 1]
         shift = [sb("shift%d" % ib, [P, D]) for ib in every]
 
         def gather_b(j):
@@ -146,21 +148,21 @@ def tile_attend_gtwoemb_rms_kernel(tc, aT, bT, W, dz, gam, offs, soffs, out_0, o
             nc.gpsimd.tensor_tensor(products[j][:, cols(lo, hi)], xT[j][:, cols(lo, hi)], hT[j][:, cols(lo, hi)], ALU.mult)
 
         def square_part(ib, part, lo, hi, out=None):
-            nc.scalar.activation(squares[ib][:, cols(lo, hi)] if out is None else out, x_ps[ib][:, cols(lo, hi)], ACT.Square,
+            nc.scalar.activation(squares[ib][:, cols(lo, hi)] if out is None else out, x_ps[ib][:, cols(lo, hi)] if lo < LAST else x_last[ib], ACT.Square,
                                  accum_out=parts[ib][:, part : part + 1])
 
         for j in range(LAST):
             gather_b(j)
             nc.vector.tensor_tensor(xT[j][:], a_tab[j][:].indirect(tok[:]), b_got[j][:], ALU.add)
-            for lo, hi in ((0, BLOCKS),) if j < LAST - 1 else ((1, BLOCKS), (0, 1)):
+            for lo, hi in ((0, BLOCKS),) if j < LAST - 1 else ((0, 1), (1, BLOCKS)):
                 product(j, lo, hi)
             for ib in every:
                 turn(x_ps[ib][:, cols(j)], xT[j][:, cols(ib)])
+            turn(first[:, cols(1)], products[j][:, cols(0)], j == 0, False)
             for ib in rest:
                 turn(early[:, cols(ib)], products[j][:, cols(ib)], j == 0 and ib == 1, j == LAST - 1 and ib == LAST)
-            turn(first[:, cols(1)], products[j][:, cols(0)], j == 0, False)
             if j > 0:
-                for ib in rest if j == 1 else (1, 2):
+                for ib in rest:
                     square_part(ib, j - 1, 0 if j == 1 else j, j + 1)
         gather_b(LAST)
 
@@ -175,13 +177,13 @@ def tile_attend_gtwoemb_rms_kernel(tc, aT, bT, W, dz, gam, offs, soffs, out_0, o
                 turn(y_bank[:, cols(place)], shift[ib][:, cols(j)], False, n == len(places) - 1)
 
         def spread_rstd(lo, hi, tag):
-            row_ps = bank("row_ps", tag)
+            row_ps = bank("row_ps", tag)[:, cols(lo, hi)] if tag else x_ps[LAST][:, cols(LAST)]
             for ib in range(lo, hi):
-                turn(row_ps[:, cols(ib)], (inv[:, ib : ib + 1] if ib else inv0).to_broadcast([P, P]))
-            nc.scalar.activation(rstd_row[:, cols(lo, hi)], row_ps[:, cols(lo, hi)], ACT.Sqrt, scale=float(D))
+                turn(row_ps[:, cols(ib - lo)], (inv[:, ib : ib + 1] if ib else inv0).to_broadcast([P, P]))
+            nc.scalar.activation(rstd_row[:, cols(lo, hi)], row_ps, ACT.Sqrt, scale=float(D))
 
         def make_shift(ib, lo, hi, factor=None):
-            nc.scalar.activation(shift[ib][:, cols(lo, hi)], x_ps[ib][:, cols(lo, hi)], ACT.Copy,
+            nc.scalar.activation(shift[ib][:, cols(lo, hi)], x_cols(ib, lo, hi), ACT.Copy,
                                  scale=coef[:, ib : ib + 1] if factor is None else factor)
 
         def scatter(window, offsets, j, lo, hi, values=None):
@@ -189,12 +191,20 @@ def tile_attend_gtwoemb_rms_kernel(tc, aT, bT, W, dz, gam, offs, soffs, out_0, o
             nc.vector.tensor_tensor(window[:].indirect(offsets[:, entries(lo, hi)]), y[j][:, span] if values is None else values,
                                     rstd_row[:, span], ALU.mult)
 
+        def early_dot(ib, out):
+            nc.scalar.activation(out, early[:, cols(ib)], ACT.Copy, scale=-1.0, accum_out=dots[:, ib, 0:1])
+
+        x_last = [x_ps[ib][:, cols(LAST)] for ib in every]
+
+        def x_cols(ib, lo, hi):
+            return x_last[ib] if lo == LAST else x_ps[ib][:, cols(lo, hi)]
+
         def late_x(ib):
-            turn(x_ps[ib][:, cols(LAST)], a_late[:, cols(ib - 1)], True, False)
-            turn(x_ps[ib][:, cols(LAST)], b_got[LAST][:, cols(ib)], False, True)
+            turn(x_last[ib], a_late[:, cols(ib - 1)], True, False)
+            turn(x_last[ib], b_got[LAST][:, cols(ib)], False, True)
 
         def late_dot(ib):
-            nc.vector.scalar_tensor_tensor(late_terms[:, cols(0)], x_ps[ib][:, cols(LAST)], -1.0, h[ib][:, cols(LAST)],
+            nc.vector.scalar_tensor_tensor(late_terms[:, cols(ib - 1)], x_last[ib], -1.0, h[ib][:, cols(LAST)],
                                            ALU.mult, ALU.mult, accum_out=dots[:, ib, 1:2])
 
         def sum_parts(ib):
@@ -208,57 +218,59 @@ def tile_attend_gtwoemb_rms_kernel(tc, aT, bT, W, dz, gam, offs, soffs, out_0, o
         nc.vector.tensor_copy(a_late[:], a_tab[LAST][:].indirect(tok[:, entries(1, BLOCKS)]))
         turn(x_ps[0][:, cols(LAST)], x_first[:])
         turn(first[:, cols(0)], x_first[:], False, True)
-        for ib in rest:
-            nc.scalar.activation(squares[0][:, cols(ib)], early[:, cols(ib)], ACT.Copy, scale=-1.0, accum_out=dots[:, ib, 0:1])
         nc.scalar.activation(squares[0][:], x_ps[0][:], ACT.Square, accum_out=squares[1][:, D - 1 : D])
         nc.vector.scalar_tensor_tensor(first_terms[:], first[:, cols(0, 2)], -1.0, h[0][:, cols(LAST, LAST + 2)],
                                        ALU.mult, ALU.mult, accum_out=dot0)
-        nc.vector.reciprocal(inv0, squares[1][:, D - 1 : D])
+        nc.vector.reciprocal(inv0_pair, squares[1][:, D - 1 : D].to_broadcast([P, 2]))
         for ib in (1, 2):
             late_x(ib)
-        nc.vector.tensor_scalar(shift[0][:, cols(LAST)], first[:, cols(0)], dot0, inv0, ALU.mult, ALU.mult)
+        nc.vector.tensor_scalar(shift[0][:, cols(LAST)], first[:, cols(0)], dot0, inv0_shift, ALU.mult, ALU.mult)
         nc.scalar.activation(rstd_row[:, 0 : SLOTS + 1 : SLOTS], dot0.to_broadcast([P, 2]), ACT.Copy, scale=inv0)
         square_part(1, 2, LAST, BLOCKS)
         make_shift(0, 0, 1, rstd_row[:, 0:1])
-        spread_rstd(0, 1, "B")
+        spread_rstd(0, 1, None)
         y_first = bank("y_first", "C")
         add_turned(y_first, [(0, 0, LAST)])
         nc.scalar.copy(y[LAST][:, cols(0)], y_first[:, cols(0)])
-        square_part(LAST, 1, 2, LAST, shift[0][:, cols(LAST)])
+        x_last[LAST] = bank("x_tail", "C")[:, cols(0)]
         late_dot(2)
-        nc.vector.tensor_reduce(inv0, parts[1], AXIS.X, ALU.add)
+        nc.vector.tensor_reduce(s2[:, 1:2], parts[1], AXIS.X, ALU.add)
         late_dot(1)
-        nc.vector.reciprocal(inv[:, 1:2], inv0)
+        nc.vector.reciprocal(inv[:, 1:2], s2[:, 1:2])
         make_shift(0, 1, LAST, rstd_row[:, SLOTS : SLOTS + 1])
         y_second = bank("y_second", "D")
         add_turned(y_second, [(0, 0, 0)])
         nc.scalar.copy(y[0][:, cols(0)], y_second[:, cols(0)])
         y_next = bank("y_next", "A")
         add_turned(y_next, [(j, 0, j) for j in range(1, LAST)])
+        nc.scalar.copy(y[1][:, cols(0)], y_next[:, cols(1)])
         late_x(LAST)
         scatter(win1[0], seg, LAST, 0, 1)
         for ib in (2, 3):
             square_part(ib, 2, LAST, BLOCKS, shift[0][:, cols(2)] if ib == 2 else None)
             sum_parts(ib)
-        nc.scalar.copy(y_rest[:, 1:LAST, cols(0)], y_next[:, cols(1, LAST)].rearrange("p (j i) -> p j i", i=P))
+        nc.scalar.copy(y[2][:, cols(0)], y_next[:, cols(2)])
         late_dot(3)
+        early_dot(1, shift[0][:, cols(0)])
         late_coef(1)
         make_shift(1, LAST, BLOCKS)
         spread_rstd(1, 2, "x0")
-        y_ps = bank("y_ps", "C")
+        y_ps = bank("y_ps", "D")
         add_turned(y_ps, [(1, 1, LAST)])
         nc.scalar.copy(y[LAST][:, cols(1)], y_ps[:, cols(1)])
         scatter(win1[1], seg, 0, 0, 1)
-        nc.vector.reciprocal(inv[:, 2:BLOCKS], s2[:, 2:BLOCKS])
         scatter(win1[2], seg, 1, 0, 1)
+        nc.vector.reciprocal(inv[:, 2:BLOCKS], s2[:, 2:BLOCKS])
         scatter(win1[3], seg, 2, 0, 1)
         scatter(win0[0], tok, LAST, 0, 2)
         scatter(win1[0], seg, LAST, 1, 2)
+        early_dot(2, shift[0][:, cols(1)])
+        early_dot(3, a_late[:, cols(2)])
         for ib in (2, 3):
             late_coef(ib)
             make_shift(ib, LAST, BLOCKS)
         spread_rstd(2, BLOCKS, "B")
-        y_ps = bank("y_ps", "D")
+        y_ps = bank("y_ps", "x0")
         add_turned(y_ps, [(ib, ib, LAST) for ib in (2, 3)])
         nc.scalar.copy(y[LAST][:, cols(2, BLOCKS)], y_ps[:, cols(2, BLOCKS)])
         scatter(win0[0], tok, LAST, 2, BLOCKS)

@@ -154,13 +154,12 @@ def tile_attend_gtwoemb_rms_kernel(tc, aT, bT, W, dz, gam, offs, soffs, out_0, o
         for j in range(LAST):
             gather_b(j)
             nc.vector.tensor_tensor(xT[j][:], a_tab[j][:].indirect(tok[:]), b_got[j][:], ALU.add)
-            for lo, hi in ((0, BLOCKS),) if j < LAST - 1 else ((0, 1), (1, BLOCKS)):
-                product(j, lo, hi)
+            product(j, 0, BLOCKS if j < LAST - 1 else LAST)
             for ib in every:
                 turn(x_ps[ib][:, cols(j)], xT[j][:, cols(ib)])
             turn(first[:, cols(1)], products[j][:, cols(0)], j == 0, False)
-            for ib in rest:
-                turn(early[:, cols(ib)], products[j][:, cols(ib)], j == 0 and ib == 1, j == LAST - 1 and ib == LAST)
+            for ib in rest if j < LAST - 1 else (1, 2):
+                turn(early[:, cols(ib)], products[j][:, cols(ib)], j == 0 and ib == 1, False)
             if j > 0:
                 for ib in rest:
                     square_part(ib, j - 1, 0 if j == 1 else j, j + 1)
@@ -218,6 +217,9 @@ def tile_attend_gtwoemb_rms_kernel(tc, aT, bT, W, dz, gam, offs, soffs, out_0, o
         nc.vector.tensor_copy(a_late[:], a_tab[LAST][:].indirect(tok[:, entries(1, BLOCKS)]))
         turn(x_ps[0][:, cols(LAST)], x_first[:])
         turn(first[:, cols(0)], x_first[:], False, True)
+        product_tail = b_got[LAST][:, cols(0)]
+        nc.gpsimd.tensor_tensor(product_tail, xT[2][:, cols(LAST)], hT[2][:, cols(LAST)], ALU.mult)
+        turn(early[:, cols(LAST)], product_tail, False, True)
         nc.scalar.activation(squares[0][:], x_ps[0][:], ACT.Square, accum_out=squares[1][:, D - 1 : D])
         nc.vector.scalar_tensor_tensor(first_terms[:], first[:, cols(0, 2)], -1.0, h[0][:, cols(LAST, LAST + 2)],
                                        ALU.mult, ALU.mult, accum_out=dot0)

@@ -24,7 +24,6 @@ TOKENS = 2048
 SEGMENTS = 1024
 BLOCKS = 4
 LAST = BLOCKS - 1
-HALF = D // 2
 LIST_ROWS = 16
 RUN = 4
 
@@ -54,8 +53,9 @@ def tile_attend_gtwoemb_rms_kernel(tc, aT, bT, W, dz, gam, offs, soffs, out_0, o
             return psum.tile([P, SLOTS], F32, name=name, tag=tag)
 
         every = range(BLOCKS)
-        rest = range(1, BLOCKS)
 
+        gam_col = sb("gam_col", [P, BLOCKS], tag="dz_woven")
+        nc.sync.dma_start(gam_col[:], gam[0:1, :].rearrange("r (p j) -> (r p) j", j=BLOCKS))
         dz_raw = sb("dz_raw", [P, PACK, SLOTS])
         nc.sync.dma_start(dz_raw[:], dz.rearrange("(p t) i -> p t i", t=PACK))
         w_raw = sb("w_raw", [P, PACK, D])
@@ -64,8 +64,6 @@ def tile_attend_gtwoemb_rms_kernel(tc, aT, bT, W, dz, gam, offs, soffs, out_0, o
         nc.sync.dma_start(tok[:], offs)
         seg = pool.tile([P, SLOTS // LIST_ROWS], U16, name="seg")
         nc.sync.dma_start(seg[:], soffs)
-        gam_col = sb("gam_col", [P, BLOCKS])
-        nc.sync.dma_start(gam_col[:], gam[0:1, :].rearrange("r (p j) -> (r p) j", j=BLOCKS))
         a_tab = [sb("a_tab%d" % j, [P, TOKENS]) for j in every]
         b_tab = [sb("b_tab%d" % j, [P, SEGMENTS]) for j in every]
         for j in every:
@@ -74,226 +72,147 @@ def tile_attend_gtwoemb_rms_kernel(tc, aT, bT, W, dz, gam, offs, soffs, out_0, o
 
         ident = sb("ident", [P, P])
         make_identity(nc, ident[:])
-        h = [sb("h%d" % ib, [P, D + (P if ib == 0 else 0)]) for ib in every]
-        nc.gpsimd.memset(h[0][:, cols(BLOCKS)], 1.0)
         warm = sb("warm", [P, 1])
-        nc.scalar.activation(warm[:], h[0][:, D : D + 1], ACT.Sqrt)
+        nc.scalar.activation(warm[:], gam_col[:, 0:1], ACT.Sqrt, scale=0.0, bias=1.0)
 
-        win1 = [sb("win1_%d" % n, [P, SEGMENTS]) for n in every]
-        win0 = [sb("win0_%d" % half, [P, TOKENS]) for half in range(2)]
-        for window in win1 + win0:
+        win0 = [sb("win0_%d" % j, [P, TOKENS]) for j in every]
+        win1 = [sb("win1_%d" % j, [P, SEGMENTS]) for j in every]
+        for window in win0 + win1:
             nc.vector.memset(window[:].bitcast(U32), 0)
-
-        def quantise(name, woven, fmt):
-            width = woven.shape[1]
-            codes = sb(name + "_codes", [P, width], U32)
-            scales = sb(name + "_scales", [P, width], U8)
-            nc.vector.quantize_mx(out=codes[:].bitcast(fmt), scales=scales[:], in_=woven[:].rearrange("p c t -> p (c t)"))
-            return codes, scales
-
-        dz_woven = sb("dz_woven", [P, SLOTS, PACK], BF16)
-        nc.scalar.copy(dz_woven[:].rearrange("p (c i) t -> p c t i", i=RUN),
-                       dz_raw[:].rearrange("p t (c i) -> p c t i", i=RUN))
-        dz_codes, dz_scales = quantise("dz", dz_woven, E5M2)
-        w_woven = [sb("w_woven%d" % half, [P, HALF, PACK], BF16) for half in range(2)]
-        for half in range(2):
-            nc.scalar.copy(w_woven[half][:].rearrange("p (u m) t -> p m t u", u=2),
-                 w_raw[:].rearrange("p t (m j) -> p m t j", j=BLOCKS)[:, :, :, 2 * half : 2 * half + 2])
-        w_q = [quantise("w%d" % half, w_woven[half], E4M3) for half in range(2)]
 
         def turn(out, src, start=True, stop=True):
             nc.tensor.matmul(out, src, ident[:], start=start, stop=stop, is_transpose=True)
 
-        hT = [sb("hT%d" % j, [P, SLOTS]) for j in every]
+        def quantise(codes, scales, woven, fmt):
+            nc.vector.quantize_mx(out=codes.bitcast(fmt), scales=scales, in_=woven[:].rearrange("p c t -> p (c t)"))
+
+        gam_ps = bank("gam_ps", "y0")
         for j in every:
-            dn_ps = bank("dn_ps", "x%d" % j)
-            codes, scales = w_q[j // 2]
-            nc.tensor.matmul_mx(out=dn_ps[:], lhsT=codes[:, cols(j % 2)].bitcast(E4M3), lhsT_scale=scales[:, cols(j % 2)],
-                                rhs=dz_codes[:].bitcast(E5M2), rhs_scale=dz_scales[:], start=True, stop=True)
-            nc.scalar.activation(hT[j][:], dn_ps[:], ACT.Copy, scale=gam_col[:, j : j + 1])
-        for ib, tag in enumerate("ABCD"):
-            h_ps = bank("h_ps", tag)
-            for j in every:
-                turn(h_ps[:, cols(j)], hT[j][:, cols(ib)])
-            nc.scalar.copy(h[ib][:, 0:D], h_ps[:])
+            turn(gam_ps[:, cols(j)], gam_col[:, j : j + 1].to_broadcast([P, P]))
+        gam_row = sb("gam_row", [P, D])
+        nc.scalar.copy(gam_row[:], gam_ps[:])
+
+        dz_woven = sb("dz_woven", [P, SLOTS, PACK], BF16)
+        nc.scalar.copy(dz_woven[:].rearrange("p (c i) t -> p c t i", i=RUN),
+                       dz_raw[:].rearrange("p t (c i) -> p c t i", i=RUN))
+        dz_codes = sb("dz_codes", [P, SLOTS], U32)
+        dz_scales = sb("dz_scales", [P, SLOTS], U8)
+        quantise(dz_codes[:], dz_scales[:], dz_woven, E5M2)
+        w_codes = sb("w_codes", [P, D], U32)
+        w_scales = sb("w_scales", [P, D], U8)
+        for half, copy in enumerate((nc.vector.tensor_copy, nc.scalar.copy)):
+            w_woven = sb("w_woven%d" % half, [P, 2 * P, PACK], BF16, tag="dz_raw" if half else None)
+            copy(w_woven[:].rearrange("p (u m) t -> p m t u", u=2),
+                 w_raw[:].rearrange("p t (m j) -> p m t j", j=BLOCKS)[:, :, :, 2 * half : 2 * half + 2])
+            span = cols(2 * half, 2 * half + 2)
+            quantise(w_codes[:, span], w_scales[:, span], w_woven, E4M3)
+
+        h = sb("h", [P, BLOCKS, BLOCKS, P])
+        for ib in every:
+            dn_ps = bank("dn_ps", "x%d" % ib)
+            nc.tensor.matmul_mx(out=dn_ps[:], lhsT=dz_codes[:, cols(ib)].bitcast(E5M2), lhsT_scale=dz_scales[:, cols(ib)],
+                                rhs=w_codes[:].bitcast(E4M3), rhs_scale=w_scales[:], start=True, stop=True)
+            nc.vector.tensor_tensor(h[:, :, ib, :], dn_ps[:].rearrange("p (j m) -> p j m", j=BLOCKS),
+                                    gam_row[:].rearrange("p (j m) -> p j m", j=BLOCKS), ALU.mult)
 
         x_ps = [bank("x_ps%d" % ib, "x%d" % ib) for ib in every]
-        first = bank("first", "A")
-        early = bank("early", "B")
-        b_got = [sb("b_got%d" % j, [P, SLOTS]) for j in every]
-        xT = [sb("xT%d" % j, [P, SLOTS]) for j in range(LAST)]
-        products = [sb("products%d" % j, [P, SLOTS]) for j in range(LAST)]
-        x_first = sb("x_first", [P, P])
-        a_late = sb("a_late", [P, LAST * P])
-        squares = [sb("squares%d" % ib, [P, D]) for ib in every]
-        first_terms = sb("first_terms", [P, 2 * P])
-        y_rest = sb("y_rest", [P, LAST, SLOTS])
-        parts = [None, sb("parts1", [P, LAST])[:], sb("parts2", [P, LAST])[:], y_rest[:, 2, 0:LAST]]
-        dots = sb("dots", [P, BLOCKS, 2])
-        small = sb("small", [P, BLOCKS, 8])
-        s2 = sb("s2", [P, BLOCKS])
+        squares = sb("squares", [P, BLOCKS, 2, P])
+        products = sb("products", [P, BLOCKS, 2, P])
+        parts = sb("parts", [P, 2, BLOCKS, LAST])
+
+        def gather(engine, out, table, offsets):
+            if engine == "vector":
+                nc.vector.tensor_copy(out, table[:].indirect(offsets))
+            else:
+                nc.scalar.activation(out, table[:].indirect(offsets), ACT.Copy)
+
+        def sums(part, lo, hi):
+            def x_blocks(ib):
+                return x_ps[ib][:, cols(lo, hi)].rearrange("p (j m) -> p j m", m=P)
+
+            for ib in every:
+                nc.vector.scalar_tensor_tensor(products[:, ib, 0 : hi - lo], x_blocks(ib), -1.0, h[:, lo:hi, ib, :],
+                                               ALU.mult, ALU.mult, accum_out=parts[:, 1, ib, part : part + 1])
+                other = ib ^ 2
+                nc.scalar.activation(squares[:, other, 0 : hi - lo], x_blocks(other), ACT.Square,
+                                     accum_out=parts[:, 0, other, part : part + 1])
+
+        y_ps = [bank("y_ps%d" % j, "y%d" % j) for j in range(LAST)]
+
+        def turn_h(j):
+            for ib in every:
+                turn(y_ps[j][:, cols(ib)], h[:, j, ib, :], ib == 0, False)
+
+        for j in every:
+            b_got = sb("b_got", [P, SLOTS], tag="w_raw")
+            gather("scalar", b_got[:], b_tab[j], seg[:])
+            for ib in every:
+                turn(x_ps[ib][:, cols(j)], b_got[:, cols(ib)], True, False)
+            if j < 2:
+                a_all = sb("a_got%d" % j, [P, SLOTS], tag="gam_row" if j else "dz_raw")
+                pieces = [("vector" if j else "scalar", 0, BLOCKS, a_all[:])]
+            elif j == 2:
+                pieces = [("vector", lo, lo + 2, h[:, 1, 2 - lo : 4 - lo, :].rearrange("p b m -> p (b m)")) for lo in (0, 2)]
+            else:
+                pieces = [("scalar" if n % 2 else "vector", ib, ib + 1, h[:, 2, (LAST, 1, 2, 0)[n], :])
+                          for n, ib in enumerate((0, 2, 1, 3))]
+            for engine, lo, hi, a_got in pieces:
+                gather(engine, a_got, a_tab[j], tok[:, entries(lo, hi)])
+                for ib in range(lo, hi):
+                    turn(x_ps[ib][:, cols(j)], a_got[:, cols(ib - lo)], False, True)
+            if j < LAST:
+                turn_h(j)
+            if j > 0:
+                sums(j - 1, 0 if j == 1 else j, j + 1)
+
+        totals = sb("totals", [P, 2, BLOCKS])
         inv = sb("inv", [P, BLOCKS])
         coef = sb("coef", [P, BLOCKS])
-        late_terms = sb("late_terms", [P, LAST * P + 1])
-        dot0 = sb("dot0", [P, 1])[:]
-        inv0_pair = late_terms[:, P : LAST * P + 1 : 2 * P]
-        inv0 = late_terms[:, P : P + 1]
-        inv0_shift = late_terms[:, LAST * P : LAST * P + 1]
-        shift = [sb("shift%d" % ib, [P, D]) for ib in every]
+        nc.vector.tensor_reduce(totals[:], parts[:], AXIS.X, ALU.add)
+        nc.vector.reciprocal(inv[:], totals[:, 0, :])
+        row_ps = bank("row_ps", "y%d" % LAST)
+        for ib in every:
+            turn(row_ps[:, cols(ib)], inv[:, ib : ib + 1].to_broadcast([P, P]))
+        rstd_row = sb("rstd_row", [P, SLOTS])
+        nc.scalar.activation(rstd_row[:], row_ps[:], ACT.Sqrt, scale=float(D))
+        y_ps.append(bank("y_ps%d" % LAST, "y%d" % LAST))
 
-        def gather_b(j):
-            nc.vector.tensor_copy(b_got[j][:], b_tab[j][:].indirect(seg[:]))
+        shift = [sb("shift%d" % ib, [P, 2 * P]) for ib in every]
+        values = [sb("values%d" % j, [P, SLOTS]) for j in every]
 
-        def product(j, lo, hi):
-            nc.gpsimd.tensor_tensor(products[j][:, cols(lo, hi)], xT[j][:, cols(lo, hi)], hT[j][:, cols(lo, hi)], ALU.mult)
+        def make_shift(engine, out, ib, lo):
+            if engine == "vector":
+                nc.vector.tensor_scalar(out[:], x_ps[ib][:, cols(lo, lo + 2)], totals[:, 1, ib : ib + 1],
+                                        inv[:, ib : ib + 1], ALU.mult, ALU.mult)
+            else:
+                nc.scalar.activation(out[:], x_ps[ib][:, cols(lo, lo + 2)], ACT.Copy, scale=coef[:, ib : ib + 1])
 
-        def square_part(ib, part, lo, hi, out=None):
-            nc.scalar.activation(squares[ib][:, cols(lo, hi)] if out is None else out, x_ps[ib][:, cols(lo, hi)] if lo < LAST else x_last[ib], ACT.Square,
-                                 accum_out=parts[ib][:, part : part + 1])
+        def turn_back(lo, shifts):
+            for j in (lo, lo + 1):
+                for ib in every:
+                    turn(y_ps[j][:, cols(ib)], shifts[ib][:, cols(j - lo)], False, ib == LAST)
+            nc.scalar.copy(values[lo][:], y_ps[lo][:])
+            nc.vector.tensor_tensor(values[lo + 1][:], y_ps[lo + 1][:], rstd_row[:], ALU.mult)
 
-        for j in range(LAST):
-            gather_b(j)
-            nc.vector.tensor_tensor(xT[j][:], a_tab[j][:].indirect(tok[:]), b_got[j][:], ALU.add)
-            product(j, 0, BLOCKS if j < LAST - 1 else LAST)
-            for ib in every:
-                turn(x_ps[ib][:, cols(j)], xT[j][:, cols(ib)])
-            turn(first[:, cols(1)], products[j][:, cols(0)], j == 0, False)
-            for ib in rest if j < LAST - 1 else (1, 2):
-                turn(early[:, cols(ib)], products[j][:, cols(ib)], j == 0 and ib == 1, False)
-            if j > 0:
-                for ib in rest:
-                    square_part(ib, j - 1, 0 if j == 1 else j, j + 1)
-        gather_b(LAST)
+        def put(windows, offsets, out, lo):
+            nc.vector.tensor_tensor(windows[lo][:].indirect(offsets[:]), values[lo][:], rstd_row[:], ALU.mult)
+            nc.sync.dma_start(block_rows(out, lo), windows[lo][:])
+            for first in (0, 2):
+                nc.scalar.activation(windows[lo + 1][:].indirect(offsets[:, entries(first, first + 2)]),
+                                     values[lo + 1][:, cols(first, first + 2)], ACT.Copy)
+            nc.sync.dma_start(block_rows(out, lo + 1), windows[lo + 1][:])
 
-        order = [LAST, 0, 1, 2]
-        y = [y_rest[:, j, :] for j in range(LAST)] + [sb("y_last", [P, SLOTS])[:]]
-        rstd_row = sb("rstd_row", [P, SLOTS + 1])
-
-        def add_turned(y_bank, places):
-            for n, (place, ib, j) in enumerate(places):
-                turn(y_bank[:, cols(place)], h[ib][:, cols(j)], n == 0, False)
-            for n, (place, ib, j) in enumerate(places):
-                turn(y_bank[:, cols(place)], shift[ib][:, cols(j)], False, n == len(places) - 1)
-
-        def spread_rstd(lo, hi, tag):
-            row_ps = bank("row_ps", tag)[:, cols(lo, hi)] if tag else x_ps[LAST][:, cols(LAST)]
-            for ib in range(lo, hi):
-                turn(row_ps[:, cols(ib - lo)], (inv[:, ib : ib + 1] if ib else inv0).to_broadcast([P, P]))
-            nc.scalar.activation(rstd_row[:, cols(lo, hi)], row_ps, ACT.Sqrt, scale=float(D))
-
-        def make_shift(ib, lo, hi, factor=None):
-            nc.scalar.activation(shift[ib][:, cols(lo, hi)], x_cols(ib, lo, hi), ACT.Copy,
-                                 scale=coef[:, ib : ib + 1] if factor is None else factor)
-
-        def scatter(window, offsets, j, lo, hi, values=None):
-            span = cols(lo, hi)
-            nc.vector.tensor_tensor(window[:].indirect(offsets[:, entries(lo, hi)]), y[j][:, span] if values is None else values,
-                                    rstd_row[:, span], ALU.mult)
-
-        def early_dot(ib, out):
-            nc.scalar.activation(out, early[:, cols(ib)], ACT.Copy, scale=-1.0, accum_out=dots[:, ib, 0:1])
-
-        x_last = [x_ps[ib][:, cols(LAST)] for ib in every]
-
-        def x_cols(ib, lo, hi):
-            return x_last[ib] if lo == LAST else x_ps[ib][:, cols(lo, hi)]
-
-        def late_x(ib):
-            turn(x_last[ib], a_late[:, cols(ib - 1)], True, False)
-            turn(x_last[ib], b_got[LAST][:, cols(ib)], False, True)
-
-        def late_dot(ib):
-            nc.vector.scalar_tensor_tensor(late_terms[:, cols(ib - 1)], x_last[ib], -1.0, h[ib][:, cols(LAST)],
-                                           ALU.mult, ALU.mult, accum_out=dots[:, ib, 1:2])
-
-        def sum_parts(ib):
-            nc.scalar.activation(small[:, ib, 0:LAST], parts[ib], ACT.Copy, accum_out=s2[:, ib : ib + 1])
-
-        def late_coef(ib):
-            nc.scalar.activation(small[:, ib, 4:6], dots[:, ib, :], ACT.Copy, scale=inv[:, ib : ib + 1],
-                                 accum_out=coef[:, ib : ib + 1])
-
-        nc.vector.tensor_tensor(x_first[:], a_tab[LAST][:].indirect(tok[:, entries(0, 1)]), b_got[LAST][:, cols(0)], ALU.add)
-        nc.vector.tensor_copy(a_late[:], a_tab[LAST][:].indirect(tok[:, entries(1, BLOCKS)]))
-        turn(x_ps[0][:, cols(LAST)], x_first[:])
-        turn(first[:, cols(0)], x_first[:], False, True)
-        product_tail = b_got[LAST][:, cols(0)]
-        nc.gpsimd.tensor_tensor(product_tail, xT[2][:, cols(LAST)], hT[2][:, cols(LAST)], ALU.mult)
-        turn(early[:, cols(LAST)], product_tail, False, True)
-        nc.scalar.activation(squares[0][:], x_ps[0][:], ACT.Square, accum_out=squares[1][:, D - 1 : D])
-        nc.vector.scalar_tensor_tensor(first_terms[:], first[:, cols(0, 2)], -1.0, h[0][:, cols(LAST, LAST + 2)],
-                                       ALU.mult, ALU.mult, accum_out=dot0)
-        nc.vector.reciprocal(inv0_pair, squares[1][:, D - 1 : D].to_broadcast([P, 2]))
-        for ib in (1, 2):
-            late_x(ib)
-        nc.vector.tensor_scalar(shift[0][:, cols(LAST)], first[:, cols(0)], dot0, inv0_shift, ALU.mult, ALU.mult)
-        nc.scalar.activation(rstd_row[:, 0 : SLOTS + 1 : SLOTS], dot0.to_broadcast([P, 2]), ACT.Copy, scale=inv0)
-        square_part(1, 2, LAST, BLOCKS)
-        make_shift(0, 0, 1, rstd_row[:, 0:1])
-        spread_rstd(0, 1, None)
-        y_first = bank("y_first", "C")
-        add_turned(y_first, [(0, 0, LAST)])
-        nc.scalar.copy(y[LAST][:, cols(0)], y_first[:, cols(0)])
-        x_last[LAST] = bank("x_tail", "C")[:, cols(0)]
-        late_dot(2)
-        nc.vector.tensor_reduce(s2[:, 1:2], parts[1], AXIS.X, ALU.add)
-        late_dot(1)
-        nc.vector.reciprocal(inv[:, 1:2], s2[:, 1:2])
-        make_shift(0, 1, LAST, rstd_row[:, SLOTS : SLOTS + 1])
-        y_second = bank("y_second", "D")
-        add_turned(y_second, [(0, 0, 0)])
-        nc.scalar.copy(y[0][:, cols(0)], y_second[:, cols(0)])
-        y_next = bank("y_next", "A")
-        add_turned(y_next, [(j, 0, j) for j in range(1, LAST)])
-        nc.scalar.copy(y[1][:, cols(0)], y_next[:, cols(1)])
-        late_x(LAST)
-        scatter(win1[0], seg, LAST, 0, 1)
-        for ib in (2, 3):
-            square_part(ib, 2, LAST, BLOCKS, shift[0][:, cols(2)] if ib == 2 else None)
-            sum_parts(ib)
-        nc.scalar.copy(y[2][:, cols(0)], y_next[:, cols(2)])
-        late_dot(3)
-        early_dot(1, shift[0][:, cols(0)])
-        late_coef(1)
-        make_shift(1, LAST, BLOCKS)
-        spread_rstd(1, 2, "x0")
-        y_ps = bank("y_ps", "D")
-        add_turned(y_ps, [(1, 1, LAST)])
-        nc.scalar.copy(y[LAST][:, cols(1)], y_ps[:, cols(1)])
-        scatter(win1[1], seg, 0, 0, 1)
-        scatter(win1[2], seg, 1, 0, 1)
-        nc.vector.reciprocal(inv[:, 2:BLOCKS], s2[:, 2:BLOCKS])
-        scatter(win1[3], seg, 2, 0, 1)
-        scatter(win0[0], tok, LAST, 0, 2)
-        scatter(win1[0], seg, LAST, 1, 2)
-        early_dot(2, shift[0][:, cols(1)])
-        early_dot(3, a_late[:, cols(2)])
-        for ib in (2, 3):
-            late_coef(ib)
-            make_shift(ib, LAST, BLOCKS)
-        spread_rstd(2, BLOCKS, "B")
-        y_ps = bank("y_ps", "x0")
-        add_turned(y_ps, [(ib, ib, LAST) for ib in (2, 3)])
-        nc.scalar.copy(y[LAST][:, cols(2, BLOCKS)], y_ps[:, cols(2, BLOCKS)])
-        scatter(win0[0], tok, LAST, 2, BLOCKS)
-        nc.sync.dma_start(block_rows(out_0, LAST), win0[0][:])
-        scatter(win1[0], seg, LAST, 2, BLOCKS)
-        nc.sync.dma_start(block_rows(out_1, LAST), win1[0][:])
-
-        for ib in rest:
-            make_shift(ib, 0, LAST)
-        for n in rest:
-            j = order[n]
-            y_ps = bank("y_ps", "ACB"[j])
-            add_turned(y_ps, [(ib, ib, j) for ib in rest])
-            nc.scalar.copy(y[j][:, cols(1, BLOCKS)], y_ps[:, cols(1, BLOCKS)])
-            scatter(win0[n % 2], tok, j, 0, BLOCKS)
-            nc.sync.dma_start(block_rows(out_0, j), win0[n % 2][:])
-            if n == 1:
-                scatter(win1[n], seg, j, 1, BLOCKS)
-                nc.sync.dma_start(block_rows(out_1, j), win1[n][:])
-        y_tail = sb("y_tail", [P, 2, LAST * P], tag="win1_1")
-        nc.scalar.copy(y_tail[:], y_rest[:, 1:LAST, cols(1, BLOCKS)])
-        for n in range(2, BLOCKS):
-            scatter(win1[n], seg, order[n], 1, BLOCKS, y_tail[:, n - 2, :])
-            nc.sync.dma_start(block_rows(out_1, order[n]), win1[n][:])
+        make_shift("vector", shift[0], 0, 0)
+        nc.vector.tensor_tensor(coef[:], totals[:, 1, :], inv[:], ALU.mult)
+        make_shift("vector", shift[1], 1, 0)
+        make_shift("vector", shift[2], 2, 0)
+        make_shift("scalar", shift[3], 3, 0)
+        turn_back(0, shift)
+        put(win0, tok, out_0, 0)
+        turn_h(LAST)
+        for ib in every:
+            make_shift("scalar" if ib else "vector", shift[LAST - ib], ib, 2)
+        turn_back(2, shift[::-1])
+        put(win1, seg, out_1, 0)
+        put(win0, tok, out_0, 2)
+        put(win1, seg, out_1, 2)

@@ -54,7 +54,7 @@ def tile_attend_gtwoemb_rms_kernel(tc, aT, bT, W, dz, gam, offs, soffs, out_0, o
 
         every = range(BLOCKS)
 
-        gam_col = sb("gam_col", [P, BLOCKS], tag="dz_woven")
+        gam_col = sb("gam_col", [P, BLOCKS])
         nc.sync.dma_start(gam_col[:], gam[0:1, :].rearrange("r (p j) -> (r p) j", j=BLOCKS))
         dz_raw = sb("dz_raw", [P, PACK, SLOTS])
         nc.sync.dma_start(dz_raw[:], dz.rearrange("(p t) i -> p t i", t=PACK))
@@ -75,16 +75,15 @@ def tile_attend_gtwoemb_rms_kernel(tc, aT, bT, W, dz, gam, offs, soffs, out_0, o
         warm = sb("warm", [P, 1])
         nc.scalar.activation(warm[:], gam_col[:, 0:1], ACT.Sqrt, scale=0.0, bias=1.0)
 
-        win0 = [sb("win0_%d" % j, [P, TOKENS]) for j in every]
-        win1 = [sb("win1_%d" % j, [P, SEGMENTS]) for j in every]
-        for window in win0 + win1:
+        win0 = [sb("win0_%d" % j, [P, TOKENS]) for j in range(2)]
+        for window in win0:
             nc.vector.memset(window[:].bitcast(U32), 0)
 
         def turn(out, src, start=True, stop=True):
             nc.tensor.matmul(out, src, ident[:], start=start, stop=stop, is_transpose=True)
 
         def quantise(codes, scales, woven, fmt):
-            nc.vector.quantize_mx(out=codes.bitcast(fmt), scales=scales, in_=woven[:].rearrange("p c t -> p (c t)"))
+            nc.vector.quantize_mx(out=codes.bitcast(fmt), scales=scales, in_=woven.rearrange("p c t -> p (c t)"))
 
         gam_ps = bank("gam_ps", "y0")
         for j in every:
@@ -93,16 +92,17 @@ def tile_attend_gtwoemb_rms_kernel(tc, aT, bT, W, dz, gam, offs, soffs, out_0, o
         nc.scalar.copy(gam_row[:], gam_ps[:])
 
         dz_woven = sb("dz_woven", [P, SLOTS, PACK], BF16)
-        nc.scalar.copy(dz_woven[:].rearrange("p (c i) t -> p c t i", i=RUN),
-                       dz_raw[:].rearrange("p t (c i) -> p c t i", i=RUN))
+        nc.vector.tensor_copy(dz_woven[:].rearrange("p (c i) t -> p c t i", i=RUN),
+                              dz_raw[:].rearrange("p t (c i) -> p c t i", i=RUN))
         dz_codes = sb("dz_codes", [P, SLOTS], U32)
         dz_scales = sb("dz_scales", [P, SLOTS], U8)
-        quantise(dz_codes[:], dz_scales[:], dz_woven, E5M2)
+        quantise(dz_codes[:], dz_scales[:], dz_woven[:], E5M2)
         w_codes = sb("w_codes", [P, D], U32)
         w_scales = sb("w_scales", [P, D], U8)
+        w_halves = sb("w_halves", [P, 2, 2 * P, PACK], BF16, tag="dz_raw")
         for half, copy in enumerate((nc.vector.tensor_copy, nc.scalar.copy)):
-            w_woven = sb("w_woven%d" % half, [P, 2 * P, PACK], BF16, tag="dz_raw" if half else None)
-            copy(w_woven[:].rearrange("p (u m) t -> p m t u", u=2),
+            w_woven = w_halves[:, half]
+            copy(w_woven.rearrange("p (u m) t -> p m t u", u=2),
                  w_raw[:].rearrange("p t (m j) -> p m t j", j=BLOCKS)[:, :, :, 2 * half : 2 * half + 2])
             span = cols(2 * half, 2 * half + 2)
             quantise(w_codes[:, span], w_scales[:, span], w_woven, E4M3)
@@ -115,10 +115,15 @@ def tile_attend_gtwoemb_rms_kernel(tc, aT, bT, W, dz, gam, offs, soffs, out_0, o
             nc.vector.tensor_tensor(h[:, :, ib, :], dn_ps[:].rearrange("p (j m) -> p j m", j=BLOCKS),
                                     gam_row[:].rearrange("p (j m) -> p j m", j=BLOCKS), ALU.mult)
 
+        win1 = [sb("win1_%d" % j, [P, SEGMENTS], tag=tag) for j, tag in enumerate(("dz_woven", "dz_codes", "w_scales", "gam_row"))]
+        win0 = win0 + [sb("win0_%d" % j, [P, TOKENS], tag=tag) for j, tag in ((2, "w_codes"), (3, "dz_scales"))]
+        for window in win1[:2] + win0[2:] + win1[2:]:
+            nc.gpsimd.memset(window[:].bitcast(U32), 0)
+
         x_ps = [bank("x_ps%d" % ib, "x%d" % ib) for ib in every]
-        squares = sb("squares", [P, BLOCKS, 2, P])
-        products = sb("products", [P, BLOCKS, 2, P])
-        parts = sb("parts", [P, 2, BLOCKS, LAST])
+        squares = sb("squares", [P, BLOCKS, P])
+        products = sb("products", [P, BLOCKS, P])
+        parts = sb("parts", [P, 2, BLOCKS, BLOCKS])
 
         def gather(engine, out, table, offsets):
             if engine == "vector":
@@ -126,16 +131,17 @@ def tile_attend_gtwoemb_rms_kernel(tc, aT, bT, W, dz, gam, offs, soffs, out_0, o
             else:
                 nc.scalar.activation(out, table[:].indirect(offsets), ACT.Copy)
 
-        def sums(part, lo, hi):
-            def x_blocks(ib):
-                return x_ps[ib][:, cols(lo, hi)].rearrange("p (j m) -> p j m", m=P)
+        def sum_products(j, ib):
+            nc.vector.scalar_tensor_tensor(products[:, ib, :], x_ps[ib][:, cols(j)], -1.0, h[:, j, ib, :], ALU.mult,
+                                           ALU.mult, accum_out=parts[:, 1, ib, j : j + 1])
 
+        def sum_squares(j, ib):
+            nc.scalar.activation(squares[:, ib, :], x_ps[ib][:, cols(j)], ACT.Square, accum_out=parts[:, 0, ib, j : j + 1])
+
+        def sums(j):
             for ib in every:
-                nc.vector.scalar_tensor_tensor(products[:, ib, 0 : hi - lo], x_blocks(ib), -1.0, h[:, lo:hi, ib, :],
-                                               ALU.mult, ALU.mult, accum_out=parts[:, 1, ib, part : part + 1])
-                other = ib ^ 2
-                nc.scalar.activation(squares[:, other, 0 : hi - lo], x_blocks(other), ACT.Square,
-                                     accum_out=parts[:, 0, other, part : part + 1])
+                sum_products(j, ib)
+                sum_squares(j, ib ^ 2)
 
         y_ps = [bank("y_ps%d" % j, "y%d" % j) for j in range(LAST)]
 
@@ -143,27 +149,49 @@ def tile_attend_gtwoemb_rms_kernel(tc, aT, bT, W, dz, gam, offs, soffs, out_0, o
             for ib in every:
                 turn(y_ps[j][:, cols(ib)], h[:, j, ib, :], ib == 0, False)
 
-        for j in every:
-            b_got = sb("b_got", [P, SLOTS], tag="w_raw")
-            gather("scalar", b_got[:], b_tab[j], seg[:])
-            for ib in every:
-                turn(x_ps[ib][:, cols(j)], b_got[:, cols(ib)], True, False)
+        def gather_pieces(table, offsets, pieces):
+            for engine, lo, hi, out in pieces:
+                gather(engine, out, table, offsets[:, entries(lo, hi)])
+
+        def turn_pieces(j, pieces, first):
+            for step in range(max(hi - lo for engine, lo, hi, out in pieces)):
+                for engine, lo, hi, out in pieces:
+                    turn(x_ps[lo + step][:, cols(j)], out[:, cols(step)], first, not first)
+
+        def whole(name, tag):
+            return [("scalar", 0, BLOCKS, sb(name, [P, SLOTS], tag=tag)[:])]
+
+        def halves(room):
+            return [("vector", 0, 2, room[:, cols(2, BLOCKS)]), ("scalar", 2, BLOCKS, room[:, cols(0, 2)])]
+
+        def spent_h(j):
+            return h[:, j].rearrange("p b m -> p (b m)")
+
+        def b_pieces(j):
             if j < 2:
-                a_all = sb("a_got%d" % j, [P, SLOTS], tag="gam_row" if j else "dz_raw")
-                pieces = [("vector" if j else "scalar", 0, BLOCKS, a_all[:])]
-            elif j == 2:
-                pieces = [("vector", lo, lo + 2, h[:, 1, 2 - lo : 4 - lo, :].rearrange("p b m -> p (b m)")) for lo in (0, 2)]
+                return whole("b_got%d" % j, ("w_raw", "a_tab0")[j])
+            return halves(sb("b_got%d" % j, [P, SLOTS], tag="a_tab%d" % (j - 1)))
+
+        b_next = b_pieces(0)
+        gather_pieces(b_tab[0], seg, b_next)
+        for j in every:
+            turn_pieces(j, b_next, True)
+            if j == 0:
+                rounds = [whole("a_got0", "b_tab0")]
+            elif j < LAST:
+                rounds = [halves(spent_h(j - 1))]
             else:
-                pieces = [("scalar" if n % 2 else "vector", ib, ib + 1, h[:, 2, (LAST, 1, 2, 0)[n], :])
-                          for n, ib in enumerate((0, 2, 1, 3))]
-            for engine, lo, hi, a_got in pieces:
-                gather(engine, a_got, a_tab[j], tok[:, entries(lo, hi)])
-                for ib in range(lo, hi):
-                    turn(x_ps[ib][:, cols(j)], a_got[:, cols(ib - lo)], False, True)
+                rounds = [[("vector", ib, ib + 1, h[:, j - 1, LAST - ib, :]), ("scalar", ib + 2, ib + 3, h[:, j - 1, 1 - ib, :])]
+                          for ib in range(2)]
+            for pieces in rounds:
+                gather_pieces(a_tab[j], tok, pieces)
+                turn_pieces(j, pieces, False)
+            if j < LAST:
+                b_next = b_pieces(j + 1)
+                gather_pieces(b_tab[j + 1], seg, b_next)
             if j < LAST:
                 turn_h(j)
-            if j > 0:
-                sums(j - 1, 0 if j == 1 else j, j + 1)
+            sums(j)
 
         totals = sb("totals", [P, 2, BLOCKS])
         inv = sb("inv", [P, BLOCKS])

@@ -115,11 +115,12 @@ def tile_attend_gtwoemb_rms_kernel(tc, aT, bT, W, dz, gam, offs, soffs, out_0, o
             nc.vector.tensor_tensor(h[:, :, ib, :], dn_ps[:].rearrange("p (j m) -> p j m", j=BLOCKS),
                                     gam_row[:].rearrange("p (j m) -> p j m", j=BLOCKS), ALU.mult)
 
-        win1 = [sb("win1_%d" % j, [P, SEGMENTS], tag=tag) for j, tag in enumerate(("dz_woven", "dz_codes", "w_scales", "gam_row"))]
-        win0 = win0 + [sb("win0_%d" % j, [P, TOKENS], tag=tag) for j, tag in ((2, "w_codes"), (3, "dz_scales"))]
-        for window in win1[:2] + win0[2:] + win1[2:]:
+        def zeroed(name, width, tag):
+            window = sb(name, [P, width], tag=tag)
             nc.gpsimd.memset(window[:].bitcast(U32), 0)
+            return window
 
+        win0.append(zeroed("win0_2", TOKENS, "gam_row"))
         x_ps = [bank("x_ps%d" % ib, "x%d" % ib) for ib in every]
         squares = sb("squares", [P, BLOCKS, P])
         products = sb("products", [P, BLOCKS, P])
@@ -139,15 +140,20 @@ def tile_attend_gtwoemb_rms_kernel(tc, aT, bT, W, dz, gam, offs, soffs, out_0, o
             nc.scalar.activation(squares[:, ib, :], x_ps[ib][:, cols(j)], ACT.Square, accum_out=parts[:, 0, ib, j : j + 1])
 
         def sums(j):
-            for ib in every:
+            for ib in (0, 2, 1, 3) if j == LAST else every:
                 sum_products(j, ib)
-                sum_squares(j, ib ^ 2)
+                sum_squares(j, ib ^ (1 if j == LAST else 2))
 
-        y_ps = [bank("y_ps%d" % j, "y%d" % j) for j in range(LAST)]
+        y_ps = [bank("y_ps%d" % n, "y%d" % n) for n in range(LAST)]
+
+        def y_cols(j, first, end):
+            if j < 2:
+                return y_ps[first // 2][:, cols(2 * j + first % 2, 2 * j + first % 2 + end - first)]
+            return y_ps[j][:, cols(first, end)]
 
         def turn_h(j):
             for ib in every:
-                turn(y_ps[j][:, cols(ib)], h[:, j, ib, :], ib == 0, False)
+                turn(y_cols(j, ib, ib + 1), h[:, j, ib, :], ib % 2 == 0 if j == 0 else j > 1 and ib == 0, False)
 
         def gather_pieces(table, offsets, pieces):
             for engine, lo, hi, out in pieces:
@@ -181,8 +187,8 @@ def tile_attend_gtwoemb_rms_kernel(tc, aT, bT, W, dz, gam, offs, soffs, out_0, o
             elif j < LAST:
                 rounds = [halves(spent_h(j - 1))]
             else:
-                rounds = [[("vector", ib, ib + 1, h[:, j - 1, LAST - ib, :]), ("scalar", ib + 2, ib + 3, h[:, j - 1, 1 - ib, :])]
-                          for ib in range(2)]
+                rounds = [[("vector", 2 * n, 2 * n + 1, h[:, j - 1, LAST - n, :]), ("scalar", 2 * n + 1, 2 * n + 2, h[:, j - 1, 1 - n, :])]
+                          for n in range(2)]
             for pieces in rounds:
                 gather_pieces(a_tab[j], tok, pieces)
                 turn_pieces(j, pieces, False)
@@ -196,17 +202,18 @@ def tile_attend_gtwoemb_rms_kernel(tc, aT, bT, W, dz, gam, offs, soffs, out_0, o
         totals = sb("totals", [P, 2, BLOCKS])
         inv = sb("inv", [P, BLOCKS])
         coef = sb("coef", [P, BLOCKS])
-        nc.vector.tensor_reduce(totals[:], parts[:], AXIS.X, ALU.add)
-        nc.vector.reciprocal(inv[:], totals[:, 0, :])
+        for lo in (0, 2):
+            nc.vector.tensor_reduce(totals[:, :, lo : lo + 2], parts[:, :, lo : lo + 2, :], AXIS.X, ALU.add)
+        for lo in (0, 2):
+            nc.vector.reciprocal(inv[:, lo : lo + 2], totals[:, 0, lo : lo + 2])
         row_ps = bank("row_ps", "y%d" % LAST)
-        for ib in every:
-            turn(row_ps[:, cols(ib)], inv[:, ib : ib + 1].to_broadcast([P, P]))
         rstd_row = sb("rstd_row", [P, SLOTS])
-        nc.scalar.activation(rstd_row[:], row_ps[:], ACT.Sqrt, scale=float(D))
-        y_ps.append(bank("y_ps%d" % LAST, "y%d" % LAST))
 
         shift = [sb("shift%d" % ib, [P, 2 * P]) for ib in every]
         values = [sb("values%d" % j, [P, SLOTS]) for j in every]
+
+        def make_coef(ib):
+            nc.scalar.activation(coef[:, ib : ib + 1], totals[:, 1, ib : ib + 1], ACT.Copy, scale=inv[:, ib : ib + 1])
 
         def make_shift(engine, out, ib, lo):
             if engine == "vector":
@@ -215,32 +222,66 @@ def tile_attend_gtwoemb_rms_kernel(tc, aT, bT, W, dz, gam, offs, soffs, out_0, o
             else:
                 nc.scalar.activation(out[:], x_ps[ib][:, cols(lo, lo + 2)], ACT.Copy, scale=coef[:, ib : ib + 1])
 
-        def turn_back(lo, shifts):
-            for j in (lo, lo + 1):
-                for ib in every:
-                    turn(y_ps[j][:, cols(ib)], shifts[ib][:, cols(j - lo)], False, ib == LAST)
-            nc.scalar.copy(values[lo][:], y_ps[lo][:])
-            nc.vector.tensor_tensor(values[lo + 1][:], y_ps[lo + 1][:], rstd_row[:], ALU.mult)
+        def turn_back(lo, shifts, first, end):
+            for ib in range(first, end):
+                for j in (lo, lo + 1):
+                    turn(y_cols(j, ib, ib + 1), shifts[ib][:, cols(j - lo)], False, ib == end - 1 and (lo > 0 or j == 1))
+
+        def copy_plain(j, first, end):
+            nc.scalar.copy(values[j][:, cols(first, end)], y_cols(j, first, end))
+
+        def copy_scaled(j, first, end):
+            span = cols(first, end)
+            nc.vector.tensor_tensor(values[j][:, span], y_cols(j, first, end), rstd_row[:, span], ALU.mult)
+
+        def scatter_scaled(window, offsets, j, first, end):
+            span = cols(first, end)
+            nc.vector.tensor_tensor(window[:].indirect(offsets[:, entries(first, end)]), values[j][:, span],
+                                    rstd_row[:, span], ALU.mult)
+
+        def scatter_plain(window, offsets, j, first, end):
+            nc.scalar.activation(window[:].indirect(offsets[:, entries(first, end)]), values[j][:, cols(first, end)], ACT.Copy)
 
         def put(windows, offsets, out, lo):
-            nc.vector.tensor_tensor(windows[lo][:].indirect(offsets[:]), values[lo][:], rstd_row[:], ALU.mult)
+            scatter_scaled(windows[lo], offsets, lo, 0, BLOCKS)
             nc.sync.dma_start(block_rows(out, lo), windows[lo][:])
             for first in (0, 2):
-                nc.scalar.activation(windows[lo + 1][:].indirect(offsets[:, entries(first, first + 2)]),
-                                     values[lo + 1][:, cols(first, first + 2)], ACT.Copy)
+                scatter_plain(windows[lo + 1], offsets, lo + 1, first, first + 2)
             nc.sync.dma_start(block_rows(out, lo + 1), windows[lo + 1][:])
 
-        make_shift("vector", shift[0], 0, 0)
-        nc.vector.tensor_tensor(coef[:], totals[:, 1, :], inv[:], ALU.mult)
-        make_shift("vector", shift[1], 1, 0)
-        make_shift("vector", shift[2], 2, 0)
-        make_shift("scalar", shift[3], 3, 0)
-        turn_back(0, shift)
-        put(win0, tok, out_0, 0)
-        turn_h(LAST)
+        def spread_rstd(first, end):
+            for ib in range(first, end):
+                turn(row_ps[:, cols(ib)], inv[:, ib : ib + 1].to_broadcast([P, P]))
+            nc.scalar.activation(rstd_row[:, cols(first, end)], row_ps[:, cols(first, end)], ACT.Sqrt, scale=float(D))
+
         for ib in every:
-            make_shift("scalar" if ib else "vector", shift[LAST - ib], ib, 2)
-        turn_back(2, shift[::-1])
-        put(win1, seg, out_1, 0)
+            make_shift("vector", shift[ib], ib, 0)
+        spread_rstd(0, 2)
+        turn_back(0, shift, 0, 2)
+        copy_plain(0, 0, 2)
+        copy_scaled(1, 0, 2)
+        spread_rstd(2, BLOCKS)
+        y_ps.append(bank("y_ps%d" % LAST, "y%d" % LAST))
+        turn_back(0, shift, 2, BLOCKS)
+        copy_plain(0, 2, BLOCKS)
+        scatter_scaled(win0[0], tok, 0, 0, 2)
+        copy_scaled(1, 2, BLOCKS)
+        scatter_scaled(win0[0], tok, 0, 2, BLOCKS)
+        nc.sync.dma_start(block_rows(out_0, 0), win0[0][:])
+        for first in (0, 2):
+            scatter_plain(win0[1], tok, 1, first, first + 2)
+        nc.sync.dma_start(block_rows(out_0, 1), win0[1][:])
+        turn_h(LAST)
+        win0.append(zeroed("win0_3", TOKENS, "h"))
+        for ib in range(1, BLOCKS):
+            make_coef(ib)
+        late_shift = [sb("late_shift%d" % ib, [P, 2 * P], tag="shift%d" % (LAST - ib)) for ib in every]
+        for ib in every:
+            make_shift("scalar" if ib else "vector", late_shift[ib], ib, 2)
+        turn_back(2, late_shift, 0, BLOCKS)
+        copy_plain(2, 0, BLOCKS)
+        copy_scaled(LAST, 0, BLOCKS)
         put(win0, tok, out_0, 2)
+        win1 = {j: zeroed("win1_%d" % j, SEGMENTS, "shift%d" % (LAST - n)) for n, j in enumerate((2, 3, 0, 1))}
         put(win1, seg, out_1, 2)
+        put(win1, seg, out_1, 0)

@@ -73,10 +73,10 @@ def tile_attend_gtwoemb_rms_kernel(tc, aT, bT, W, dz, gam, offs, soffs, out_0, o
         ident = sb("ident", [P, P])
         make_identity(nc, ident[:])
         warm = sb("warm", [P, 1])
-        nc.scalar.activation(warm[:], gam_col[:, 0:1], ACT.Sqrt, scale=0.0, bias=1.0)
+        nc.scalar.activation(warm[:], gam_col[:, 0:1], ACT.Abs_reciprocal_sqrt, scale=0.0, bias=1.0)
 
-        win0 = [sb("win0_%d" % j, [P, TOKENS]) for j in range(2)]
-        for window in win0:
+        win0 = {j: sb("win0_%d" % j, [P, TOKENS]) for j in (LAST, 1)}
+        for window in win0.values():
             nc.vector.memset(window[:].bitcast(U32), 0)
 
         def turn(out, src, start=True, stop=True):
@@ -120,7 +120,7 @@ def tile_attend_gtwoemb_rms_kernel(tc, aT, bT, W, dz, gam, offs, soffs, out_0, o
             nc.gpsimd.memset(window[:].bitcast(U32), 0)
             return window
 
-        win0.append(zeroed("win0_2", TOKENS, "gam_row"))
+        win0[2] = zeroed("win0_2", TOKENS, "gam_row")
         x_ps = [bank("x_ps%d" % ib, "x%d" % ib) for ib in every]
         squares = sb("squares", [P, BLOCKS, P])
         products = sb("products", [P, BLOCKS, P])
@@ -144,16 +144,12 @@ def tile_attend_gtwoemb_rms_kernel(tc, aT, bT, W, dz, gam, offs, soffs, out_0, o
                 sum_products(j, ib)
                 sum_squares(j, ib ^ (1 if j == LAST else 2))
 
-        y_ps = [bank("y_ps%d" % n, "y%d" % n) for n in range(LAST)]
+        y_ps = {j: bank("y_ps%d" % j, "y%d" % j) for j in (1, 2)}
+        y_ps[LAST] = bank("y_early", "y0")
 
-        def y_cols(j, first, end):
-            if j < 2:
-                return y_ps[first // 2][:, cols(2 * j + first % 2, 2 * j + first % 2 + end - first)]
-            return y_ps[j][:, cols(first, end)]
-
-        def turn_h(j):
-            for ib in every:
-                turn(y_cols(j, ib, ib + 1), h[:, j, ib, :], ib % 2 == 0 if j == 0 else j > 1 and ib == 0, False)
+        def turn_h(j, first, end):
+            for ib in range(first, end):
+                turn(y_ps[j][:, cols(ib)], h[:, j, ib, :], ib == first, False)
 
         def gather_pieces(table, offsets, pieces):
             for engine, lo, hi, out in pieces:
@@ -178,12 +174,20 @@ def tile_attend_gtwoemb_rms_kernel(tc, aT, bT, W, dz, gam, offs, soffs, out_0, o
                 return whole("b_got%d" % j, ("w_raw", "a_tab0")[j])
             return halves(sb("b_got%d" % j, [P, SLOTS], tag="a_tab%d" % (j - 1)))
 
+        x_first = sb("x_first", [P, BLOCKS, P])
+        row_ps = bank("row_ps", "y%d" % LAST)
+
+        def spread(ib, column, start=True, stop=True):
+            turn(row_ps[:, cols(ib)], column.to_broadcast([P, P]), start, stop)
+
         b_next = b_pieces(0)
         gather_pieces(b_tab[0], seg, b_next)
         for j in every:
             turn_pieces(j, b_next, True)
             if j == 0:
                 rounds = [whole("a_got0", "b_tab0")]
+            elif j == 1:
+                rounds = [halves(sb("a_got1", [P, SLOTS], tag="b_tab0"))]
             elif j < LAST:
                 rounds = [halves(spent_h(j - 1))]
             else:
@@ -195,93 +199,123 @@ def tile_attend_gtwoemb_rms_kernel(tc, aT, bT, W, dz, gam, offs, soffs, out_0, o
             if j < LAST:
                 b_next = b_pieces(j + 1)
                 gather_pieces(b_tab[j + 1], seg, b_next)
-            if j < LAST:
-                turn_h(j)
+            if j == 0:
+                turn_h(LAST, 0, 2)
+            elif j < LAST:
+                turn_h(j, 0, BLOCKS)
             sums(j)
+            for ib in (1, 0):
+                spread(ib, parts[:, 0, ib, j : j + 1], j == 0 and ib == 1, j == LAST and ib == 0)
+            if j == 1:
+                for ib in every:
+                    nc.scalar.copy(x_first[:, ib, :], x_ps[ib][:, cols(0)])
 
+        win1 = {}
+        win0[0] = zeroed("win0_0", TOKENS, "a_tab%d" % LAST)
         totals = sb("totals", [P, 2, BLOCKS])
         inv = sb("inv", [P, BLOCKS])
-        coef = sb("coef", [P, BLOCKS])
-        for lo in (0, 2):
-            nc.vector.tensor_reduce(totals[:, :, lo : lo + 2], parts[:, :, lo : lo + 2, :], AXIS.X, ALU.add)
-        for lo in (0, 2):
-            nc.vector.reciprocal(inv[:, lo : lo + 2], totals[:, 0, lo : lo + 2])
-        row_ps = bank("row_ps", "y%d" % LAST)
         rstd_row = sb("rstd_row", [P, SLOTS])
-
-        shift = [sb("shift%d" % ib, [P, 2 * P]) for ib in every]
         values = [sb("values%d" % j, [P, SLOTS]) for j in every]
 
-        def make_coef(ib):
-            nc.scalar.activation(coef[:, ib : ib + 1], totals[:, 1, ib : ib + 1], ACT.Copy, scale=inv[:, ib : ib + 1])
+        def statistics(first, end):
+            nc.vector.tensor_reduce(totals[:, :, first:end], parts[:, :, first:end, :], AXIS.X, ALU.add)
+            nc.vector.reciprocal(inv[:, first:end], totals[:, 0, first:end])
 
-        def make_shift(engine, out, ib, lo):
-            if engine == "vector":
-                nc.vector.tensor_scalar(out[:], x_ps[ib][:, cols(lo, lo + 2)], totals[:, 1, ib : ib + 1],
-                                        inv[:, ib : ib + 1], ALU.mult, ALU.mult)
-            else:
-                nc.scalar.activation(out[:], x_ps[ib][:, cols(lo, lo + 2)], ACT.Copy, scale=coef[:, ib : ib + 1])
+        def make_coef(first, end):
+            nc.gpsimd.tensor_tensor(coef[first // 2][:], totals[:, 1, first:end], inv[:, first:end], ALU.mult)
 
-        def turn_back(lo, shifts, first, end):
-            for ib in range(first, end):
-                for j in (lo, lo + 1):
-                    turn(y_cols(j, ib, ib + 1), shifts[ib][:, cols(j - lo)], False, ib == end - 1 and (lo > 0 or j == 1))
+        def shift_on_vector(out, ib, first, end):
+            nc.vector.tensor_scalar(out, x_ps[ib][:, cols(first, end)], totals[:, 1, ib : ib + 1],
+                                    inv[:, ib : ib + 1], ALU.mult, ALU.mult)
 
-        def copy_plain(j, first, end):
-            nc.scalar.copy(values[j][:, cols(first, end)], y_cols(j, first, end))
+        def shift_on_scalar(out, ib, first, end, coef):
+            nc.scalar.activation(out, x_ps[ib][:, cols(first, end)], ACT.Copy, scale=coef)
+
+        def turn_back(j, ib, src, stop):
+            turn(y_ps[j][:, cols(ib)], src, False, stop)
+
+        def copy_plain(j):
+            nc.vector.tensor_copy(values[j][:], y_ps[j][:])
 
         def copy_scaled(j, first, end):
             span = cols(first, end)
-            nc.vector.tensor_tensor(values[j][:, span], y_cols(j, first, end), rstd_row[:, span], ALU.mult)
+            nc.vector.tensor_tensor(values[j][:, span], y_ps[j][:, span], rstd_row[:, span], ALU.mult)
 
-        def scatter_scaled(window, offsets, j, first, end):
-            span = cols(first, end)
-            nc.vector.tensor_tensor(window[:].indirect(offsets[:, entries(first, end)]), values[j][:, span],
-                                    rstd_row[:, span], ALU.mult)
+        def scatter_scaled(window, offsets, j):
+            nc.vector.tensor_tensor(window[:].indirect(offsets[:]), values[j][:], rstd_row[:], ALU.mult)
 
         def scatter_plain(window, offsets, j, first, end):
-            nc.scalar.activation(window[:].indirect(offsets[:, entries(first, end)]), values[j][:, cols(first, end)], ACT.Copy)
+            nc.scalar.activation(window[:].indirect(offsets[:, entries(first, end)]), values[j][:, cols(first, end)],
+                                 ACT.Copy)
 
-        def put(windows, offsets, out, lo):
-            scatter_scaled(windows[lo], offsets, lo, 0, BLOCKS)
-            nc.sync.dma_start(block_rows(out, lo), windows[lo][:])
-            for first in (0, 2):
-                scatter_plain(windows[lo + 1], offsets, lo + 1, first, first + 2)
-            nc.sync.dma_start(block_rows(out, lo + 1), windows[lo + 1][:])
+        def put(windows, offsets, out, j):
+            scatter_scaled(windows[j], offsets, j)
+            nc.sync.dma_start(block_rows(out, j), windows[j][:])
 
-        def spread_rstd(first, end):
+        def make_rstd(first, end):
+            nc.scalar.activation(rstd_row[:, cols(first, end)], row_ps[:, cols(first, end)], ACT.Abs_reciprocal_sqrt,
+                                 scale=1.0 / D)
+
+        def finish_late(first, end, tag):
+            y_ps[0] = bank("y_late%d" % first, tag)
+            turn_h(0, first, end)
             for ib in range(first, end):
-                turn(row_ps[:, cols(ib)], inv[:, ib : ib + 1].to_broadcast([P, P]))
-            nc.scalar.activation(rstd_row[:, cols(first, end)], row_ps[:, cols(first, end)], ACT.Sqrt, scale=float(D))
+                late = sb("late%d" % ib, [P, P])
+                nc.gpsimd.tensor_scalar(late[:], x_first[:, ib, :], coef[ib // 2][:, ib % 2 : ib % 2 + 1], 0.0,
+                                        ALU.mult, ALU.add)
+                turn_back(0, ib, late[:], ib == end - 1)
+            nc.scalar.copy(values[0][:, cols(first, end)], y_ps[0][:, cols(first, end)])
 
+        narrow = [sb("narrow%d" % n, [P, P]) for n in range(LAST)]
+        wide = [sb("wide%d" % ib, [P, LAST * P]) for ib in range(LAST)]
+        coef = [sb("coef%d" % half, [P, 2]) for half in range(2)]
+        make_rstd(0, 2)
+        statistics(0, 2)
+        for ib in range(2):
+            shift_on_vector(narrow[ib][:], ib, LAST, BLOCKS)
+        for ib in range(2):
+            turn_back(LAST, ib, narrow[ib][:], ib == 1)
+        statistics(2, BLOCKS)
+        shift_on_vector(wide[2][:], 2, 1, BLOCKS)
+        shift_on_vector(narrow[2][:], LAST, LAST, BLOCKS)
+        copy_scaled(LAST, 0, 2)
+        make_coef(0, 2)
+        make_coef(2, BLOCKS)
+        for ib in range(2, BLOCKS):
+            spread(ib, totals[:, 0, ib : ib + 1])
+        make_rstd(2, BLOCKS)
+        for ib in range(2):
+            shift_on_scalar(wide[ib][:, cols(0, 2)], ib, 1, LAST, coef[0][:, ib : ib + 1])
+        wide.append(sb("wide%d" % LAST, [P, 2 * P], tag="narrow1"))
+        shift_on_vector(wide[LAST][:], LAST, 1, LAST)
+        scatter_plain(win0[LAST], tok, LAST, 0, 2)
+        finish_late(0, 2, "y%d" % LAST)
+        y_ps[LAST] = bank("y_late", "y0")
+        turn_h(LAST, 2, BLOCKS)
+        turn_back(LAST, 2, wide[2][:, cols(2)], False)
+        turn_back(LAST, LAST, narrow[2][:], True)
+        copy_scaled(LAST, 2, BLOCKS)
         for ib in every:
-            make_shift("vector", shift[ib], ib, 0)
-        spread_rstd(0, 2)
-        turn_back(0, shift, 0, 2)
-        copy_plain(0, 0, 2)
-        copy_scaled(1, 0, 2)
-        spread_rstd(2, BLOCKS)
-        y_ps.append(bank("y_ps%d" % LAST, "y%d" % LAST))
-        turn_back(0, shift, 2, BLOCKS)
-        copy_plain(0, 2, BLOCKS)
-        scatter_scaled(win0[0], tok, 0, 0, 2)
-        copy_scaled(1, 2, BLOCKS)
-        scatter_scaled(win0[0], tok, 0, 2, BLOCKS)
-        nc.sync.dma_start(block_rows(out_0, 0), win0[0][:])
-        for first in (0, 2):
-            scatter_plain(win0[1], tok, 1, first, first + 2)
-        nc.sync.dma_start(block_rows(out_0, 1), win0[1][:])
-        turn_h(LAST)
-        win0.append(zeroed("win0_3", TOKENS, "h"))
-        for ib in range(1, BLOCKS):
-            make_coef(ib)
-        late_shift = [sb("late_shift%d" % ib, [P, 2 * P], tag="shift%d" % (LAST - ib)) for ib in every]
+            turn_back(1, ib, wide[ib][:, cols(0)], ib == LAST)
+        scatter_plain(win0[LAST], tok, LAST, 2, BLOCKS)
+        nc.sync.dma_start(block_rows(out_0, LAST), win0[LAST][:])
         for ib in every:
-            make_shift("scalar" if ib else "vector", late_shift[ib], ib, 2)
-        turn_back(2, late_shift, 0, BLOCKS)
-        copy_plain(2, 0, BLOCKS)
-        copy_scaled(LAST, 0, BLOCKS)
-        put(win0, tok, out_0, 2)
-        win1 = {j: zeroed("win1_%d" % j, SEGMENTS, "shift%d" % (LAST - n)) for n, j in enumerate((2, 3, 0, 1))}
-        put(win1, seg, out_1, 2)
+            turn_back(2, ib, wide[ib][:, cols(1)], ib == LAST)
+        copy_plain(1)
+        copy_scaled(2, 0, BLOCKS)
+        put(win0, tok, out_0, 1)
+        scatter_plain(win0[2], tok, 2, 0, 2)
+        finish_late(2, BLOCKS, "y1")
+        scatter_plain(win0[2], tok, 2, 2, BLOCKS)
+        nc.sync.dma_start(block_rows(out_0, 2), win0[2][:])
+        put(win0, tok, out_0, 0)
+        for j, tag in ((0, "x_first"), (2, "h"), (LAST, "late2"), (1, "late3")):
+            win1[j] = zeroed("win1_%d" % j, SEGMENTS, tag)
+        for j in (2, LAST):
+            scatter_plain(win1[j], seg, j, 0, 2)
+        scatter_plain(win1[2], seg, 2, 2, BLOCKS)
+        nc.sync.dma_start(block_rows(out_1, 2), win1[2][:])
         put(win1, seg, out_1, 0)
+        scatter_plain(win1[LAST], seg, LAST, 2, BLOCKS)
+        nc.sync.dma_start(block_rows(out_1, LAST), win1[LAST][:])
+        put(win1, seg, out_1, 1)

@@ -211,7 +211,6 @@ def tile_attend_gtwoemb_rms_kernel(tc, aT, bT, W, dz, gam, offs, soffs, out_0, o
                     nc.scalar.copy(x_first[:, ib, :], x_ps[ib][:, cols(0)])
 
         win1 = {}
-        win0[0] = zeroed("win0_0", TOKENS, "a_tab%d" % LAST)
         totals = sb("totals", [P, 2, BLOCKS])
         inv = sb("inv", [P, BLOCKS])
         rstd_row = sb("rstd_row", [P, SLOTS])
@@ -308,8 +307,9 @@ def tile_attend_gtwoemb_rms_kernel(tc, aT, bT, W, dz, gam, offs, soffs, out_0, o
         finish_late(2, BLOCKS, "y1")
         scatter_plain(win0[2], tok, 2, 2, BLOCKS)
         nc.sync.dma_start(block_rows(out_0, 2), win0[2][:])
+        win0[0] = zeroed("win0_0", TOKENS, "x_first")
         put(win0, tok, out_0, 0)
-        for j, tag in ((0, "x_first"), (2, "h"), (LAST, "late2"), (1, "late3")):
+        for j, tag in ((2, "coef1"), (0, "h"), (LAST, "late2"), (1, "late3")):
             win1[j] = zeroed("win1_%d" % j, SEGMENTS, tag)
         for j in (2, LAST):
             scatter_plain(win1[j], seg, j, 0, 2)

@@ -56,10 +56,10 @@ def tile_attend_gtwoemb_rms_kernel(tc, aT, bT, W, dz, gam, offs, soffs, out_0, o
 
         gam_col = sb("gam_col", [P, BLOCKS])
         nc.sync.dma_start(gam_col[:], gam[0:1, :].rearrange("r (p j) -> (r p) j", j=BLOCKS))
-        dz_raw = sb("dz_raw", [P, PACK, SLOTS])
-        nc.sync.dma_start(dz_raw[:], dz.rearrange("(p t) i -> p t i", t=PACK))
         w_raw = sb("w_raw", [P, PACK, D])
         nc.sync.dma_start(w_raw[:], W.rearrange("(p t) d -> p t d", t=PACK))
+        dz_raw = sb("dz_raw", [P, PACK, SLOTS])
+        nc.sync.dma_start(dz_raw[:], dz.rearrange("(p t) i -> p t i", t=PACK))
         tok = pool.tile([P, SLOTS // LIST_ROWS], U16, name="tok")
         nc.sync.dma_start(tok[:], offs)
         seg = pool.tile([P, SLOTS // LIST_ROWS], U16, name="seg")
@@ -91,21 +91,23 @@ def tile_attend_gtwoemb_rms_kernel(tc, aT, bT, W, dz, gam, offs, soffs, out_0, o
         gam_row = sb("gam_row", [P, D])
         nc.scalar.copy(gam_row[:], gam_ps[:])
 
-        dz_woven = sb("dz_woven", [P, SLOTS, PACK], BF16)
-        nc.vector.tensor_copy(dz_woven[:].rearrange("p (c i) t -> p c t i", i=RUN),
-                              dz_raw[:].rearrange("p t (c i) -> p c t i", i=RUN))
-        dz_codes = sb("dz_codes", [P, SLOTS], U32)
-        dz_scales = sb("dz_scales", [P, SLOTS], U8)
-        quantise(dz_codes[:], dz_scales[:], dz_woven[:], E5M2)
         w_codes = sb("w_codes", [P, D], U32)
         w_scales = sb("w_scales", [P, D], U8)
-        w_halves = sb("w_halves", [P, 2, 2 * P, PACK], BF16, tag="dz_raw")
         for half, copy in enumerate((nc.vector.tensor_copy, nc.scalar.copy)):
-            w_woven = w_halves[:, half]
-            copy(w_woven.rearrange("p (u m) t -> p m t u", u=2),
+            w_woven = sb("w_woven%d" % half, [P, 2 * P, PACK], BF16, tag="gam_col" if half else None)
+            copy(w_woven[:].rearrange("p (u m) t -> p m t u", u=2),
                  w_raw[:].rearrange("p t (m j) -> p m t j", j=BLOCKS)[:, :, :, 2 * half : 2 * half + 2])
             span = cols(2 * half, 2 * half + 2)
-            quantise(w_codes[:, span], w_scales[:, span], w_woven, E4M3)
+            quantise(w_codes[:, span], w_scales[:, span], w_woven[:], E4M3)
+        dz_woven = sb("dz_woven", [P, SLOTS, PACK], BF16, tag="w_raw")
+        dz_codes = sb("dz_codes", [P, SLOTS], U32)
+        dz_scales = sb("dz_scales", [P, SLOTS], U8)
+        for ib in every:
+            copy = nc.vector.tensor_copy if ib < 2 else nc.scalar.copy
+            copy(dz_woven[:, cols(ib), :].rearrange("p (c i) t -> p c t i", i=RUN),
+                 dz_raw[:, :, cols(ib)].rearrange("p t (c i) -> p c t i", i=RUN))
+        for ib in every:
+            quantise(dz_codes[:, cols(ib)], dz_scales[:, cols(ib)], dz_woven[:, cols(ib), :], E5M2)
 
         h = sb("h", [P, BLOCKS, BLOCKS, P])
         for ib in every:
@@ -120,7 +122,7 @@ def tile_attend_gtwoemb_rms_kernel(tc, aT, bT, W, dz, gam, offs, soffs, out_0, o
             nc.gpsimd.memset(window[:].bitcast(U32), 0)
             return window
 
-        win0[2] = zeroed("win0_2", TOKENS, "gam_row")
+        win0[2] = zeroed("win0_2", TOKENS, "w_raw")
         x_ps = [bank("x_ps%d" % ib, "x%d" % ib) for ib in every]
         squares = sb("squares", [P, BLOCKS, P])
         products = sb("products", [P, BLOCKS, P])
@@ -142,7 +144,7 @@ def tile_attend_gtwoemb_rms_kernel(tc, aT, bT, W, dz, gam, offs, soffs, out_0, o
         def sums(j):
             for ib in (0, 2, 1, 3) if j == LAST else every:
                 sum_products(j, ib)
-                sum_squares(j, ib ^ (1 if j == LAST else 2))
+                sum_squares(j, ib ^ (0, 2, 2, 1)[j])
 
         y_ps = {j: bank("y_ps%d" % j, "y%d" % j) for j in (1, 2)}
         y_ps[LAST] = bank("y_early", "y0")
@@ -164,15 +166,15 @@ def tile_attend_gtwoemb_rms_kernel(tc, aT, bT, W, dz, gam, offs, soffs, out_0, o
             return [("scalar", 0, BLOCKS, sb(name, [P, SLOTS], tag=tag)[:])]
 
         def halves(room):
-            return [("vector", 0, 2, room[:, cols(2, BLOCKS)]), ("scalar", 2, BLOCKS, room[:, cols(0, 2)])]
+            return [("vector", 0, 2, room[:, cols(0, 2)]), ("scalar", 2, BLOCKS, room[:, cols(2, BLOCKS)])]
 
         def spent_h(j):
             return h[:, j].rearrange("p b m -> p (b m)")
 
         def b_pieces(j):
-            if j < 2:
-                return whole("b_got%d" % j, ("w_raw", "a_tab0")[j])
-            return halves(sb("b_got%d" % j, [P, SLOTS], tag="a_tab%d" % (j - 1)))
+            if j == 0:
+                return whole("b_got0", "dz_raw")
+            return halves(sb("b_got%d" % j, [P, SLOTS], tag="gam_row" if j == 1 else "a_tab%d" % (j - 1)))
 
         x_first = sb("x_first", [P, BLOCKS, P])
         row_ps = bank("row_ps", "y%d" % LAST)
@@ -185,13 +187,14 @@ def tile_attend_gtwoemb_rms_kernel(tc, aT, bT, W, dz, gam, offs, soffs, out_0, o
         for j in every:
             turn_pieces(j, b_next, True)
             if j == 0:
-                rounds = [whole("a_got0", "b_tab0")]
+                a_first = sb("a_got0", [P, SLOTS], tag="b_tab0")
+                rounds = [[("scalar", n, n + 2, a_first[:, cols(n, n + 2)])] for n in (0, 2)]
             elif j == 1:
                 rounds = [halves(sb("a_got1", [P, SLOTS], tag="b_tab0"))]
             elif j < LAST:
                 rounds = [halves(spent_h(j - 1))]
             else:
-                rounds = [[("vector", 2 * n, 2 * n + 1, h[:, j - 1, LAST - n, :]), ("scalar", 2 * n + 1, 2 * n + 2, h[:, j - 1, 1 - n, :])]
+                rounds = [[("vector", 2 * n, 2 * n + 1, h[:, j - 1, LAST * n, :]), ("scalar", 2 * n + 1, 2 * n + 2, h[:, j - 1, 1 + n, :])]
                           for n in range(2)]
             for pieces in rounds:
                 gather_pieces(a_tab[j], tok, pieces)
@@ -206,9 +209,10 @@ def tile_attend_gtwoemb_rms_kernel(tc, aT, bT, W, dz, gam, offs, soffs, out_0, o
             sums(j)
             for ib in (1, 0):
                 spread(ib, parts[:, 0, ib, j : j + 1], j == 0 and ib == 1, j == LAST and ib == 0)
-            if j == 1:
-                for ib in every:
-                    nc.scalar.copy(x_first[:, ib, :], x_ps[ib][:, cols(0)])
+            if j < 2:
+                for ib in (2 * j, 2 * j + 1):
+                    copy = nc.scalar.copy if ib == LAST else nc.vector.tensor_copy
+                    copy(x_first[:, ib, :], x_ps[ib][:, cols(0)])
 
         win1 = {}
         totals = sb("totals", [P, 2, BLOCKS])

@@ -269,8 +269,8 @@ def tile_attend_gtwoemb_rms_kernel(tc, aT, bT, W, dz, gam, offs, soffs, out_0, o
                 turn_back(0, ib, late[:], ib == end - 1)
             nc.scalar.copy(values[0][:, cols(first, end)], y_ps[0][:, cols(first, end)])
 
-        narrow = [sb("narrow%d" % n, [P, P]) for n in range(LAST)]
-        wide = [sb("wide%d" % ib, [P, LAST * P]) for ib in range(LAST)]
+        narrow = [sb("narrow%d" % ib, [P, P]) for ib in every]
+        wide = [sb("wide%d" % ib, [P, 2 * P]) for ib in every]
         coef = [sb("coef%d" % half, [P, 2]) for half in range(2)]
         make_rstd(0, 2)
         statistics(0, 2)
@@ -279,45 +279,45 @@ def tile_attend_gtwoemb_rms_kernel(tc, aT, bT, W, dz, gam, offs, soffs, out_0, o
         for ib in range(2):
             turn_back(LAST, ib, narrow[ib][:], ib == 1)
         statistics(2, BLOCKS)
-        shift_on_vector(wide[2][:], 2, 1, BLOCKS)
-        shift_on_vector(narrow[2][:], LAST, LAST, BLOCKS)
+        shift_on_vector(wide[2][:], 2, 1, LAST)
         copy_scaled(LAST, 0, 2)
+        shift_on_vector(wide[LAST][:], LAST, 1, LAST)
         make_coef(0, 2)
         make_coef(2, BLOCKS)
         for ib in range(2, BLOCKS):
             spread(ib, totals[:, 0, ib : ib + 1])
         make_rstd(2, BLOCKS)
         for ib in range(2):
-            shift_on_scalar(wide[ib][:, cols(0, 2)], ib, 1, LAST, coef[0][:, ib : ib + 1])
-        wide.append(sb("wide%d" % LAST, [P, 2 * P], tag="narrow1"))
-        shift_on_vector(wide[LAST][:], LAST, 1, LAST)
+            shift_on_scalar(wide[ib][:], ib, 1, LAST, coef[0][:, ib : ib + 1])
         scatter_plain(win0[LAST], tok, LAST, 0, 2)
-        finish_late(0, 2, "y%d" % LAST)
-        y_ps[LAST] = bank("y_late", "y0")
-        turn_h(LAST, 2, BLOCKS)
-        turn_back(LAST, 2, wide[2][:, cols(2)], False)
-        turn_back(LAST, LAST, narrow[2][:], True)
-        copy_scaled(LAST, 2, BLOCKS)
         for ib in every:
             turn_back(1, ib, wide[ib][:, cols(0)], ib == LAST)
-        scatter_plain(win0[LAST], tok, LAST, 2, BLOCKS)
-        nc.sync.dma_start(block_rows(out_0, LAST), win0[LAST][:])
+        y_ps[LAST] = bank("y_late", "y0")
+        for ib in range(2, BLOCKS):
+            nc.vector.scalar_tensor_tensor(narrow[ib][:], x_ps[ib][:, cols(LAST)], coef[1][:, ib - 2 : ib - 1],
+                                           h[:, LAST, ib, :], ALU.mult, ALU.add)
+            turn(y_ps[LAST][:, cols(ib)], narrow[ib][:])
         for ib in every:
             turn_back(2, ib, wide[ib][:, cols(1)], ib == LAST)
         copy_plain(1)
+        copy_scaled(LAST, 2, BLOCKS)
+        finish_late(0, 2, "y%d" % LAST)
+        scatter_plain(win0[LAST], tok, LAST, 2, BLOCKS)
+        nc.sync.dma_start(block_rows(out_0, LAST), win0[LAST][:])
         copy_scaled(2, 0, BLOCKS)
         put(win0, tok, out_0, 1)
-        scatter_plain(win0[2], tok, 2, 0, 2)
         finish_late(2, BLOCKS, "y1")
+        win1[2] = zeroed("win1_2", SEGMENTS, "x_first")
+        win0[0] = zeroed("win0_0", TOKENS, "coef1")
+        scatter_plain(win0[2], tok, 2, 0, 2)
+        scatter_plain(win1[2], seg, 2, 0, 1)
         scatter_plain(win0[2], tok, 2, 2, BLOCKS)
         nc.sync.dma_start(block_rows(out_0, 2), win0[2][:])
-        win0[0] = zeroed("win0_0", TOKENS, "x_first")
         put(win0, tok, out_0, 0)
-        for j, tag in ((2, "coef1"), (0, "h"), (LAST, "late2"), (1, "late3")):
+        for j, tag in ((LAST, "h"), (0, "late2"), (1, "late3")):
             win1[j] = zeroed("win1_%d" % j, SEGMENTS, tag)
-        for j in (2, LAST):
-            scatter_plain(win1[j], seg, j, 0, 2)
-        scatter_plain(win1[2], seg, 2, 2, BLOCKS)
+        scatter_plain(win1[LAST], seg, LAST, 0, 2)
+        scatter_plain(win1[2], seg, 2, 1, BLOCKS)
         nc.sync.dma_start(block_rows(out_1, 2), win1[2][:])
         put(win1, seg, out_1, 0)
         scatter_plain(win1[LAST], seg, LAST, 2, BLOCKS)

@@ -142,9 +142,9 @@ def tile_attend_gtwoemb_rms_kernel(tc, aT, bT, W, dz, gam, offs, soffs, out_0, o
             nc.scalar.activation(squares[:, ib, :], x_ps[ib][:, cols(j)], ACT.Square, accum_out=parts[:, 0, ib, j : j + 1])
 
         def sums(j):
-            for ib in (0, 2, 1, 3) if j == LAST else every:
+            for ib in (0, 2, 1, 3) if j > 1 else every:
                 sum_products(j, ib)
-                sum_squares(j, ib ^ (0, 2, 2, 1)[j])
+                sum_squares(j, ib ^ (0, 2, 1, 1)[j])
 
         y_ps = {j: bank("y_ps%d" % j, "y%d" % j) for j in (1, 2)}
         y_ps[LAST] = bank("y_early", "y0")
@@ -194,7 +194,7 @@ def tile_attend_gtwoemb_rms_kernel(tc, aT, bT, W, dz, gam, offs, soffs, out_0, o
             elif j < LAST:
                 rounds = [halves(spent_h(j - 1))]
             else:
-                rounds = [[("vector", 2 * n, 2 * n + 1, h[:, j - 1, LAST * n, :]), ("scalar", 2 * n + 1, 2 * n + 2, h[:, j - 1, 1 + n, :])]
+                rounds = [[("vector", 2 * n, 2 * n + 1, h[:, j - 1, 1 + 2 * n, :]), ("scalar", 2 * n + 1, 2 * n + 2, h[:, j - 1, 2 - 2 * n, :])]
                           for n in range(2)]
             for pieces in rounds:
                 gather_pieces(a_tab[j], tok, pieces)
@@ -223,9 +223,6 @@ def tile_attend_gtwoemb_rms_kernel(tc, aT, bT, W, dz, gam, offs, soffs, out_0, o
         def statistics(first, end):
             nc.vector.tensor_reduce(totals[:, :, first:end], parts[:, :, first:end, :], AXIS.X, ALU.add)
             nc.vector.reciprocal(inv[:, first:end], totals[:, 0, first:end])
-
-        def make_coef(first, end):
-            nc.gpsimd.tensor_tensor(coef[first // 2][:], totals[:, 1, first:end], inv[:, first:end], ALU.mult)
 
         def shift_on_vector(out, ib, first, end):
             nc.vector.tensor_scalar(out, x_ps[ib][:, cols(first, end)], totals[:, 1, ib : ib + 1],
@@ -280,10 +277,11 @@ def tile_attend_gtwoemb_rms_kernel(tc, aT, bT, W, dz, gam, offs, soffs, out_0, o
             turn_back(LAST, ib, narrow[ib][:], ib == 1)
         statistics(2, BLOCKS)
         shift_on_vector(wide[2][:], 2, 1, LAST)
+        nc.vector.tensor_tensor(coef[1][:], totals[:, 1, 2:BLOCKS], inv[:, 2:BLOCKS], ALU.mult)
         copy_scaled(LAST, 0, 2)
         shift_on_vector(wide[LAST][:], LAST, 1, LAST)
-        make_coef(0, 2)
-        make_coef(2, BLOCKS)
+        for ib in range(2):
+            nc.scalar.activation(coef[0][:, ib : ib + 1], totals[:, 1, ib : ib + 1], ACT.Copy, scale=inv[:, ib : ib + 1])
         for ib in range(2, BLOCKS):
             spread(ib, totals[:, 0, ib : ib + 1])
         make_rstd(2, BLOCKS)

@@ -146,12 +146,18 @@ def tile_attend_gtwoemb_rms_kernel(tc, aT, bT, W, dz, gam, offs, soffs, out_0, o
                 sum_products(j, ib)
                 sum_squares(j, ib ^ (0, 2, 1, 1)[j])
 
-        y_ps = {j: bank("y_ps%d" % j, "y%d" % j) for j in (1, 2)}
-        y_ps[LAST] = bank("y_early", "y0")
+        y_pair = [bank("y_pair%d" % half, "y%d" % (half + 1)) for half in range(2)]
+        y_ps = {LAST: bank("y_early", "y0")}
+
+        def y_cols(j, first, end):
+            if j in y_ps:
+                return y_ps[j][:, cols(first, end)]
+            lo = 2 * (j - 1) + first % 2
+            return y_pair[first // 2][:, cols(lo, lo + end - first)]
 
         def turn_h(j, first, end):
             for ib in range(first, end):
-                turn(y_ps[j][:, cols(ib)], h[:, j, ib, :], ib == first, False)
+                turn(y_cols(j, ib, ib + 1), h[:, j, ib, :], ib == first if j in y_ps else j == 1 and ib % 2 == 0, False)
 
         def gather_pieces(table, offsets, pieces):
             for engine, lo, hi, out in pieces:
@@ -232,14 +238,14 @@ def tile_attend_gtwoemb_rms_kernel(tc, aT, bT, W, dz, gam, offs, soffs, out_0, o
             nc.scalar.activation(out, x_ps[ib][:, cols(first, end)], ACT.Copy, scale=coef)
 
         def turn_back(j, ib, src, stop):
-            turn(y_ps[j][:, cols(ib)], src, False, stop)
+            turn(y_cols(j, ib, ib + 1), src, False, stop)
 
-        def copy_plain(j):
-            nc.vector.tensor_copy(values[j][:], y_ps[j][:])
+        def copy_plain(j, first, end):
+            nc.vector.tensor_copy(values[j][:, cols(first, end)], y_cols(j, first, end))
 
         def copy_scaled(j, first, end):
             span = cols(first, end)
-            nc.vector.tensor_tensor(values[j][:, span], y_ps[j][:, span], rstd_row[:, span], ALU.mult)
+            nc.vector.tensor_tensor(values[j][:, span], y_cols(j, first, end), rstd_row[:, span], ALU.mult)
 
         def scatter_scaled(window, offsets, j):
             nc.vector.tensor_tensor(window[:].indirect(offsets[:]), values[j][:], rstd_row[:], ALU.mult)
@@ -258,12 +264,18 @@ def tile_attend_gtwoemb_rms_kernel(tc, aT, bT, W, dz, gam, offs, soffs, out_0, o
 
         def finish_late(first, end, tag):
             y_ps[0] = bank("y_late%d" % first, tag)
-            turn_h(0, first, end)
+            if first == 0:
+                turn_h(0, first, end)
             for ib in range(first, end):
                 late = sb("late%d" % ib, [P, P])
                 nc.gpsimd.tensor_scalar(late[:], x_first[:, ib, :], coef[ib // 2][:, ib % 2 : ib % 2 + 1], 0.0,
                                         ALU.mult, ALU.add)
-                turn_back(0, ib, late[:], ib == end - 1)
+                if first == 0:
+                    turn_back(0, ib, late[:], ib == end - 1)
+                else:
+                    whole_y = sb("late_y%d" % ib, [P, P])
+                    nc.gpsimd.tensor_tensor(whole_y[:], late[:], h[:, 0, ib, :], ALU.add)
+                    turn(y_ps[0][:, cols(ib)], whole_y[:])
             nc.scalar.copy(values[0][:, cols(first, end)], y_ps[0][:, cols(first, end)])
 
         narrow = [sb("narrow%d" % ib, [P, P]) for ib in every]
@@ -279,7 +291,6 @@ def tile_attend_gtwoemb_rms_kernel(tc, aT, bT, W, dz, gam, offs, soffs, out_0, o
         shift_on_vector(wide[2][:], 2, 1, LAST)
         nc.vector.tensor_tensor(coef[1][:], totals[:, 1, 2:BLOCKS], inv[:, 2:BLOCKS], ALU.mult)
         copy_scaled(LAST, 0, 2)
-        shift_on_vector(wide[LAST][:], LAST, 1, LAST)
         for ib in range(2):
             nc.scalar.activation(coef[0][:, ib : ib + 1], totals[:, 1, ib : ib + 1], ACT.Copy, scale=inv[:, ib : ib + 1])
         for ib in range(2, BLOCKS):
@@ -287,35 +298,36 @@ def tile_attend_gtwoemb_rms_kernel(tc, aT, bT, W, dz, gam, offs, soffs, out_0, o
         make_rstd(2, BLOCKS)
         for ib in range(2):
             shift_on_scalar(wide[ib][:], ib, 1, LAST, coef[0][:, ib : ib + 1])
-        scatter_plain(win0[LAST], tok, LAST, 0, 2)
-        for ib in every:
-            turn_back(1, ib, wide[ib][:, cols(0)], ib == LAST)
-        y_ps[LAST] = bank("y_late", "y0")
+        y_ps[LAST] = bank("y_late", "x0")
         for ib in range(2, BLOCKS):
             nc.vector.scalar_tensor_tensor(narrow[ib][:], x_ps[ib][:, cols(LAST)], coef[1][:, ib - 2 : ib - 1],
                                            h[:, LAST, ib, :], ALU.mult, ALU.add)
             turn(y_ps[LAST][:, cols(ib)], narrow[ib][:])
-        for ib in every:
-            turn_back(2, ib, wide[ib][:, cols(1)], ib == LAST)
-        copy_plain(1)
+        shift_on_vector(wide[LAST][:], LAST, 1, LAST)
+        scatter_plain(win0[LAST], tok, LAST, 0, 2)
         copy_scaled(LAST, 2, BLOCKS)
-        finish_late(0, 2, "y%d" % LAST)
+        for first in (0, 2):
+            for ib in (first, first + 1):
+                for j in (1, 2):
+                    turn_back(j, ib, wide[ib][:, cols(j - 1)], ib > first and j == 2)
+            copy_plain(1, first, first + 2)
+            copy_scaled(2, first, first + 2)
+        finish_late(0, 2, "x%d" % LAST)
         scatter_plain(win0[LAST], tok, LAST, 2, BLOCKS)
         nc.sync.dma_start(block_rows(out_0, LAST), win0[LAST][:])
-        copy_scaled(2, 0, BLOCKS)
         put(win0, tok, out_0, 1)
-        finish_late(2, BLOCKS, "y1")
+        finish_late(2, BLOCKS, "y0")
         win1[2] = zeroed("win1_2", SEGMENTS, "x_first")
         win0[0] = zeroed("win0_0", TOKENS, "coef1")
-        scatter_plain(win0[2], tok, 2, 0, 2)
-        scatter_plain(win1[2], seg, 2, 0, 1)
         scatter_plain(win0[2], tok, 2, 2, BLOCKS)
+        scatter_plain(win1[2], seg, 2, LAST, BLOCKS)
+        scatter_plain(win0[2], tok, 2, 0, 2)
         nc.sync.dma_start(block_rows(out_0, 2), win0[2][:])
         put(win0, tok, out_0, 0)
-        for j, tag in ((LAST, "h"), (0, "late2"), (1, "late3")):
+        for j, tag in ((LAST, "h"), (0, "late_y2"), (1, "late_y3")):
             win1[j] = zeroed("win1_%d" % j, SEGMENTS, tag)
         scatter_plain(win1[LAST], seg, LAST, 0, 2)
-        scatter_plain(win1[2], seg, 2, 1, BLOCKS)
+        scatter_plain(win1[2], seg, 2, 0, LAST)
         nc.sync.dma_start(block_rows(out_1, 2), win1[2][:])
         put(win1, seg, out_1, 0)
         scatter_plain(win1[LAST], seg, LAST, 2, BLOCKS)

@@ -210,8 +210,8 @@ def tile_attend_gtwoemb_rms_kernel(tc, aT, bT, W, dz, gam, offs, soffs, out_0, o
                 gather_pieces(b_tab[j + 1], seg, b_next)
             if j == 0:
                 turn_h(LAST, 0, 2)
-            elif j < LAST:
-                turn_h(j, 0, BLOCKS)
+                turn_h(1, 0, BLOCKS)
+                turn_h(2, 0, BLOCKS)
             sums(j)
             for ib in (1, 0):
                 spread(ib, parts[:, 0, ib, j : j + 1], j == 0 and ib == 1, j == LAST and ib == 0)

@@ -142,9 +142,9 @@ def tile_attend_gtwoemb_rms_kernel(tc, aT, bT, W, dz, gam, offs, soffs, out_0, o
             nc.scalar.activation(squares[:, ib, :], x_ps[ib][:, cols(j)], ACT.Square, accum_out=parts[:, 0, ib, j : j + 1])
 
         def sums(j):
-            for ib in (0, 2, 1, 3) if j > 1 else every:
+            for ib in (0, 2, 1, 3) if j else every:
                 sum_products(j, ib)
-                sum_squares(j, ib ^ (0, 2, 1, 1)[j])
+                sum_squares(j, ib ^ 1 if j else ib)
 
         y_pair = [bank("y_pair%d" % half, "y%d" % (half + 1)) for half in range(2)]
         y_ps = {LAST: bank("y_early", "y0")}
@@ -164,9 +164,9 @@ def tile_attend_gtwoemb_rms_kernel(tc, aT, bT, W, dz, gam, offs, soffs, out_0, o
                 gather(engine, out, table, offsets[:, entries(lo, hi)])
 
         def turn_pieces(j, pieces, first):
-            for step in range(max(hi - lo for engine, lo, hi, out in pieces)):
-                for engine, lo, hi, out in pieces:
-                    turn(x_ps[lo + step][:, cols(j)], out[:, cols(step)], first, not first)
+            for engine, lo, hi, out in pieces:
+                for ib in range(lo, hi):
+                    turn(x_ps[ib][:, cols(j)], out[:, cols(ib - lo)], first, not first)
 
         def whole(name, tag):
             return [("scalar", 0, BLOCKS, sb(name, [P, SLOTS], tag=tag)[:])]
@@ -217,7 +217,7 @@ def tile_attend_gtwoemb_rms_kernel(tc, aT, bT, W, dz, gam, offs, soffs, out_0, o
                 spread(ib, parts[:, 0, ib, j : j + 1], j == 0 and ib == 1, j == LAST and ib == 0)
             if j < 2:
                 for ib in (2 * j, 2 * j + 1):
-                    copy = nc.scalar.copy if ib == LAST else nc.vector.tensor_copy
+                    copy = nc.scalar.copy if ib == 2 else nc.vector.tensor_copy
                     copy(x_first[:, ib, :], x_ps[ib][:, cols(0)])
 
         win1 = {}

@@ -26,6 +26,7 @@ BLOCKS = 4
 LAST = BLOCKS - 1
 LIST_ROWS = 16
 RUN = 4
+SHARE = 192
 
 
 def cols(first, end=None):
@@ -124,9 +125,10 @@ def tile_attend_gtwoemb_rms_kernel(tc, aT, bT, W, dz, gam, offs, soffs, out_0, o
 
         win0[2] = zeroed("win0_2", TOKENS, "w_raw")
         x_ps = [bank("x_ps%d" % ib, "x%d" % ib) for ib in every]
-        squares = sb("squares", [P, BLOCKS, P])
+        squares = sb("squares", [P, BLOCKS, 2 * P])
         products = sb("products", [P, BLOCKS, P])
         parts = sb("parts", [P, 2, BLOCKS, BLOCKS])
+        nc.gpsimd.memset(parts[:, 0, 2:BLOCKS, 2:LAST], 0.0)
 
         def gather(engine, out, table, offsets):
             if engine == "vector":
@@ -139,12 +141,19 @@ def tile_attend_gtwoemb_rms_kernel(tc, aT, bT, W, dz, gam, offs, soffs, out_0, o
                                            ALU.mult, accum_out=parts[:, 1, ib, j : j + 1])
 
         def sum_squares(j, ib):
-            nc.scalar.activation(squares[:, ib, :], x_ps[ib][:, cols(j)], ACT.Square, accum_out=parts[:, 0, ib, j : j + 1])
+            if ib < 2 or j < 2:
+                nc.scalar.activation(squares[:, ib, cols(0)], x_ps[ib][:, cols(j)], ACT.Square,
+                                     accum_out=parts[:, 0, ib, j : j + 1])
+            elif j == LAST:
+                nc.scalar.activation(squares[:, ib, :], x_ps[ib][:, cols(2, BLOCKS)], ACT.Square,
+                                     accum_out=parts[:, 0, ib, j : j + 1])
 
         def sums(j):
             for ib in (0, 2, 1, 3) if j else every:
                 sum_products(j, ib)
-                sum_squares(j, ib ^ 1 if j else ib)
+                if j == 0 and ib < 2:
+                    nc.vector.tensor_copy(x_first[:, ib, :], x_ps[ib][:, cols(0)])
+                sum_squares(j, ib ^ (1 if j else 2))
 
         y_pair = [bank("y_pair%d" % half, "y%d" % (half + 1)) for half in range(2)]
         y_ps = {LAST: bank("y_early", "y0")}
@@ -205,9 +214,14 @@ def tile_attend_gtwoemb_rms_kernel(tc, aT, bT, W, dz, gam, offs, soffs, out_0, o
             for pieces in rounds:
                 gather_pieces(a_tab[j], tok, pieces)
                 turn_pieces(j, pieces, False)
-            if j < LAST:
+            if j < 2:
                 b_next = b_pieces(j + 1)
                 gather_pieces(b_tab[j + 1], seg, b_next)
+            elif j == 2:
+                b_next = whole("b_got%d" % LAST, "a_tab2")
+                b_last = b_next[0][-1]
+                gather("vector", b_last[:, :SHARE], b_tab[LAST], seg[:, : SHARE // LIST_ROWS])
+                gather("scalar", b_last[:, SHARE:], b_tab[LAST], seg[:, SHARE // LIST_ROWS :])
             if j == 0:
                 turn_h(LAST, 0, 2)
                 turn_h(1, 0, BLOCKS)
@@ -215,10 +229,9 @@ def tile_attend_gtwoemb_rms_kernel(tc, aT, bT, W, dz, gam, offs, soffs, out_0, o
             sums(j)
             for ib in (1, 0):
                 spread(ib, parts[:, 0, ib, j : j + 1], j == 0 and ib == 1, j == LAST and ib == 0)
-            if j < 2:
-                for ib in (2 * j, 2 * j + 1):
-                    copy = nc.scalar.copy if ib == 2 else nc.vector.tensor_copy
-                    copy(x_first[:, ib, :], x_ps[ib][:, cols(0)])
+            if j == 1:
+                nc.scalar.copy(x_first[:, 2, :], x_ps[2][:, cols(0)])
+                nc.vector.tensor_copy(x_first[:, LAST, :], x_ps[LAST][:, cols(0)])
 
         win1 = {}
         totals = sb("totals", [P, 2, BLOCKS])

@@ -192,6 +192,9 @@ def tile_attend_gtwoemb_rms_kernel(tc, aT, bT, W, dz, gam, offs, soffs, out_0, o
             return halves(sb("b_got%d" % j, [P, SLOTS], tag="gam_row" if j == 1 else "a_tab%d" % (j - 1)))
 
         x_first = sb("x_first", [P, BLOCKS, P])
+        early = sb("early", [P, 2, 2])
+        root = sb("root", [P, 2])
+        half_coef = sb("half_coef", [P, 2])
         row_ps = bank("row_ps", "y%d" % LAST)
 
         def spread(ib, column, start=True, stop=True):
@@ -226,7 +229,16 @@ def tile_attend_gtwoemb_rms_kernel(tc, aT, bT, W, dz, gam, offs, soffs, out_0, o
                 turn_h(LAST, 0, 2)
                 turn_h(1, 0, BLOCKS)
                 turn_h(2, 0, BLOCKS)
-            sums(j)
+            if j == LAST:
+                nc.vector.tensor_reduce(early[:], parts[:, :, 0:2, 0:LAST], AXIS.X, ALU.add)
+                for ib in range(2):
+                    sum_squares(j, ib)
+                    sum_products(j, ib)
+                for ib in range(2, BLOCKS):
+                    sum_products(j, ib)
+                    sum_squares(j, ib)
+            else:
+                sums(j)
             for ib in (1, 0):
                 spread(ib, parts[:, 0, ib, j : j + 1], j == 0 and ib == 1, j == LAST and ib == 0)
             if j == 1:
@@ -294,10 +306,15 @@ def tile_attend_gtwoemb_rms_kernel(tc, aT, bT, W, dz, gam, offs, soffs, out_0, o
         narrow = [sb("narrow%d" % ib, [P, P]) for ib in every]
         wide = [sb("wide%d" % ib, [P, 2 * P]) for ib in every]
         coef = [sb("coef%d" % half, [P, 2]) for half in range(2)]
-        make_rstd(0, 2)
-        statistics(0, 2)
         for ib in range(2):
-            shift_on_vector(narrow[ib][:], ib, LAST, BLOCKS)
+            nc.scalar.activation(root[:, ib : ib + 1], parts[:, 0, ib, LAST:BLOCKS], ACT.Abs_reciprocal_sqrt,
+                                 bias=early[:, 0, ib : ib + 1])
+            nc.vector.tensor_scalar(half_coef[:, ib : ib + 1], parts[:, 1, ib, LAST:BLOCKS], early[:, 1, ib : ib + 1],
+                                    root[:, ib : ib + 1], ALU.add, ALU.mult)
+        make_rstd(0, 2)
+        for ib in range(2):
+            nc.vector.tensor_scalar(narrow[ib][:], x_ps[ib][:, cols(LAST)], half_coef[:, ib : ib + 1],
+                                    root[:, ib : ib + 1], ALU.mult, ALU.mult)
         for ib in range(2):
             turn_back(LAST, ib, narrow[ib][:], ib == 1)
         statistics(2, BLOCKS)
@@ -305,7 +322,7 @@ def tile_attend_gtwoemb_rms_kernel(tc, aT, bT, W, dz, gam, offs, soffs, out_0, o
         nc.vector.tensor_tensor(coef[1][:], totals[:, 1, 2:BLOCKS], inv[:, 2:BLOCKS], ALU.mult)
         copy_scaled(LAST, 0, 2)
         for ib in range(2):
-            nc.scalar.activation(coef[0][:, ib : ib + 1], totals[:, 1, ib : ib + 1], ACT.Copy, scale=inv[:, ib : ib + 1])
+            nc.scalar.activation(coef[0][:, ib : ib + 1], half_coef[:, ib : ib + 1], ACT.Copy, scale=root[:, ib : ib + 1])
         for ib in range(2, BLOCKS):
             spread(ib, totals[:, 0, ib : ib + 1])
         make_rstd(2, BLOCKS)
@@ -330,19 +347,21 @@ def tile_attend_gtwoemb_rms_kernel(tc, aT, bT, W, dz, gam, offs, soffs, out_0, o
         nc.sync.dma_start(block_rows(out_0, LAST), win0[LAST][:])
         put(win0, tok, out_0, 1)
         finish_late(2, BLOCKS, "y0")
-        win1[2] = zeroed("win1_2", SEGMENTS, "x_first")
-        win0[0] = zeroed("win0_0", TOKENS, "coef1")
+        win0[0] = zeroed("win0_0", TOKENS, "x_first")
+        win1[0] = zeroed("win1_0", SEGMENTS, "coef1")
+        win1[LAST] = sb("win1_%d" % LAST, [P, SEGMENTS], tag="h")
+        nc.gpsimd.memset(win1[LAST][:, P:].bitcast(U32), 0)
+        win1[2] = zeroed("win1_2", SEGMENTS, "late_y2")
+        nc.gpsimd.memset(win1[LAST][:, :P].bitcast(U32), 0)
+        win1[1] = zeroed("win1_1", SEGMENTS, "late_y3")
         scatter_plain(win0[2], tok, 2, 2, BLOCKS)
-        scatter_plain(win1[2], seg, 2, LAST, BLOCKS)
         scatter_plain(win0[2], tok, 2, 0, 2)
         nc.sync.dma_start(block_rows(out_0, 2), win0[2][:])
         put(win0, tok, out_0, 0)
-        for j, tag in ((LAST, "h"), (0, "late_y2"), (1, "late_y3")):
-            win1[j] = zeroed("win1_%d" % j, SEGMENTS, tag)
-        scatter_plain(win1[LAST], seg, LAST, 0, 2)
-        scatter_plain(win1[2], seg, 2, 0, LAST)
-        nc.sync.dma_start(block_rows(out_1, 2), win1[2][:])
         put(win1, seg, out_1, 0)
-        scatter_plain(win1[LAST], seg, LAST, 2, BLOCKS)
-        nc.sync.dma_start(block_rows(out_1, LAST), win1[LAST][:])
+        for first in (0, 2):
+            for j in (2, LAST):
+                scatter_plain(win1[j], seg, j, first, first + 2)
+                if first:
+                    nc.sync.dma_start(block_rows(out_1, j), win1[j][:])
         put(win1, seg, out_1, 1)

@@ -56,7 +56,7 @@ def tile_attend_gtwoemb_rms_kernel(tc, aT, bT, W, dz, gam, offs, soffs, out_0, o
         every = range(BLOCKS)
 
         gam_col = sb("gam_col", [P, BLOCKS])
-        nc.sync.dma_start(gam_col[:], gam[0:1, :].rearrange("r (p j) -> (r p) j", j=BLOCKS))
+        nc.scalar.dma_start(gam_col[:], gam[0:1, :].rearrange("r (p j) -> (r p) j", j=BLOCKS))
         w_raw = sb("w_raw", [P, PACK, D])
         nc.sync.dma_start(w_raw[:], W.rearrange("(p t) d -> p t d", t=PACK))
         dz_raw = sb("dz_raw", [P, PACK, SLOTS])
@@ -126,9 +126,9 @@ def tile_attend_gtwoemb_rms_kernel(tc, aT, bT, W, dz, gam, offs, soffs, out_0, o
         win0[2] = zeroed("win0_2", TOKENS, "w_raw")
         x_ps = [bank("x_ps%d" % ib, "x%d" % ib) for ib in every]
         squares = sb("squares", [P, BLOCKS, 2 * P])
-        products = sb("products", [P, BLOCKS, P])
+        products = sb("products", [P, BLOCKS, 2, P])
         parts = sb("parts", [P, 2, BLOCKS, BLOCKS])
-        nc.gpsimd.memset(parts[:, 0, 2:BLOCKS, 2:LAST], 0.0)
+        nc.gpsimd.memset(parts[:, :, 2:BLOCKS, :], 0.0)
 
         def gather(engine, out, table, offsets):
             if engine == "vector":
@@ -137,15 +137,20 @@ def tile_attend_gtwoemb_rms_kernel(tc, aT, bT, W, dz, gam, offs, soffs, out_0, o
                 nc.scalar.activation(out, table[:].indirect(offsets), ACT.Copy)
 
         def sum_products(j, ib):
-            nc.vector.scalar_tensor_tensor(products[:, ib, :], x_ps[ib][:, cols(j)], -1.0, h[:, j, ib, :], ALU.mult,
-                                           ALU.mult, accum_out=parts[:, 1, ib, j : j + 1])
+            if ib >= 2 and j == 0:
+                return
+            first = 0 if ib >= 2 and j == 1 else j
+            nc.vector.scalar_tensor_tensor(products[:, ib, : j + 1 - first, :],
+                                           x_ps[ib][:, cols(first, j + 1)].rearrange("p (j m) -> p j m", m=P), -1.0,
+                                           h[:, first : j + 1, ib, :], ALU.mult, ALU.mult,
+                                           accum_out=parts[:, 1, ib, j : j + 1])
 
         def sum_squares(j, ib):
-            if ib < 2 or j < 2:
+            if ib < 2:
                 nc.scalar.activation(squares[:, ib, cols(0)], x_ps[ib][:, cols(j)], ACT.Square,
                                      accum_out=parts[:, 0, ib, j : j + 1])
-            elif j == LAST:
-                nc.scalar.activation(squares[:, ib, :], x_ps[ib][:, cols(2, BLOCKS)], ACT.Square,
+            elif j % 2:
+                nc.scalar.activation(squares[:, ib, :], x_ps[ib][:, cols(j - 1, j + 1)], ACT.Square,
                                      accum_out=parts[:, 0, ib, j : j + 1])
 
         def sums(j):
@@ -153,7 +158,7 @@ def tile_attend_gtwoemb_rms_kernel(tc, aT, bT, W, dz, gam, offs, soffs, out_0, o
                 sum_products(j, ib)
                 if j == 0 and ib < 2:
                     nc.vector.tensor_copy(x_first[:, ib, :], x_ps[ib][:, cols(0)])
-                sum_squares(j, ib ^ (1 if j else 2))
+                sum_squares(j, ib ^ 1 if j else ib)
 
         y_pair = [bank("y_pair%d" % half, "y%d" % (half + 1)) for half in range(2)]
         y_ps = {LAST: bank("y_early", "y0")}
@@ -187,9 +192,9 @@ def tile_attend_gtwoemb_rms_kernel(tc, aT, bT, W, dz, gam, offs, soffs, out_0, o
             return h[:, j].rearrange("p b m -> p (b m)")
 
         def b_pieces(j):
-            if j == 0:
-                return whole("b_got0", "dz_raw")
-            return halves(sb("b_got%d" % j, [P, SLOTS], tag="gam_row" if j == 1 else "a_tab%d" % (j - 1)))
+            if j < 2:
+                return whole("b_got%d" % j, "gam_row" if j else "dz_raw")
+            return halves(sb("b_got%d" % j, [P, SLOTS], tag="a_tab%d" % (j - 1)))
 
         x_first = sb("x_first", [P, BLOCKS, P])
         early = sb("early", [P, 2, 2])

@@ -26,7 +26,7 @@ BLOCKS = 4
 LAST = BLOCKS - 1
 LIST_ROWS = 16
 RUN = 4
-SHARE = 192
+SHARE = 256
 
 
 def cols(first, end=None):
@@ -242,13 +242,19 @@ def tile_attend_gtwoemb_rms_kernel(tc, aT, bT, W, dz, gam, offs, soffs, out_0, o
                 for ib in range(2, BLOCKS):
                     sum_products(j, ib)
                     sum_squares(j, ib)
+            elif j == 2:
+                for ib in (0, 2):
+                    sum_products(j, ib)
+                    sum_squares(j, 1 - ib // 2)
+                for ib in (1, LAST):
+                    sum_products(j, ib)
             else:
                 sums(j)
             for ib in (1, 0):
                 spread(ib, parts[:, 0, ib, j : j + 1], j == 0 and ib == 1, j == LAST and ib == 0)
-            if j == 1:
-                nc.scalar.copy(x_first[:, 2, :], x_ps[2][:, cols(0)])
-                nc.vector.tensor_copy(x_first[:, LAST, :], x_ps[LAST][:, cols(0)])
+            if j == 0:
+                for ib in range(2, BLOCKS):
+                    nc.vector.tensor_copy(x_first[:, ib, :], x_ps[ib][:, cols(0)])
 
         win1 = {}
         totals = sb("totals", [P, 2, BLOCKS])

@@ -146,10 +146,10 @@ def tile_attend_gtwoemb_rms_kernel(tc, aT, bT, W, dz, gam, offs, soffs, out_0, o
                                            accum_out=parts[:, 1, ib, j : j + 1])
 
         def sum_squares(j, ib):
-            if ib < 2:
+            if ib < 2 or j >= 2:
                 nc.scalar.activation(squares[:, ib, cols(0)], x_ps[ib][:, cols(j)], ACT.Square,
                                      accum_out=parts[:, 0, ib, j : j + 1])
-            elif j % 2:
+            elif j:
                 nc.scalar.activation(squares[:, ib, :], x_ps[ib][:, cols(j - 1, j + 1)], ACT.Square,
                                      accum_out=parts[:, 0, ib, j : j + 1])
 
@@ -242,12 +242,6 @@ def tile_attend_gtwoemb_rms_kernel(tc, aT, bT, W, dz, gam, offs, soffs, out_0, o
                 for ib in range(2, BLOCKS):
                     sum_products(j, ib)
                     sum_squares(j, ib)
-            elif j == 2:
-                for ib in (0, 2):
-                    sum_products(j, ib)
-                    sum_squares(j, 1 - ib // 2)
-                for ib in (1, LAST):
-                    sum_products(j, ib)
             else:
                 sums(j)
             for ib in (1, 0):

@@ -294,13 +294,13 @@ def tile_attend_gtwoemb_rms_kernel(tc, aT, bT, W, dz, gam, offs, soffs, out_0, o
 
         def finish_late(first, end, tag):
             y_ps[0] = bank("y_late%d" % first, tag)
-            if first == 0:
+            if first:
                 turn_h(0, first, end)
             for ib in range(first, end):
                 late = sb("late%d" % ib, [P, P])
                 nc.gpsimd.tensor_scalar(late[:], x_first[:, ib, :], coef[ib // 2][:, ib % 2 : ib % 2 + 1], 0.0,
                                         ALU.mult, ALU.add)
-                if first == 0:
+                if first:
                     turn_back(0, ib, late[:], ib == end - 1)
                 else:
                     whole_y = sb("late_y%d" % ib, [P, P])
@@ -347,18 +347,18 @@ def tile_attend_gtwoemb_rms_kernel(tc, aT, bT, W, dz, gam, offs, soffs, out_0, o
                     turn_back(j, ib, wide[ib][:, cols(j - 1)], ib > first and j == 2)
             copy_plain(1, first, first + 2)
             copy_scaled(2, first, first + 2)
-        finish_late(0, 2, "x%d" % LAST)
+        finish_late(0, 2, "y0")
         scatter_plain(win0[LAST], tok, LAST, 2, BLOCKS)
         nc.sync.dma_start(block_rows(out_0, LAST), win0[LAST][:])
         put(win0, tok, out_0, 1)
-        finish_late(2, BLOCKS, "y0")
+        finish_late(2, BLOCKS, "x%d" % LAST)
         win0[0] = zeroed("win0_0", TOKENS, "x_first")
         win1[0] = zeroed("win1_0", SEGMENTS, "coef1")
         win1[LAST] = sb("win1_%d" % LAST, [P, SEGMENTS], tag="h")
         nc.gpsimd.memset(win1[LAST][:, P:].bitcast(U32), 0)
-        win1[2] = zeroed("win1_2", SEGMENTS, "late_y2")
+        win1[2] = zeroed("win1_2", SEGMENTS, "late_y0")
         nc.gpsimd.memset(win1[LAST][:, :P].bitcast(U32), 0)
-        win1[1] = zeroed("win1_1", SEGMENTS, "late_y3")
+        win1[1] = zeroed("win1_1", SEGMENTS, "late_y1")
         scatter_plain(win0[2], tok, 2, 2, BLOCKS)
         scatter_plain(win0[2], tok, 2, 0, 2)
         nc.sync.dma_start(block_rows(out_0, 2), win0[2][:])

from contextlib import ExitStack

import concourse.mybir as mybir
from concourse.masks import make_identity

FLOPS = 2 * 512 * 512 * 512

F32 = mybir.dt.float32
BF16 = mybir.dt.bfloat16
U32 = mybir.dt.uint32
U16 = mybir.dt.uint16
U8 = mybir.dt.uint8
E4M3 = mybir.dt.float8_e4m3fn_x4
E5M2 = mybir.dt.float8_e5m2_x4
ACT = mybir.ActivationFunctionType
ALU = mybir.AluOpType
AXIS = mybir.AxisListType

P = 128
PACK = 4
D = 512
SLOTS = 512
TOKENS = 2048
SEGMENTS = 1024
BLOCKS = 4
LAST = BLOCKS - 1
LIST_ROWS = 16
RUN = 4
SHARE = 256


def cols(first, end=None):
    return slice(first * P, (first + 1 if end is None else end) * P)


def entries(first, end):
    return slice(first * P // LIST_ROWS, end * P // LIST_ROWS)


def block_rows(table, j):
    return table.rearrange("(p j) c -> j p c", j=BLOCKS)[j]


def tile_attend_gtwoemb_rms_kernel(tc, aT, bT, W, dz, gam, offs, soffs, out_0, out_1):
    nc = tc.nc
    with ExitStack() as ctx:
        pool = ctx.enter_context(tc.tile_pool(name="pool", bufs=1))
        psum = ctx.enter_context(tc.psum_pool(name="psum", bufs=1))

        def sb(name, shape, dtype=F32, tag=None):
            return pool.tile(shape, dtype, name=name, tag=tag or name, align_bytes=64)

        def bank(name, tag):
            return psum.tile([P, SLOTS], F32, name=name, tag=tag)

        every = range(BLOCKS)

        gam_col = sb("gam_col", [P, BLOCKS])
        nc.scalar.dma_start(gam_col[:], gam[0:1, :].rearrange("r (p j) -> (r p) j", j=BLOCKS))
        w_raw = sb("w_raw", [P, PACK, D])
        nc.sync.dma_start(w_raw[:], W.rearrange("(p t) d -> p t d", t=PACK))
        dz_raw = sb("dz_raw", [P, PACK, SLOTS])
        nc.sync.dma_start(dz_raw[:], dz.rearrange("(p t) i -> p t i", t=PACK))
        tok = pool.tile([P, SLOTS // LIST_ROWS], U16, name="tok")
        nc.sync.dma_start(tok[:], offs)
        seg = pool.tile([P, SLOTS // LIST_ROWS], U16, name="seg")
        nc.sync.dma_start(seg[:], soffs)
        a_tab = [sb("a_tab%d" % j, [P, TOKENS]) for j in every]
        b_tab = [sb("b_tab%d" % j, [P, SEGMENTS]) for j in every]
        for j in every:
            nc.sync.dma_start(b_tab[j][:], block_rows(bT, j))
            nc.sync.dma_start(a_tab[j][:], block_rows(aT, j))

        ident = sb("ident", [P, P])
        make_identity(nc, ident[:])
        warm = sb("warm", [P, 1])
        nc.scalar.activation(warm[:], gam_col[:, 0:1], ACT.Abs_reciprocal_sqrt, scale=0.0, bias=1.0)

        win0 = {j: sb("win0_%d" % j, [P, TOKENS]) for j in (LAST, 1)}
        for window in win0.values():
            nc.vector.memset(window[:].bitcast(U32), 0)

        def turn(out, src, start=True, stop=True):
            nc.tensor.matmul(out, src, ident[:], start=start, stop=stop, is_transpose=True)

        def quantise(codes, scales, woven, fmt):
            nc.vector.quantize_mx(out=codes.bitcast(fmt), scales=scales, in_=woven.rearrange("p c t -> p (c t)"))

        gam_ps = bank("gam_ps", "y0")
        for j in every:
            turn(gam_ps[:, cols(j)], gam_col[:, j : j + 1].to_broadcast([P, P]))
        gam_row = sb("gam_row", [P, D])
        nc.scalar.copy(gam_row[:], gam_ps[:])

        w_codes = sb("w_codes", [P, D], U32)
        w_scales = sb("w_scales", [P, D], U8)
        for half, copy in enumerate((nc.vector.tensor_copy, nc.scalar.copy)):
            w_woven = sb("w_woven%d" % half, [P, 2 * P, PACK], BF16, tag="gam_col" if half else None)
            copy(w_woven[:].rearrange("p (u m) t -> p m t u", u=2),
                 w_raw[:].rearrange("p t (m j) -> p m t j", j=BLOCKS)[:, :, :, 2 * half : 2 * half + 2])
            span = cols(2 * half, 2 * half + 2)
            quantise(w_codes[:, span], w_scales[:, span], w_woven[:], E4M3)
        dz_woven = sb("dz_woven", [P, SLOTS, PACK], BF16, tag="w_raw")
        dz_codes = sb("dz_codes", [P, SLOTS], U32)
        dz_scales = sb("dz_scales", [P, SLOTS], U8)
        for ib in every:
            copy = nc.vector.tensor_copy if ib < 2 else nc.scalar.copy
            copy(dz_woven[:, cols(ib), :].rearrange("p (c i) t -> p c t i", i=RUN),
                 dz_raw[:, :, cols(ib)].rearrange("p t (c i) -> p c t i", i=RUN))
        for ib in every:
            quantise(dz_codes[:, cols(ib)], dz_scales[:, cols(ib)], dz_woven[:, cols(ib), :], E5M2)

        h = sb("h", [P, BLOCKS, BLOCKS, P])
        for ib in every:
            dn_ps = bank("dn_ps", "x%d" % ib)
            nc.tensor.matmul_mx(out=dn_ps[:], lhsT=dz_codes[:, cols(ib)].bitcast(E5M2), lhsT_scale=dz_scales[:, cols(ib)],
                                rhs=w_codes[:].bitcast(E4M3), rhs_scale=w_scales[:], start=True, stop=True)
            nc.vector.tensor_tensor(h[:, :, ib, :], dn_ps[:].rearrange("p (j m) -> p j m", j=BLOCKS),
                                    gam_row[:].rearrange("p (j m) -> p j m", j=BLOCKS), ALU.mult)

        def zeroed(name, width, tag):
            window = sb(name, [P, width], tag=tag)
            nc.gpsimd.memset(window[:].bitcast(U32), 0)
            return window

        win0[2] = zeroed("win0_2", TOKENS, "w_raw")
        x_ps = [bank("x_ps%d" % ib, "x%d" % ib) for ib in every]
        squares = sb("squares", [P, BLOCKS, 2 * P])
        products = sb("products", [P, BLOCKS, 2, P])
        parts = sb("parts", [P, 2, BLOCKS, BLOCKS])
        nc.gpsimd.memset(parts[:, :, 2:BLOCKS, :], 0.0)

        def gather(engine, out, table, offsets):
            if engine == "vector":
                nc.vector.tensor_copy(out, table[:].indirect(offsets))
            else:
                nc.scalar.activation(out, table[:].indirect(offsets), ACT.Copy)

        def sum_products(j, ib):
            if ib >= 2 and j == 0:
                return
            first = 0 if ib >= 2 and j == 1 else j
            nc.vector.scalar_tensor_tensor(products[:, ib, : j + 1 - first, :],
                                           x_ps[ib][:, cols(first, j + 1)].rearrange("p (j m) -> p j m", m=P), -1.0,
                                           h[:, first : j + 1, ib, :], ALU.mult, ALU.mult,
                                           accum_out=parts[:, 1, ib, j : j + 1])

        def sum_squares(j, ib):
            if ib < 2 or j >= 2:
                nc.scalar.activation(squares[:, ib, cols(0)], x_ps[ib][:, cols(j)], ACT.Square,
                                     accum_out=parts[:, 0, ib, j : j + 1])
            elif j:
                nc.scalar.activation(squares[:, ib, :], x_ps[ib][:, cols(j - 1, j + 1)], ACT.Square,
                                     accum_out=parts[:, 0, ib, j : j + 1])

        def sums(j):
            for ib in (0, 2, 1, 3) if j else every:
                sum_products(j, ib)
                if j == 0 and ib < 2:
                    nc.vector.tensor_copy(x_first[:, ib, :], x_ps[ib][:, cols(0)])
                sum_squares(j, ib ^ 1 if j else ib)

        y_pair = [bank("y_pair%d" % half, "y%d" % (half + 1)) for half in range(2)]
        y_ps = {LAST: bank("y_early", "y0")}

        def y_cols(j, first, end):
            if j in y_ps:
                return y_ps[j][:, cols(first, end)]
            lo = 2 * (j - 1) + first % 2
            return y_pair[first // 2][:, cols(lo, lo + end - first)]

        def turn_h(j, first, end):
            for ib in range(first, end):
                turn(y_cols(j, ib, ib + 1), h[:, j, ib, :], ib == first if j in y_ps else j == 1 and ib % 2 == 0, False)

        def gather_pieces(table, offsets, pieces):
            for engine, lo, hi, out in pieces:
                gather(engine, out, table, offsets[:, entries(lo, hi)])

        def turn_pieces(j, pieces, first):
            for engine, lo, hi, out in pieces:
                for ib in range(lo, hi):
                    turn(x_ps[ib][:, cols(j)], out[:, cols(ib - lo)], first, not first)

        def whole(name, tag):
            return [("scalar", 0, BLOCKS, sb(name, [P, SLOTS], tag=tag)[:])]

        def halves(room):
            return [("vector", 0, 2, room[:, cols(0, 2)]), ("scalar", 2, BLOCKS, room[:, cols(2, BLOCKS)])]

        def spent_h(j):
            return h[:, j].rearrange("p b m -> p (b m)")

        def b_pieces(j):
            if j < 2:
                return whole("b_got%d" % j, "gam_row" if j else "dz_raw")
            return halves(sb("b_got%d" % j, [P, SLOTS], tag="a_tab%d" % (j - 1)))

        x_first = sb("x_first", [P, BLOCKS, P])
        early = sb("early", [P, 2, 2])
        root = sb("root", [P, 2])
        half_coef = sb("half_coef", [P, 2])
        row_ps = bank("row_ps", "y%d" % LAST)

        def spread(ib, column, start=True, stop=True):
            turn(row_ps[:, cols(ib)], column.to_broadcast([P, P]), start, stop)

        b_next = b_pieces(0)
        gather_pieces(b_tab[0], seg, b_next)
        for j in every:
            turn_pieces(j, b_next, True)
            if j == 0:
                a_first = sb("a_got0", [P, SLOTS], tag="b_tab0")
                rounds = [[("scalar", n, n + 2, a_first[:, cols(n, n + 2)])] for n in (0, 2)]
            elif j == 1:
                rounds = [halves(sb("a_got1", [P, SLOTS], tag="b_tab0"))]
            elif j < LAST:
                rounds = [halves(spent_h(j - 1))]
            else:
                rounds = [[("vector", 2 * n, 2 * n + 1, h[:, j - 1, 1 + 2 * n, :]), ("scalar", 2 * n + 1, 2 * n + 2, h[:, j - 1, 2 - 2 * n, :])]
                          for n in range(2)]
            for pieces in rounds:
                gather_pieces(a_tab[j], tok, pieces)
                turn_pieces(j, pieces, False)
            if j < 2:
                b_next = b_pieces(j + 1)
                gather_pieces(b_tab[j + 1], seg, b_next)
            elif j == 2:
                b_next = whole("b_got%d" % LAST, "a_tab2")
                b_last = b_next[0][-1]
                gather("vector", b_last[:, :SHARE], b_tab[LAST], seg[:, : SHARE // LIST_ROWS])
                gather("scalar", b_last[:, SHARE:], b_tab[LAST], seg[:, SHARE // LIST_ROWS :])
            if j == 0:
                turn_h(LAST, 0, 2)
                turn_h(1, 0, BLOCKS)
                turn_h(2, 0, BLOCKS)
            if j == LAST:
                nc.vector.tensor_reduce(early[:], parts[:, :, 0:2, 0:LAST], AXIS.X, ALU.add)
                for ib in range(2):
                    sum_squares(j, ib)
                    sum_products(j, ib)
                for ib in range(2, BLOCKS):
                    sum_products(j, ib)
                    sum_squares(j, ib)
            else:
                sums(j)
            for ib in (1, 0):
                spread(ib, parts[:, 0, ib, j : j + 1], j == 0 and ib == 1, j == LAST and ib == 0)
            if j == 0:
                for ib in range(2, BLOCKS):
                    nc.vector.tensor_copy(x_first[:, ib, :], x_ps[ib][:, cols(0)])

        win1 = {}
        totals = sb("totals", [P, 2, BLOCKS])
        inv = sb("inv", [P, BLOCKS])
        rstd_row = sb("rstd_row", [P, SLOTS])
        values = [sb("values%d" % j, [P, SLOTS]) for j in every]

        def statistics(first, end):
            nc.vector.tensor_reduce(totals[:, :, first:end], parts[:, :, first:end, :], AXIS.X, ALU.add)
            nc.vector.reciprocal(inv[:, first:end], totals[:, 0, first:end])

        def shift_on_vector(out, ib, first, end):
            nc.vector.tensor_scalar(out, x_ps[ib][:, cols(first, end)], totals[:, 1, ib : ib + 1],
                                    inv[:, ib : ib + 1], ALU.mult, ALU.mult)

        def shift_on_scalar(out, ib, first, end, coef):
            nc.scalar.activation(out, x_ps[ib][:, cols(first, end)], ACT.Copy, scale=coef)

        def turn_back(j, ib, src, stop):
            turn(y_cols(j, ib, ib + 1), src, False, stop)

        def copy_plain(j, first, end):
            nc.vector.tensor_copy(values[j][:, cols(first, end)], y_cols(j, first, end))

        def copy_scaled(j, first, end):
            span = cols(first, end)
            nc.vector.tensor_tensor(values[j][:, span], y_cols(j, first, end), rstd_row[:, span], ALU.mult)

        def scatter_scaled(window, offsets, j):
            nc.vector.tensor_tensor(window[:].indirect(offsets[:]), values[j][:], rstd_row[:], ALU.mult)

        def scatter_plain(window, offsets, j, first, end):
            nc.scalar.activation(window[:].indirect(offsets[:, entries(first, end)]), values[j][:, cols(first, end)],
                                 ACT.Copy)

        def put(windows, offsets, out, j):
            scatter_scaled(windows[j], offsets, j)
            nc.sync.dma_start(block_rows(out, j), windows[j][:])

        def make_rstd(first, end):
            nc.scalar.activation(rstd_row[:, cols(first, end)], row_ps[:, cols(first, end)], ACT.Abs_reciprocal_sqrt,
                                 scale=1.0 / D)

        def finish_late(first, end, tag):
            y_ps[0] = bank("y_late%d" % first, tag)
            if first:
                turn_h(0, first, end)
            for ib in range(first, end):
                late = sb("late%d" % ib, [P, P])
                nc.gpsimd.tensor_scalar(late[:], x_first[:, ib, :], coef[ib // 2][:, ib % 2 : ib % 2 + 1], 0.0,
                                        ALU.mult, ALU.add)
                if first:
                    turn_back(0, ib, late[:], ib == end - 1)
                else:
                    whole_y = sb("late_y%d" % ib, [P, P])
                    nc.gpsimd.tensor_tensor(whole_y[:], late[:], h[:, 0, ib, :], ALU.add)
                    turn(y_ps[0][:, cols(ib)], whole_y[:])
            nc.scalar.copy(values[0][:, cols(first, end)], y_ps[0][:, cols(first, end)])

        narrow = [sb("narrow%d" % ib, [P, P]) for ib in every]
        wide = [sb("wide%d" % ib, [P, 2 * P]) for ib in every]
        coef = [sb("coef%d" % half, [P, 2]) for half in range(2)]
        for ib in range(2):
            nc.scalar.activation(root[:, ib : ib + 1], parts[:, 0, ib, LAST:BLOCKS], ACT.Abs_reciprocal_sqrt,
                                 bias=early[:, 0, ib : ib + 1])
            nc.vector.tensor_scalar(half_coef[:, ib : ib + 1], parts[:, 1, ib, LAST:BLOCKS], early[:, 1, ib : ib + 1],
                                    root[:, ib : ib + 1], ALU.add, ALU.mult)
        make_rstd(0, 2)
        for ib in range(2):
            nc.vector.tensor_scalar(narrow[ib][:], x_ps[ib][:, cols(LAST)], half_coef[:, ib : ib + 1],
                                    root[:, ib : ib + 1], ALU.mult, ALU.mult)
        for ib in range(2):
            turn_back(LAST, ib, narrow[ib][:], ib == 1)
        statistics(2, BLOCKS)
        shift_on_vector(wide[2][:], 2, 1, LAST)
        nc.vector.tensor_tensor(coef[1][:], totals[:, 1, 2:BLOCKS], inv[:, 2:BLOCKS], ALU.mult)
        copy_scaled(LAST, 0, 2)
        for ib in range(2):
            nc.scalar.activation(coef[0][:, ib : ib + 1], half_coef[:, ib : ib + 1], ACT.Copy, scale=root[:, ib : ib + 1])
        for ib in range(2, BLOCKS):
            spread(ib, totals[:, 0, ib : ib + 1])
        make_rstd(2, BLOCKS)
        for ib in range(2):
            shift_on_scalar(wide[ib][:], ib, 1, LAST, coef[0][:, ib : ib + 1])
        y_ps[LAST] = bank("y_late", "x0")
        for ib in range(2, BLOCKS):
            nc.vector.scalar_tensor_tensor(narrow[ib][:], x_ps[ib][:, cols(LAST)], coef[1][:, ib - 2 : ib - 1],
                                           h[:, LAST, ib, :], ALU.mult, ALU.add)
            turn(y_ps[LAST][:, cols(ib)], narrow[ib][:])
        shift_on_vector(wide[LAST][:], LAST, 1, LAST)
        scatter_plain(win0[LAST], tok, LAST, 0, 2)
        copy_scaled(LAST, 2, BLOCKS)
        for first in (0, 2):
            for ib in (first, first + 1):
                for j in (1, 2):
                    turn_back(j, ib, wide[ib][:, cols(j - 1)], ib > first and j == 2)
            copy_plain(1, first, first + 2)
            copy_scaled(2, first, first + 2)
        finish_late(0, 2, "y0")
        scatter_plain(win0[LAST], tok, LAST, 2, BLOCKS)
        nc.sync.dma_start(block_rows(out_0, LAST), win0[LAST][:])
        put(win0, tok, out_0, 1)
        finish_late(2, BLOCKS, "x%d" % LAST)
        win0[0] = zeroed("win0_0", TOKENS, "x_first")
        win1[0] = zeroed("win1_0", SEGMENTS, "coef1")
        win1[LAST] = sb("win1_%d" % LAST, [P, SEGMENTS], tag="h")
        nc.gpsimd.memset(win1[LAST][:, P:].bitcast(U32), 0)
        win1[2] = zeroed("win1_2", SEGMENTS, "late_y0")
        nc.gpsimd.memset(win1[LAST][:, :P].bitcast(U32), 0)
        win1[1] = zeroed("win1_1", SEGMENTS, "late_y1")
        scatter_plain(win0[2], tok, 2, 2, BLOCKS)
        scatter_plain(win0[2], tok, 2, 0, 2)
        nc.sync.dma_start(block_rows(out_0, 2), win0[2][:])
        put(win0, tok, out_0, 0)
        put(win1, seg, out_1, 0)
        for first in (0, 2):
            for j in (2, LAST):
                scatter_plain(win1[j], seg, j, first, first + 2)
                if first:
                    nc.sync.dma_start(block_rows(out_1, j), win1[j][:])
        put(win1, seg, out_1, 1)
